import numpy as np
import ml_dtypes


def mxq(x, axis, fmt="e4m3"):
    dtype, down = {"e4m3": (ml_dtypes.float8_e4m3fn, 7), "e5m2": (ml_dtypes.float8_e5m2, 14)}[fmt]
    v = np.moveaxis(np.asarray(x, np.float32).astype(ml_dtypes.bfloat16).astype(np.float64), axis, -1)
    blocks = v.reshape(v.shape[:-1] + (-1, 32))
    amax = np.abs(blocks).max(-1, keepdims=True)
    byte = np.maximum(np.where(amax > 0, np.frexp(amax)[1] - 1 + 127, 0) - down, 1)
    scale = np.exp2(byte - 127.0)
    codes = (blocks / scale).astype(np.float32).astype(dtype).astype(np.float64)
    return np.moveaxis((codes * scale).reshape(v.shape), -1, axis)


WIDE = False


def mx_kscale(k):
    if not WIDE:
        return np.ones(k)
    levels = np.array([24, -24, 12, -12, 0])
    if k % 512:
        return np.exp2(np.random.permutation(np.resize(levels, k // 32))).repeat(32)
    a = np.empty((k // 512, 16))
    for p in range(k // 512):
        a[p, :8] = np.random.permutation(np.resize(levels, 8))
        for g in range(8):
            far = levels[np.abs(levels - a[p, g]) >= 10]
            a[p, g + 8] = far[np.random.randint(len(far))]
    return np.exp2(a.ravel()).repeat(32)


def f64(x):
    return np.asarray(x).astype(np.float64)


def striped(idx):
    return np.tile(idx.reshape(-1, 16).T, (8, 1)).astype(np.uint16)


def unstriped(offs):
    return offs[:16].T.reshape(-1).astype(np.int64)


E2M1 = np.array([0.0, 0.5, 1.0, 1.5, 2.0, 3.0, 4.0, 6.0, -0.0, -0.5, -1.0, -1.5, -2.0, -3.0, -4.0, -6.0])


def pack_weight(w, fmt):
    k, n = w.shape
    w = f64(np.asarray(w, np.float32).astype(ml_dtypes.bfloat16)).reshape(k // 32, 32, n)
    amax = np.abs(w).max(1)
    if fmt == "e4m3":
        byte = np.frexp(amax)[1] - 1 + 127 - 7
    else:
        mant, ex = np.frexp(amax / 6.0)
        byte = np.where(mant > 0.5, ex, ex - 1) + 127
    byte = np.clip(np.where(amax > 0, byte, 1), 1, 254)
    scaled = (w * np.exp2(127.0 - byte)[:, None, :]).reshape(k, n).astype(np.float32)
    by_word = np.ascontiguousarray(scaled.reshape(k // 512, 128, 4, n).transpose(0, 1, 3, 2))
    if fmt == "e4m3":
        words = by_word.astype(ml_dtypes.float8_e4m3fn).view(np.uint8)
    else:
        c = by_word.astype(ml_dtypes.float4_e2m1fn).view(np.uint8) & 0xF
        words = (c[..., 0::2] | (c[..., 1::2] << 4)).reshape(k // 512, 128, 2 * n)
    return np.ascontiguousarray(words), np.ascontiguousarray(byte.astype(np.uint8).reshape(k // 512, 16, n))


def unpack_weight(words, scales, fmt):
    g, _, n = scales.shape
    words = np.ascontiguousarray(words).reshape(g, 128, n, -1)
    if fmt == "e4m3":
        vals = words.view(ml_dtypes.float8_e4m3fn).astype(np.float64)
    else:
        nib = np.empty((g, 128, n, 4), np.uint8)
        nib[..., 0::2] = words & 0xF
        nib[..., 1::2] = words >> 4
        vals = E2M1[nib]
    vals = vals * np.repeat(np.exp2(scales.astype(np.float64) - 127.0), 8, axis=1)[..., None]
    return vals.transpose(0, 1, 3, 2).reshape(g * 512, n)


def pack_table4(v):
    words, scales = pack_weight(v, "e2m1")
    g, t = words.shape[0] // 2, v.shape[1]
    return np.ascontiguousarray(words.reshape(g, 2, 128, t, 2).transpose(0, 2, 3, 1, 4).reshape(g, 128, t, 4)), scales


def unpack_table4(words, scales):
    g, _, t, _ = words.shape
    return unpack_weight(words.reshape(g, 128, t, 2, 2).transpose(0, 3, 1, 2, 4).reshape(2 * g, 128, 2 * t), scales, "e2m1")


def planes(y):
    n, m = y.shape
    v = y.astype(np.float32).astype(ml_dtypes.bfloat16).astype(np.float64).reshape(n // 32, 32, m)
    top = np.abs(v).max(1)
    byte = np.clip(np.where(top > 0, np.frexp(top)[1] - 1 + 127 - 7, 1), 1, 254)
    codes = (v * np.exp2(127.0 - byte)[:, None, :]).reshape(n, m).astype(np.float32).astype(ml_dtypes.float8_e4m3fn).view(np.uint8)
    words = codes.reshape(n // 512, 128, 4, m).transpose(0, 1, 3, 2)
    return np.ascontiguousarray(words), np.ascontiguousarray(byte.astype(np.uint8).reshape(n // 512, 16, m))


K, R, N, T, J = 1024, 512, 512, 2048, 1024


def setup_inputs():
    n = np.random.standard_normal
    s = mx_kscale(K)[:, None]
    u = mx_kscale(R)[:, None]
    wd = n((R, N)) / np.sqrt(R) / u
    wd4 = pack_weight(wd, "e2m1")
    wdrest = wd - unpack_weight(*wd4, "e2m1")
    p_tab = pack_table4(n((K, T)) * s)
    p_wd8 = pack_weight(wdrest, "e4m3")
    return {
        "tab_words": p_tab[0],
        "tab_scales": p_tab[1],
        "ws": (n((K, R)) / np.sqrt(2 * K) / s).astype(np.float32),
        "wt": (n((K, R)) / np.sqrt(2 * K) / s).astype(np.float32),
        "sm": (np.random.uniform(0.5, 2.0, R) * u[:, 0]).astype(np.float32),
        "wd4_words": wd4[0],
        "wd4_scales": wd4[1],
        "wd8_words": p_wd8[0],
        "wd8_scales": p_wd8[1],
        "b": (0.3 * n(N)).astype(np.float32),
        "wgo": np.tile(np.random.uniform(0.5, 2.0, J), (128, 1)).astype(np.float32),
        "offs": striped(np.random.permutation(T)[:J]),
        "offs2": striped(np.random.permutation(T)[:J]),
    }


def reference(tab_words, tab_scales, ws, wt, sm, wd4_words, wd4_scales, wd8_words, wd8_scales, b, wgo, offs, offs2):
    idx = unstriped(offs)
    idx2 = unstriped(offs2)
    tab_ = unpack_table4(tab_words, tab_scales)[:, idx]
    tabb_ = unpack_table4(tab_words, tab_scales)[:, idx2]
    ws_ = mxq(f64(ws), 0, "e4m3")
    wt_ = mxq(f64(wt), 0, "e4m3")
    a = ws_.T @ tab_ + wt_.T @ tabb_
    h = f64(sm)[:, None] * np.tanh(a)
    h_ = mxq(h, 0, "e4m3")
    wd4_ = unpack_weight(wd4_words, wd4_scales, "e2m1")
    wd8_ = unpack_weight(wd8_words, wd8_scales, "e4m3")
    y = wd4_.T @ h_ + wd8_.T @ h_
    out = np.zeros((N, T))
    out[:, idx2] = f64(wgo)[0] * (y + f64(b)[:, None])
    return (out,) + planes(out)

@@ -1,0 +1,287 @@
+from contextlib import ExitStack
+
+import concourse.mybir as mybir
+
+K, R, N, T, J = 1024, 512, 512, 2048, 1024
+FLOPS = 2 * J * (2 * K * R + 2 * R * N)
+
+F32 = mybir.dt.float32
+BF16 = mybir.dt.bfloat16
+I32 = mybir.dt.int32
+U32 = mybir.dt.uint32
+U16 = mybir.dt.uint16
+U8 = mybir.dt.uint8
+FP8X4 = mybir.dt.float8_e4m3fn_x4
+FP4X4 = mybir.dt.float4_e2m1fn_x4
+ACT = mybir.ActivationFunctionType
+MULT = mybir.AluOpType.mult
+
+P = 128
+PACK = 4
+K_PASS = P * PACK
+PASSES = K // K_PASS
+QUADS = 4
+HALF = J // 2
+HALF_COLS = HALF // 16
+W_SPLIT = 2
+OUT_CHUNK = 256
+OUT_CHUNKS = T // OUT_CHUNK
+SCALAR_WEAVES = 2
+VECTOR_CASTS = 2
+
+
+def tile_list_msg_tanh_res_biasP_kernel(
+    tc, tab_words, tab_scales, ws, wt, sm, wd4_words, wd4_scales, wd8_words, wd8_scales, b, wgo, offs, offs2,
+    out_0, out_1, out_2,
+):
+    nc = tc.nc
+    with ExitStack() as ctx:
+        keep = ctx.enter_context(tc.tile_pool(name="keep", bufs=1))
+        psum = ctx.enter_context(tc.psum_pool(name="psum", bufs=1))
+
+        def sb(shape, dtype, name, tag=None):
+            return keep.tile(shape, dtype, name=name, tag=tag or name, align_bytes=64)
+
+        def bank(i, name):
+            return psum.tile([P, HALF], F32, name=name, tag="bank%d" % i)
+
+        src_list = keep.tile([P, J // 16], U16, name="src_list")
+        dst_list = keep.tile([P, J // 16], U16, name="dst_list")
+        lists = (src_list, dst_list)
+        table = sb([P, T], I32, "table")
+        table_scales = sb([P, T], U8, "table_scales")
+
+        nc.sync.dma_start(src_list[:], offs)
+        nc.sync.dma_start(dst_list[:], offs2)
+        for q in range(QUADS):
+            nc.sync.dma_start(
+                table_scales[32 * q + 24 : 32 * q + 32, :].bitcast(I32),
+                tab_scales[:, 4 * q : 4 * q + 4, :].bitcast(I32).rearrange("a r n -> r a n"),
+            )
+            nc.gpsimd.memset(table_scales[32 * q : 32 * q + 24, :].bitcast(I32), 0)
+
+        warm = sb([P, 8], F32, "warm")
+        nc.gpsimd.memset(warm[:], 0.0)
+        nc.scalar.activation(warm[:, 4:5], warm[:, 0:1], ACT.Tanh)
+
+        pages = [sb([P, T], F32, "page%d" % t) for t in range(PACK)]
+        for page in pages[:2]:
+            nc.vector.memset(page[:], 0.0)
+        moved = sb([P, PASSES, 2 * J], U8, "moved")
+        nc.gpsimd.memset(moved[:].bitcast(I32), 0)
+        for page in pages[2:]:
+            for u in range(2):
+                nc.gpsimd.memset(page[:, u * J : (u + 1) * J], 0.0)
+
+        w_order = [(a, s) for a in range(PASSES) for s in range(2)]
+        cols = R // W_SPLIT
+        raw = {}
+
+        def load_raw(a, s, u):
+            rows = (ws, wt)[s][a * K_PASS : (a + 1) * K_PASS, :].rearrange("(p j) r -> p j r", j=PACK)
+            raw[a, s, u] = sb([P, PACK, cols], F32, "raw%d%d%d" % (a, s, u), tag="raw%d%d" % (s, u))
+            nc.sync.dma_start(raw[a, s, u][:], rows[:, :, u * cols : (u + 1) * cols])
+
+        for s in range(2):
+            for u in range(W_SPLIT):
+                load_raw(0, s, u)
+            if s == 0:
+                nc.sync.dma_start(table[:], tab_words[0].rearrange("p t c -> p (t c)").bitcast(I32))
+
+        sm_sb = sb([P, PACK], F32, "sm_sb")
+        nc.sync.dma_start(sm_sb[:], sm.rearrange("(p t) -> p t", t=PACK))
+        b_sb = sb([P, PACK], F32, "b_sb")
+        nc.sync.dma_start(b_sb[:], b.rearrange("(p t) -> p t", t=PACK))
+
+        picked_scales = sb([P, 2 * J], U8, "picked_scales")
+        for s in range(2):
+            nc.vector.tensor_copy(picked_scales[:, s * J : (s + 1) * J], table_scales[:].indirect(lists[s][:]))
+        for q in range(QUADS):
+            nc.sync.dma_start(
+                moved[32 * q : 32 * q + 4, :, :].bitcast(I32), picked_scales[32 * q + 24 : 32 * q + 32, :].bitcast(I32)
+            )
+
+        def look_up(h, tag):
+            cut = slice(h * HALF_COLS, (h + 1) * HALF_COLS)
+            picked = sb([P, 2, HALF], U32, "picked%d" % h, tag=tag)
+            for s in range(2):
+                nc.vector.tensor_copy(picked[:, s, :], table[:].bitcast(U32).indirect(lists[s][:, cut]))
+            return picked
+
+        def part(h, picked, tag):
+            parted = sb([P, 2, PASSES, 2 * HALF], U8, "parted%d" % h, tag=tag)
+            for s in range(2):
+                nc.vector.tensor_copy(
+                    parted[:, s, :, :].bitcast(U16),
+                    picked[:, s, :].bitcast(U16).rearrange("p (n d) -> p d n", d=PASSES),
+                )
+            return parted
+
+        parted0 = part(0, look_up(0, None), None)
+
+        w_codes = {}
+        w_scales = {}
+        m_cols = P // W_SPLIT
+        for a, s in w_order:
+            grouped = sb([P, PACK, P, PACK], BF16, "grouped%d%d" % (a, s))
+            for u in range(W_SPLIT):
+                dst = grouped[:, :, u * m_cols : (u + 1) * m_cols, :].rearrange("p t m j -> p m j t")
+                src = raw[a, s, u][:].rearrange("p j (m t) -> p m j t", t=PACK)
+                if (a, s) == w_order[-1] and u == W_SPLIT - 1:
+                    nc.vector.tensor_copy(dst, src)
+                else:
+                    nc.scalar.activation(dst, src, ACT.Copy)
+                if a + 1 < PASSES:
+                    load_raw(a + 1, s, u)
+            w_codes[a, s] = sb([P, R], U32, "w_codes%d%d" % (a, s))
+            w_scales[a, s] = sb([P, R], U8, "w_scales%d%d" % (a, s))
+            nc.vector.quantize_mx(
+                w_codes[a, s][:].bitcast(FP8X4), w_scales[a, s][:], grouped[:].rearrange("p t m j -> p (t m j)")
+            )
+
+        wd4_raw = sb([P, 2 * N], U8, "wd4_raw", tag="grouped00")
+        wd8_raw = sb([P, N], I32, "wd8_raw", tag="raw00")
+        nc.sync.dma_start(wd4_raw[:].bitcast(I32), wd4_words[0].bitcast(I32))
+        nc.sync.dma_start(wd8_raw[:], wd8_words[0].rearrange("p n c -> p (n c)").bitcast(I32))
+        wd_scales_raw = sb([P, 2 * N], U8, "wd_scales_raw", tag="grouped01")
+        nc.gpsimd.memset(wd_scales_raw[:].bitcast(I32), 0)
+        for w, scales in enumerate((wd4_scales, wd8_scales)):
+            for q in range(QUADS):
+                nc.sync.dma_start(
+                    wd_scales_raw[32 * q : 32 * q + 4, w * N : (w + 1) * N].bitcast(I32),
+                    scales[0, 4 * q : 4 * q + 4, :].bitcast(I32),
+                )
+        wgo_sb = sb([P, J], F32, "wgo_sb", tag="raw01")
+        nc.sync.dma_start(wgo_sb[:], wgo)
+
+        def first_pass(acc, h, t, a, s, parted):
+            wc = slice(t * P, (t + 1) * P)
+            nc.tensor.matmul_mx(
+                acc[:],
+                lhsT=w_codes[a, s][:, wc].bitcast(FP8X4),
+                lhsT_scale=w_scales[a, s][:, wc],
+                rhs=parted[:, s, a, :].bitcast(FP4X4),
+                rhs_scale=moved[:, a, s * J + h * HALF : s * J + (h + 1) * HALF],
+                start=(a, s) == w_order[0],
+                stop=(a, s) == w_order[-1],
+            )
+
+        def activate(h, accs, tag):
+            hidden = sb([P, PACK, HALF], BF16, "hidden%d" % h, tag=tag)
+            for t in range(PACK):
+                th = sb([P, HALF], F32, "th%d%d" % (h, t), tag="th%d" % (t % 2))
+                nc.scalar.activation(th[:], accs[t][:], ACT.Tanh)
+                nc.scalar.activation(hidden[:, t, :], th[:], ACT.Copy, scale=sm_sb[:, t : t + 1])
+            return hidden
+
+        def weave_hidden(h, hidden):
+            woven = sb([P, HALF, PACK], BF16, "woven%d" % h)
+            dst = woven[:].rearrange("p (c i) t -> p c t i", i=4)
+            src = hidden[:].rearrange("p t (c i) -> p c t i", i=4)
+            if h == 0:
+                nc.vector.tensor_copy(dst, src)
+            else:
+                nc.scalar.copy(dst, src)
+            codes = sb([P, HALF], U32, "h_codes%d" % h)
+            scales = sb([P, HALF], U8, "h_scales%d" % h)
+            nc.vector.quantize_mx(codes[:].bitcast(FP8X4), scales[:], woven[:].rearrange("p n t -> p (n t)"))
+            return codes, scales
+
+        accs0 = [bank(t, "a0%d" % t) for t in range(PACK)]
+        for a, s in w_order:
+            for t in range(PACK):
+                first_pass(accs0[t], 0, t, a, s, parted0)
+
+        picked1 = look_up(1, "grouped11")
+
+        hidden0 = activate(0, accs0, "hidden0")
+        h_codes0, h_scales0 = weave_hidden(0, hidden0)
+
+        wd4 = sb([P, PACK, 2 * P], U8, "wd4")
+        wd8 = sb([P, PACK, P], I32, "wd8")
+        wd_scales = sb([P, 2, PACK, P], U8, "wd_scales")
+        nc.vector.tensor_copy(
+            wd4[:].bitcast(U16).rearrange("p t m -> p m t"),
+            wd4_raw[:].bitcast(U16).rearrange("p (m t) -> p m t", t=PACK),
+        )
+        nc.vector.tensor_copy(wd8[:].rearrange("p t m -> p m t"), wd8_raw[:].rearrange("p (m t) -> p m t", t=PACK))
+        nc.vector.tensor_copy(
+            wd_scales[:].rearrange("p w t m -> p w m t"),
+            wd_scales_raw[:].rearrange("p (w m t) -> p w m t", w=2, t=PACK),
+        )
+
+        parted1 = part(1, picked1, "woven0")
+
+        def second_layer(h, t, codes, scales):
+            acc = bank(PACK + t, "y%d%d" % (h, t))
+            nc.tensor.matmul_mx(
+                acc[:], lhsT=wd8[:, t, :].bitcast(FP8X4), lhsT_scale=wd_scales[:, 1, t, :],
+                rhs=codes[:].bitcast(FP8X4), rhs_scale=scales[:], start=True, stop=False,
+            )
+            nc.tensor.matmul_mx(
+                acc[:], lhsT=wd4[:, t, :].bitcast(FP4X4), lhsT_scale=wd_scales[:, 0, t, :],
+                rhs=codes[:].bitcast(FP8X4), rhs_scale=scales[:], start=False, stop=True,
+            )
+            return acc
+
+        def put(h, t, acc, tag=None):
+            message = sb([P, HALF], F32, "message%d%d" % (h, t), tag=tag)
+            nc.scalar.activation(message[:], acc[:], ACT.Identity, bias=b_sb[:, t : t + 1])
+            nc.vector.tensor_tensor(
+                pages[t][:].indirect(dst_list[:, h * HALF_COLS : (h + 1) * HALF_COLS]),
+                message[:],
+                wgo_sb[:, h * HALF : (h + 1) * HALF],
+                MULT,
+            )
+
+        ys0 = [second_layer(0, t, h_codes0, h_scales0) for t in range(PACK)]
+        for t in range(PACK - 1):
+            put(0, t, ys0[t])
+
+        accs1 = [bank(t, "a1%d" % t) for t in range(PACK)]
+        for t in range(PACK):
+            for a, s in w_order:
+                first_pass(accs1[t], 1, t, a, s, parted1)
+        hidden1 = activate(1, accs1, "hidden1")
+        h_codes1, h_scales1 = weave_hidden(1, hidden1)
+        put(0, PACK - 1, ys0[PACK - 1], tag="hidden1")
+
+        out_rows = out_0.rearrange("(p t) c -> t p c", t=PACK)
+        pairs = [sb([P, 2, OUT_CHUNK, 2], BF16, "pairs%d" % c) for c in range(OUT_CHUNKS)]
+        ys1 = [second_layer(1, t, h_codes1, h_scales1) for t in range(PACK)]
+        for t in range(PACK):
+            put(1, t, ys1[t])
+        out_words = out_1[0].rearrange("p t c -> p (t c)").bitcast(I32)
+        out_scales = sb([P, 2 * OUT_CHUNK], U8, "out_scales")
+        out_codes = [sb([P, 2 * OUT_CHUNK], U32, "out_codes%d" % g) for g in range(OUT_CHUNKS // 2)]
+        for t in range(PACK):
+            nc.sync.dma_start(out_rows[t], pages[t][:])
+            for c in range(OUT_CHUNKS):
+                nc.scalar.activation(
+                    pairs[c][:, t // 2, :, t % 2], pages[t][:, c * OUT_CHUNK : (c + 1) * OUT_CHUNK], ACT.Copy
+                )
+        for c in range(OUT_CHUNKS):
+            g, e = divmod(c, 2)
+            woven_out = sb([P, OUT_CHUNK, PACK], BF16, "woven_out%d" % c)
+            word = U32 if c >= OUT_CHUNKS - SCALAR_WEAVES else I32
+            dst = woven_out[:].rearrange("p n t -> p (n t)").bitcast(word).rearrange("p (n u) -> p n u", u=2)
+            src = pairs[c][:].rearrange("p u n e -> p u (n e)").bitcast(word).rearrange("p u n -> p n u")
+            if c >= OUT_CHUNKS - SCALAR_WEAVES:
+                nc.scalar.copy(dst, src)
+            else:
+                nc.vector.tensor_copy(dst, src)
+            cut = slice(e * OUT_CHUNK, (e + 1) * OUT_CHUNK)
+            nc.vector.quantize_mx(
+                out_codes[g][:, cut].bitcast(FP8X4),
+                out_scales[4 * g : P, cut],
+                woven_out[:].rearrange("p n t -> p (n t)"),
+            )
+            if e == 1:
+                nc.sync.dma_start(
+                    out_words[:, g * 2 * OUT_CHUNK : (g + 1) * 2 * OUT_CHUNK], out_codes[g][:].bitcast(I32)
+                )
+        for q in range(QUADS):
+            nc.sync.dma_start(
+                out_2[0, 4 * q : 4 * q + 4, :].bitcast(I32).rearrange("r (g n) -> g r n", g=OUT_CHUNKS // 2),
+                out_scales[32 * q : 32 * q + 16, :].bitcast(I32),
+            )

@@ -27,7 +27,7 @@ W_SPLIT = 2
 OUT_CHUNK = 256
 OUT_CHUNKS = T // OUT_CHUNK
 SCALAR_WEAVES = 2
-VECTOR_CASTS = 2
+QUARTER = HALF // 2
 
 
 def tile_list_msg_tanh_res_biasP_kernel(
@@ -51,6 +51,10 @@ def tile_list_msg_tanh_res_biasP_kernel(
         table = sb([P, T], I32, "table")
         table_scales = sb([P, T], U8, "table_scales")
 
+        warm = sb([P, 8], F32, "warm")
+        nc.vector.memset(warm[:], 0.0)
+        nc.scalar.activation(warm[:, 4:5], warm[:, 0:1], ACT.Tanh)
+
         nc.sync.dma_start(src_list[:], offs)
         nc.sync.dma_start(dst_list[:], offs2)
         for q in range(QUADS):
@@ -58,35 +62,29 @@ def tile_list_msg_tanh_res_biasP_kernel(
                 table_scales[32 * q + 24 : 32 * q + 32, :].bitcast(I32),
                 tab_scales[:, 4 * q : 4 * q + 4, :].bitcast(I32).rearrange("a r n -> r a n"),
             )
-            nc.gpsimd.memset(table_scales[32 * q : 32 * q + 24, :].bitcast(I32), 0)
+            nc.vector.memset(table_scales[32 * q : 32 * q + 24, :].bitcast(I32), 0)
 
-        warm = sb([P, 8], F32, "warm")
-        nc.gpsimd.memset(warm[:], 0.0)
-        nc.scalar.activation(warm[:, 4:5], warm[:, 0:1], ACT.Tanh)
-
-        pages = [sb([P, T], F32, "page%d" % t) for t in range(PACK)]
-        for page in pages[:2]:
-            nc.vector.memset(page[:], 0.0)
         moved = sb([P, PASSES, 2 * J], U8, "moved")
-        nc.gpsimd.memset(moved[:].bitcast(I32), 0)
-        for page in pages[2:]:
-            for u in range(2):
-                nc.gpsimd.memset(page[:, u * J : (u + 1) * J], 0.0)
+        nc.vector.memset(moved[:].bitcast(I32), 0)
+        pages = [sb([P, T], F32, "page0")]
+        nc.vector.memset(pages[0][:], 0.0)
+
+        def late_page(tag):
+            page = sb([P, T], F32, "page%d" % len(pages), tag=tag)
+            nc.gpsimd.memset(page[:], 0.0)
+            pages.append(page)
 
         w_order = [(a, s) for a in range(PASSES) for s in range(2)]
-        cols = R // W_SPLIT
         raw = {}
 
-        def load_raw(a, s, u):
+        def load_raw(a, s, tag=None):
             rows = (ws, wt)[s][a * K_PASS : (a + 1) * K_PASS, :].rearrange("(p j) r -> p j r", j=PACK)
-            raw[a, s, u] = sb([P, PACK, cols], F32, "raw%d%d%d" % (a, s, u), tag="raw%d%d" % (s, u))
-            nc.sync.dma_start(raw[a, s, u][:], rows[:, :, u * cols : (u + 1) * cols])
+            raw[a, s] = sb([P, PACK, R], F32, "raw%d%d" % (a, s), tag=tag)
+            nc.sync.dma_start(raw[a, s][:], rows)
 
-        for s in range(2):
-            for u in range(W_SPLIT):
-                load_raw(0, s, u)
-            if s == 0:
-                nc.sync.dma_start(table[:], tab_words[0].rearrange("p t c -> p (t c)").bitcast(I32))
+        load_raw(0, 0)
+        nc.sync.dma_start(table[:], tab_words[0].rearrange("p t c -> p (t c)").bitcast(I32))
+        load_raw(0, 1)
 
         sm_sb = sb([P, PACK], F32, "sm_sb")
         nc.sync.dma_start(sm_sb[:], sm.rearrange("(p t) -> p t", t=PACK))
@@ -101,38 +99,39 @@ def tile_list_msg_tanh_res_biasP_kernel(
                 moved[32 * q : 32 * q + 4, :, :].bitcast(I32), picked_scales[32 * q + 24 : 32 * q + 32, :].bitcast(I32)
             )
 
-        def look_up(h, tag):
+        load_raw(1, 0, "table_scales")
+
+        def look_up(h, s, tag=None):
             cut = slice(h * HALF_COLS, (h + 1) * HALF_COLS)
-            picked = sb([P, 2, HALF], U32, "picked%d" % h, tag=tag)
-            for s in range(2):
-                nc.vector.tensor_copy(picked[:, s, :], table[:].bitcast(U32).indirect(lists[s][:, cut]))
+            picked = sb([P, HALF], U32, "picked%d%d" % (h, s), tag=tag)
+            nc.vector.tensor_copy(picked[:], table[:].bitcast(U32).indirect(lists[s][:, cut]))
             return picked
 
-        def part(h, picked, tag):
-            parted = sb([P, 2, PASSES, 2 * HALF], U8, "parted%d" % h, tag=tag)
-            for s in range(2):
-                nc.vector.tensor_copy(
-                    parted[:, s, :, :].bitcast(U16),
-                    picked[:, s, :].bitcast(U16).rearrange("p (n d) -> p d n", d=PASSES),
-                )
+        def part(h, s, picked, tag=None):
+            parted = sb([P, PASSES, 2 * HALF], U8, "parted%d%d" % (h, s), tag=tag)
+            nc.vector.tensor_copy(
+                parted[:].bitcast(U16), picked[:].bitcast(U16).rearrange("p (n d) -> p d n", d=PASSES)
+            )
             return parted
 
-        parted0 = part(0, look_up(0, None), None)
+        picked0 = [look_up(0, s) for s in range(2)]
+        parted0 = [part(0, s, picked0[s]) for s in range(2)]
 
         w_codes = {}
         w_scales = {}
         m_cols = P // W_SPLIT
+        cols = R // W_SPLIT
         for a, s in w_order:
             grouped = sb([P, PACK, P, PACK], BF16, "grouped%d%d" % (a, s))
             for u in range(W_SPLIT):
                 dst = grouped[:, :, u * m_cols : (u + 1) * m_cols, :].rearrange("p t m j -> p m j t")
-                src = raw[a, s, u][:].rearrange("p j (m t) -> p m j t", t=PACK)
+                src = raw[a, s][:, :, u * cols : (u + 1) * cols].rearrange("p j (m t) -> p m j t", t=PACK)
                 if (a, s) == w_order[-1] and u == W_SPLIT - 1:
                     nc.vector.tensor_copy(dst, src)
                 else:
                     nc.scalar.activation(dst, src, ACT.Copy)
-                if a + 1 < PASSES:
-                    load_raw(a + 1, s, u)
+            if (a, s) == w_order[0]:
+                load_raw(1, 1, "raw00")
             w_codes[a, s] = sb([P, R], U32, "w_codes%d%d" % (a, s))
             w_scales[a, s] = sb([P, R], U8, "w_scales%d%d" % (a, s))
             nc.vector.quantize_mx(
@@ -140,62 +139,61 @@ def tile_list_msg_tanh_res_biasP_kernel(
             )
 
         wd4_raw = sb([P, 2 * N], U8, "wd4_raw", tag="grouped00")
-        wd8_raw = sb([P, N], I32, "wd8_raw", tag="raw00")
+        wd8_raw = sb([P, N], I32, "wd8_raw", tag="raw01")
         nc.sync.dma_start(wd4_raw[:].bitcast(I32), wd4_words[0].bitcast(I32))
         nc.sync.dma_start(wd8_raw[:], wd8_words[0].rearrange("p n c -> p (n c)").bitcast(I32))
-        wd_scales_raw = sb([P, 2 * N], U8, "wd_scales_raw", tag="grouped01")
-        nc.gpsimd.memset(wd_scales_raw[:].bitcast(I32), 0)
+        wd_scales_raw = sb([P, 2 * N], U8, "wd_scales_raw", tag="picked00")
+        nc.vector.memset(wd_scales_raw[:].bitcast(I32), 0)
         for w, scales in enumerate((wd4_scales, wd8_scales)):
             for q in range(QUADS):
                 nc.sync.dma_start(
                     wd_scales_raw[32 * q : 32 * q + 4, w * N : (w + 1) * N].bitcast(I32),
                     scales[0, 4 * q : 4 * q + 4, :].bitcast(I32),
                 )
-        wgo_sb = sb([P, J], F32, "wgo_sb", tag="raw01")
+        wgo_sb = sb([P, J], F32, "wgo_sb", tag="table_scales")
         nc.sync.dma_start(wgo_sb[:], wgo)
 
-        def first_pass(acc, h, t, a, s, parted):
+        def first_pass(acc, h, t, a, s, parted, order):
             wc = slice(t * P, (t + 1) * P)
             nc.tensor.matmul_mx(
                 acc[:],
                 lhsT=w_codes[a, s][:, wc].bitcast(FP8X4),
                 lhsT_scale=w_scales[a, s][:, wc],
-                rhs=parted[:, s, a, :].bitcast(FP4X4),
+                rhs=parted[s][:, a, :].bitcast(FP4X4),
                 rhs_scale=moved[:, a, s * J + h * HALF : s * J + (h + 1) * HALF],
-                start=(a, s) == w_order[0],
-                stop=(a, s) == w_order[-1],
+                start=(a, s) == order[0],
+                stop=(a, s) == order[-1],
             )
 
-        def activate(h, accs, tag):
-            hidden = sb([P, PACK, HALF], BF16, "hidden%d" % h, tag=tag)
-            for t in range(PACK):
-                th = sb([P, HALF], F32, "th%d%d" % (h, t), tag="th%d" % (t % 2))
-                nc.scalar.activation(th[:], accs[t][:], ACT.Tanh)
-                nc.scalar.activation(hidden[:, t, :], th[:], ACT.Copy, scale=sm_sb[:, t : t + 1])
-            return hidden
+        def quantise_hidden(h, woven, codes, scales):
+            nc.vector.quantize_mx(codes.bitcast(FP8X4), scales, woven[:].rearrange("p n t -> p (n t)"))
 
-        def weave_hidden(h, hidden):
-            woven = sb([P, HALF, PACK], BF16, "woven%d" % h)
-            dst = woven[:].rearrange("p (c i) t -> p c t i", i=4)
-            src = hidden[:].rearrange("p t (c i) -> p c t i", i=4)
-            if h == 0:
-                nc.vector.tensor_copy(dst, src)
-            else:
-                nc.scalar.copy(dst, src)
-            codes = sb([P, HALF], U32, "h_codes%d" % h)
-            scales = sb([P, HALF], U8, "h_scales%d" % h)
-            nc.vector.quantize_mx(codes[:].bitcast(FP8X4), scales[:], woven[:].rearrange("p n t -> p (n t)"))
-            return codes, scales
+        def weave_views(woven, hidden):
+            return (
+                woven[:].rearrange("p (c i) t -> p c t i", i=4),
+                hidden[:].rearrange("p t (c i) -> p c t i", i=4),
+            )
+
+        h_codes = [sb([P, HALF], U32, "h_codes%d" % h) for h in range(2)]
+        h_scales = [sb([P, HALF], U8, "h_scales%d" % h) for h in range(2)]
 
         accs0 = [bank(t, "a0%d" % t) for t in range(PACK)]
         for a, s in w_order:
             for t in range(PACK):
-                first_pass(accs0[t], 0, t, a, s, parted0)
+                first_pass(accs0[t], 0, t, a, s, parted0, w_order)
 
-        picked1 = look_up(1, "grouped11")
+        parted1 = [part(1, 0, look_up(1, 0, "grouped01"))]
 
-        hidden0 = activate(0, accs0, "hidden0")
-        h_codes0, h_scales0 = weave_hidden(0, hidden0)
+        for u in range(2):
+            cut = slice(u * QUARTER, (u + 1) * QUARTER)
+            hidden = sb([P, PACK, QUARTER], BF16, "hidden0%d" % u)
+            for t in range(PACK):
+                th = sb([P, QUARTER], F32, "th0%d%d" % (u, t))
+                nc.scalar.activation(th[:], accs0[t][:, cut], ACT.Tanh)
+                nc.vector.tensor_scalar(hidden[:, t, :], th[:], sm_sb[:, t : t + 1], None, MULT)
+            woven = sb([P, QUARTER, PACK], BF16, "woven0%d" % u)
+            nc.vector.tensor_copy(*weave_views(woven, hidden))
+            quantise_hidden(0, woven, h_codes[0][:, cut], h_scales[0][:, cut])
 
         wd4 = sb([P, PACK, 2 * P], U8, "wd4")
         wd8 = sb([P, PACK, P], I32, "wd8")
@@ -210,9 +208,11 @@ def tile_list_msg_tanh_res_biasP_kernel(
             wd_scales_raw[:].rearrange("p (w m t) -> p w m t", w=2, t=PACK),
         )
 
-        parted1 = part(1, picked1, "woven0")
+        parted1.append(part(1, 1, look_up(1, 1, "woven01")))
+        late_page("woven01")
 
-        def second_layer(h, t, codes, scales):
+        def second_layer(h, t):
+            codes, scales = h_codes[h], h_scales[h]
             acc = bank(PACK + t, "y%d%d" % (h, t))
             nc.tensor.matmul_mx(
                 acc[:], lhsT=wd8[:, t, :].bitcast(FP8X4), lhsT_scale=wd_scales[:, 1, t, :],
@@ -234,21 +234,32 @@ def tile_list_msg_tanh_res_biasP_kernel(
                 MULT,
             )
 
-        ys0 = [second_layer(0, t, h_codes0, h_scales0) for t in range(PACK)]
-        for t in range(PACK - 1):
+        ys0 = [second_layer(0, t) for t in range(PACK - 1)]
+        for t in range(2):
             put(0, t, ys0[t])
 
         accs1 = [bank(t, "a1%d" % t) for t in range(PACK)]
+        by_list = sorted(w_order, key=lambda pair: pair[1])
+        for s in range(2):
+            for t in range(PACK):
+                for a in range(PASSES):
+                    first_pass(accs1[t], 1, t, a, s, parted1, by_list)
+        late_page("message00")
+        late_page("parted11")
+        put(0, 2, ys0[2])
+        hidden = sb([P, PACK, HALF], BF16, "hidden1")
         for t in range(PACK):
-            for a, s in w_order:
-                first_pass(accs1[t], 1, t, a, s, parted1)
-        hidden1 = activate(1, accs1, "hidden1")
-        h_codes1, h_scales1 = weave_hidden(1, hidden1)
-        put(0, PACK - 1, ys0[PACK - 1], tag="hidden1")
+            th = sb([P, HALF], F32, "th1%d" % t, tag="th1%d" % (t % 2))
+            nc.scalar.activation(th[:], accs1[t][:], ACT.Tanh)
+            nc.scalar.activation(hidden[:, t, :], th[:], ACT.Copy, scale=sm_sb[:, t : t + 1])
+        woven = sb([P, HALF, PACK], BF16, "woven1")
+        nc.scalar.copy(*weave_views(woven, hidden))
+        quantise_hidden(1, woven, h_codes[1][:], h_scales[1][:])
+        put(0, PACK - 1, second_layer(0, PACK - 1), tag="hidden1")
 
         out_rows = out_0.rearrange("(p t) c -> t p c", t=PACK)
         pairs = [sb([P, 2, OUT_CHUNK, 2], BF16, "pairs%d" % c) for c in range(OUT_CHUNKS)]
-        ys1 = [second_layer(1, t, h_codes1, h_scales1) for t in range(PACK)]
+        ys1 = [second_layer(1, t) for t in range(PACK)]
         for t in range(PACK):
             put(1, t, ys1[t])
         out_words = out_1[0].rearrange("p t c -> p (t c)").bitcast(I32)
@@ -281,7 +292,7 @@ def tile_list_msg_tanh_res_biasP_kernel(
                     out_words[:, g * 2 * OUT_CHUNK : (g + 1) * 2 * OUT_CHUNK], out_codes[g][:].bitcast(I32)
                 )
         for q in range(QUADS):
-            nc.sync.dma_start(
+            (nc.sync, nc.scalar)[q % 2].dma_start(
                 out_2[0, 4 * q : 4 * q + 4, :].bitcast(I32).rearrange("r (g n) -> g r n", g=OUT_CHUNKS // 2),
                 out_scales[32 * q : 32 * q + 16, :].bitcast(I32),
             )

@@ -51,23 +51,36 @@ def tile_list_msg_tanh_res_biasP_kernel(
         table = sb([P, T], I32, "table")
         table_scales = sb([P, T], U8, "table_scales")
 
-        warm = sb([P, 8], F32, "warm")
-        nc.vector.memset(warm[:], 0.0)
-        nc.scalar.activation(warm[:, 4:5], warm[:, 0:1], ACT.Tanh)
-
         nc.sync.dma_start(src_list[:], offs)
         nc.sync.dma_start(dst_list[:], offs2)
-        for q in range(QUADS):
-            nc.sync.dma_start(
-                table_scales[32 * q + 24 : 32 * q + 32, :].bitcast(I32),
-                tab_scales[:, 4 * q : 4 * q + 4, :].bitcast(I32).rearrange("a r n -> r a n"),
-            )
-            nc.vector.memset(table_scales[32 * q : 32 * q + 24, :].bitcast(I32), 0)
+        nc.sync.dma_start(
+            table_scales[96:P, :].bitcast(I32), tab_scales.bitcast(I32).rearrange("a r n -> r a n")
+        )
+        nc.vector.memset(table_scales[0:96, :].bitcast(I32), 0)
 
         moved = sb([P, PASSES, 2 * J], U8, "moved")
         nc.vector.memset(moved[:].bitcast(I32), 0)
-        pages = [sb([P, T], F32, "page0")]
+        pages = [sb([P, T], F32, "page%d" % t) for t in range(2)]
         nc.vector.memset(pages[0][:], 0.0)
+
+        wd_scales_raw = sb([P, 2 * N], U8, "wd_scales_raw")
+        nc.gpsimd.memset(wd_scales_raw[:].bitcast(I32), 0)
+
+        def load_wd_scales(w):
+            for q in range(QUADS):
+                nc.gpsimd.dma_start(
+                    wd_scales_raw[32 * q : 32 * q + 4, w * N : (w + 1) * N].bitcast(I32),
+                    (wd4_scales, wd8_scales)[w][0, 4 * q : 4 * q + 4, :].bitcast(I32),
+                )
+
+        vectors = sb([P, 16], F32, "vectors")
+        sm_sb = vectors[:, 0:PACK]
+        b_sb = vectors[:, 8 : 8 + PACK]
+        load_wd_scales(0)
+        nc.gpsimd.memset(pages[1][:], 0.0)
+        nc.gpsimd.dma_start(sm_sb, sm.rearrange("(p t) -> p t", t=PACK))
+        load_wd_scales(1)
+        nc.gpsimd.dma_start(b_sb, b.rearrange("(p t) -> p t", t=PACK))
 
         def late_page(tag):
             page = sb([P, T], F32, "page%d" % len(pages), tag=tag)
@@ -86,19 +99,13 @@ def tile_list_msg_tanh_res_biasP_kernel(
         nc.sync.dma_start(table[:], tab_words[0].rearrange("p t c -> p (t c)").bitcast(I32))
         load_raw(0, 1)
 
-        sm_sb = sb([P, PACK], F32, "sm_sb")
-        nc.sync.dma_start(sm_sb[:], sm.rearrange("(p t) -> p t", t=PACK))
-        b_sb = sb([P, PACK], F32, "b_sb")
-        nc.sync.dma_start(b_sb[:], b.rearrange("(p t) -> p t", t=PACK))
-
         picked_scales = sb([P, 2 * J], U8, "picked_scales")
         for s in range(2):
             nc.vector.tensor_copy(picked_scales[:, s * J : (s + 1) * J], table_scales[:].indirect(lists[s][:]))
         for q in range(QUADS):
             nc.sync.dma_start(
-                moved[32 * q : 32 * q + 4, :, :].bitcast(I32), picked_scales[32 * q + 24 : 32 * q + 32, :].bitcast(I32)
+                moved[32 * q : 32 * q + 4, :, :].bitcast(I32), picked_scales[96 + 8 * q : 104 + 8 * q, :].bitcast(I32)
             )
-
         load_raw(1, 0, "table_scales")
 
         def look_up(h, s, tag=None):
@@ -114,14 +121,12 @@ def tile_list_msg_tanh_res_biasP_kernel(
             )
             return parted
 
-        picked0 = [look_up(0, s) for s in range(2)]
-        parted0 = [part(0, s, picked0[s]) for s in range(2)]
-
         w_codes = {}
         w_scales = {}
         m_cols = P // W_SPLIT
         cols = R // W_SPLIT
-        for a, s in w_order:
+
+        def quantise_weight(a, s):
             grouped = sb([P, PACK, P, PACK], BF16, "grouped%d%d" % (a, s))
             for u in range(W_SPLIT):
                 dst = grouped[:, :, u * m_cols : (u + 1) * m_cols, :].rearrange("p t m j -> p m j t")
@@ -130,43 +135,45 @@ def tile_list_msg_tanh_res_biasP_kernel(
                     nc.vector.tensor_copy(dst, src)
                 else:
                     nc.scalar.activation(dst, src, ACT.Copy)
-            if (a, s) == w_order[0]:
-                load_raw(1, 1, "raw00")
             w_codes[a, s] = sb([P, R], U32, "w_codes%d%d" % (a, s))
             w_scales[a, s] = sb([P, R], U8, "w_scales%d%d" % (a, s))
             nc.vector.quantize_mx(
                 w_codes[a, s][:].bitcast(FP8X4), w_scales[a, s][:], grouped[:].rearrange("p t m j -> p (t m j)")
             )
 
-        wd4_raw = sb([P, 2 * N], U8, "wd4_raw", tag="grouped00")
-        wd8_raw = sb([P, N], I32, "wd8_raw", tag="raw01")
-        nc.sync.dma_start(wd4_raw[:].bitcast(I32), wd4_words[0].bitcast(I32))
-        nc.sync.dma_start(wd8_raw[:], wd8_words[0].rearrange("p n c -> p (n c)").bitcast(I32))
-        wd_scales_raw = sb([P, 2 * N], U8, "wd_scales_raw", tag="picked00")
-        nc.vector.memset(wd_scales_raw[:].bitcast(I32), 0)
-        for w, scales in enumerate((wd4_scales, wd8_scales)):
-            for q in range(QUADS):
-                nc.sync.dma_start(
-                    wd_scales_raw[32 * q : 32 * q + 4, w * N : (w + 1) * N].bitcast(I32),
-                    scales[0, 4 * q : 4 * q + 4, :].bitcast(I32),
-                )
-        wgo_sb = sb([P, J], F32, "wgo_sb", tag="table_scales")
+        quantise_weight(0, 0)
+        load_raw(1, 1, "raw00")
+        picked0 = [look_up(0, s) for s in range(2)]
+        parted0 = [part(0, s, picked0[s]) for s in range(2)]
+        for a, s in w_order[1:]:
+            quantise_weight(a, s)
+
+        wd_raw = sb([P, N + N // 2], I32, "wd_raw", tag="picked00")
+        wd8_raw = wd_raw[:, 0:N]
+        wd4_raw = wd_raw[:, N : N + N // 2]
+        nc.sync.dma_start(wd4_raw, wd4_words[0].bitcast(I32))
+        nc.sync.dma_start(wd8_raw, wd8_words[0].rearrange("p n c -> p (n c)").bitcast(I32))
+        wgo_sb = sb([P, J], F32, "wgo_sb", tag="raw01")
         nc.sync.dma_start(wgo_sb[:], wgo)
 
-        def first_pass(acc, h, t, a, s, parted, order):
+        def first_pass(out, h, lo, width, t, a, s, parted, start, stop):
             wc = slice(t * P, (t + 1) * P)
+            at = s * J + h * HALF + lo
             nc.tensor.matmul_mx(
-                acc[:],
+                out,
                 lhsT=w_codes[a, s][:, wc].bitcast(FP8X4),
                 lhsT_scale=w_scales[a, s][:, wc],
-                rhs=parted[s][:, a, :].bitcast(FP4X4),
-                rhs_scale=moved[:, a, s * J + h * HALF : s * J + (h + 1) * HALF],
-                start=(a, s) == order[0],
-                stop=(a, s) == order[-1],
+                rhs=parted[s][:, a, 2 * lo : 2 * (lo + width)].bitcast(FP4X4),
+                rhs_scale=moved[:, a, at : at + width],
+                start=start,
+                stop=stop,
             )
 
-        def quantise_hidden(h, woven, codes, scales):
-            nc.vector.quantize_mx(codes.bitcast(FP8X4), scales, woven[:].rearrange("p n t -> p (n t)"))
+        def quantise_hidden(name, woven, width):
+            codes = sb([P, width], U32, "h_codes" + name)
+            scales = sb([P, width], U8, "h_scales" + name)
+            nc.vector.quantize_mx(codes[:].bitcast(FP8X4), scales[:], woven[:].rearrange("p n t -> p (n t)"))
+            return codes, scales
 
         def weave_views(woven, hidden):
             return (
@@ -174,94 +181,111 @@ def tile_list_msg_tanh_res_biasP_kernel(
                 hidden[:].rearrange("p t (c i) -> p c t i", i=4),
             )
 
-        h_codes = [sb([P, HALF], U32, "h_codes%d" % h) for h in range(2)]
-        h_scales = [sb([P, HALF], U8, "h_scales%d" % h) for h in range(2)]
-
-        accs0 = [bank(t, "a0%d" % t) for t in range(PACK)]
+        accs0 = [bank(e, "a0%d" % e) for e in range(HALF // P)]
         for a, s in w_order:
-            for t in range(PACK):
-                first_pass(accs0[t], 0, t, a, s, parted0, w_order)
+            for e in range(HALF // P):
+                for t in range(PACK):
+                    first_pass(
+                        accs0[e][:, t * P : (t + 1) * P], 0, e * P, P, t, a, s, parted0,
+                        (a, s) == w_order[0] and t == 0, (a, s) == w_order[-1] and t == PACK - 1,
+                    )
 
-        parted1 = [part(1, 0, look_up(1, 0, "grouped01"))]
-
-        for u in range(2):
-            cut = slice(u * QUARTER, (u + 1) * QUARTER)
-            hidden = sb([P, PACK, QUARTER], BF16, "hidden0%d" % u)
-            for t in range(PACK):
-                th = sb([P, QUARTER], F32, "th0%d%d" % (u, t))
-                nc.scalar.activation(th[:], accs0[t][:, cut], ACT.Tanh)
-                nc.vector.tensor_scalar(hidden[:, t, :], th[:], sm_sb[:, t : t + 1], None, MULT)
-            woven = sb([P, QUARTER, PACK], BF16, "woven0%d" % u)
-            nc.vector.tensor_copy(*weave_views(woven, hidden))
-            quantise_hidden(0, woven, h_codes[0][:, cut], h_scales[0][:, cut])
+        picked10 = look_up(1, 0, "grouped01")
+        parted1 = [part(1, 0, picked10)]
 
         wd4 = sb([P, PACK, 2 * P], U8, "wd4")
         wd8 = sb([P, PACK, P], I32, "wd8")
-        wd_scales = sb([P, 2, PACK, P], U8, "wd_scales")
+        wd_scales = sb([P, 2, PACK, P], U8, "wd_scales", tag="grouped10")
         nc.vector.tensor_copy(
             wd4[:].bitcast(U16).rearrange("p t m -> p m t"),
-            wd4_raw[:].bitcast(U16).rearrange("p (m t) -> p m t", t=PACK),
+            wd4_raw.bitcast(U16).rearrange("p (m t) -> p m t", t=PACK),
         )
-        nc.vector.tensor_copy(wd8[:].rearrange("p t m -> p m t"), wd8_raw[:].rearrange("p (m t) -> p m t", t=PACK))
+        nc.vector.tensor_copy(wd8[:].rearrange("p t m -> p m t"), wd8_raw.rearrange("p (m t) -> p m t", t=PACK))
         nc.vector.tensor_copy(
             wd_scales[:].rearrange("p w t m -> p w m t"),
             wd_scales_raw[:].rearrange("p (w m t) -> p w m t", w=2, t=PACK),
         )
 
-        parted1.append(part(1, 1, look_up(1, 1, "woven01")))
-        late_page("woven01")
+        woven_a = sb([P, QUARTER, PACK], BF16, "woven_a")
+        for e in range(2):
+            th = sb([P, P, PACK], F32, "th_a%d" % e)
+            nc.scalar.activation(th[:], accs0[e][:].rearrange("p (t n) -> p n t", t=PACK), ACT.Tanh)
+            nc.vector.tensor_tensor(
+                woven_a[:, e * P : (e + 1) * P, :], th[:], sm_sb.unsqueeze(1).to_broadcast([P, P, PACK]), MULT
+            )
+        h_a = quantise_hidden("a", woven_a, QUARTER)
 
-        def second_layer(h, t):
-            codes, scales = h_codes[h], h_scales[h]
-            acc = bank(PACK + t, "y%d%d" % (h, t))
+        th_b = sb([P, 2, PACK, P], F32, "th_b")
+        for e in range(2):
+            nc.scalar.activation(th_b[:, e, :, :].rearrange("p t n -> p (t n)"), accs0[2 + e][:], ACT.Tanh)
+
+        parted1.append(part(1, 1, look_up(1, 1, "woven_a")))
+        late_page("woven_a")
+
+        def second_layer(name, hidden_mx, width, t):
+            codes, scales = hidden_mx
+            acc = bank(PACK + t, "y%s%d" % (name, t))
             nc.tensor.matmul_mx(
-                acc[:], lhsT=wd8[:, t, :].bitcast(FP8X4), lhsT_scale=wd_scales[:, 1, t, :],
+                acc[:, 0:width], lhsT=wd8[:, t, :].bitcast(FP8X4), lhsT_scale=wd_scales[:, 1, t, :],
                 rhs=codes[:].bitcast(FP8X4), rhs_scale=scales[:], start=True, stop=False,
             )
-            nc.tensor.matmul_mx(
-                acc[:], lhsT=wd4[:, t, :].bitcast(FP4X4), lhsT_scale=wd_scales[:, 0, t, :],
-                rhs=codes[:].bitcast(FP8X4), rhs_scale=scales[:], start=False, stop=True,
-            )
+            step = HALF if width == HALF else P
+            for lo in range(0, width, step):
+                nc.tensor.matmul_mx(
+                    acc[:, lo : lo + step], lhsT=wd4[:, t, :].bitcast(FP4X4), lhsT_scale=wd_scales[:, 0, t, :],
+                    rhs=codes[:, lo : lo + step].bitcast(FP8X4), rhs_scale=scales[:, lo : lo + step],
+                    start=False, stop=lo + step == width,
+                )
             return acc
 
-        def put(h, t, acc, tag=None):
-            message = sb([P, HALF], F32, "message%d%d" % (h, t), tag=tag)
-            nc.scalar.activation(message[:], acc[:], ACT.Identity, bias=b_sb[:, t : t + 1])
+        def put(name, lo, width, t, acc, tag=None):
+            message = sb([P, width], F32, "message%s%d" % (name, t), tag=tag)
+            nc.scalar.activation(message[:], acc[:, 0:width], ACT.Identity, bias=b_sb[:, t : t + 1])
             nc.vector.tensor_tensor(
-                pages[t][:].indirect(dst_list[:, h * HALF_COLS : (h + 1) * HALF_COLS]),
+                pages[t][:].indirect(dst_list[:, lo // 16 : (lo + width) // 16]),
                 message[:],
-                wgo_sb[:, h * HALF : (h + 1) * HALF],
+                wgo_sb[:, lo : lo + width],
                 MULT,
             )
 
-        ys0 = [second_layer(0, t) for t in range(PACK - 1)]
-        for t in range(2):
-            put(0, t, ys0[t])
+        ys_a = [second_layer("a", h_a, QUARTER, t) for t in range(PACK)]
+        put("a", 0, QUARTER, 0, ys_a[0])
+        late_page("messagea0")
+        for t in range(1, PACK - 1):
+            put("a", 0, QUARTER, t, ys_a[t])
 
-        accs1 = [bank(t, "a1%d" % t) for t in range(PACK)]
-        by_list = sorted(w_order, key=lambda pair: pair[1])
-        for s in range(2):
-            for t in range(PACK):
-                for a in range(PASSES):
-                    first_pass(accs1[t], 1, t, a, s, parted1, by_list)
-        late_page("message00")
-        late_page("parted11")
-        put(0, 2, ys0[2])
-        hidden = sb([P, PACK, HALF], BF16, "hidden1")
+        hidden_b = sb([P, PACK, QUARTER], BF16, "hidden_b")
         for t in range(PACK):
-            th = sb([P, HALF], F32, "th1%d" % t, tag="th1%d" % (t % 2))
-            nc.scalar.activation(th[:], accs1[t][:], ACT.Tanh)
-            nc.scalar.activation(hidden[:, t, :], th[:], ACT.Copy, scale=sm_sb[:, t : t + 1])
-        woven = sb([P, HALF, PACK], BF16, "woven1")
-        nc.scalar.copy(*weave_views(woven, hidden))
-        quantise_hidden(1, woven, h_codes[1][:], h_scales[1][:])
-        put(0, PACK - 1, second_layer(0, PACK - 1), tag="hidden1")
+            nc.scalar.activation(
+                hidden_b[:, t, :].rearrange("p (e n) -> p e n", e=2), th_b[:, :, t, :], ACT.Copy,
+                scale=sm_sb[:, t : t + 1],
+            )
+        woven_b = sb([P, QUARTER, PACK], BF16, "woven_b", tag="h_codesa")
+        nc.scalar.copy(*weave_views(woven_b, hidden_b))
+        h_b = quantise_hidden("b", woven_b, QUARTER)
+        put("a", 0, QUARTER, PACK - 1, ys_a[PACK - 1], tag="hidden_b")
+        ys_b = [second_layer("b", h_b, QUARTER, t) for t in range(PACK)]
+        for t in range(PACK - 1):
+            put("b", QUARTER, QUARTER, t, ys_b[t])
+
+        hidden_c = sb([P, PACK, HALF], BF16, "hidden_c")
+        for t in range(PACK):
+            acc = bank(t, "a1%d" % t)
+            for a, s in w_order:
+                first_pass(acc[:], 1, 0, HALF, t, a, s, parted1, (a, s) == w_order[0], (a, s) == w_order[-1])
+            th = sb([P, HALF], F32, "th_c%d" % t, tag="th_c%d" % (t % 2))
+            nc.scalar.activation(th[:], acc[:], ACT.Tanh)
+            nc.scalar.activation(hidden_c[:, t, :], th[:], ACT.Copy, scale=sm_sb[:, t : t + 1])
+        woven_c = sb([P, HALF, PACK], BF16, "woven_c")
+        nc.scalar.copy(*weave_views(woven_c, hidden_c))
+        h_c = quantise_hidden("c", woven_c, HALF)
+        put("b", QUARTER, QUARTER, PACK - 1, ys_b[PACK - 1], tag="hidden_c")
 
         out_rows = out_0.rearrange("(p t) c -> t p c", t=PACK)
         pairs = [sb([P, 2, OUT_CHUNK, 2], BF16, "pairs%d" % c) for c in range(OUT_CHUNKS)]
-        ys1 = [second_layer(1, t) for t in range(PACK)]
+        ys_c = [second_layer("c", h_c, HALF, t) for t in range(PACK)]
         for t in range(PACK):
-            put(1, t, ys1[t])
+            put("c", HALF, HALF, t, ys_c[t])
         out_words = out_1[0].rearrange("p t c -> p (t c)").bitcast(I32)
         out_scales = sb([P, 2 * OUT_CHUNK], U8, "out_scales")
         out_codes = [sb([P, 2 * OUT_CHUNK], U32, "out_codes%d" % g) for g in range(OUT_CHUNKS // 2)]

@@ -24,8 +24,8 @@ QUADS = 4
 HALF = J // 2
 HALF_COLS = HALF // 16
 W_SPLIT = 2
-OUT_CHUNK = 256
-OUT_CHUNKS = T // OUT_CHUNK
+OUT_GROUP = 512
+OUT_WIDTHS = (256, 256, 512, 512, 256, 256)
 SCALAR_WEAVES = 2
 QUARTER = HALF // 2
 
@@ -56,31 +56,20 @@ def tile_list_msg_tanh_res_biasP_kernel(
         nc.sync.dma_start(
             table_scales[96:P, :].bitcast(I32), tab_scales.bitcast(I32).rearrange("a r n -> r a n")
         )
-        nc.vector.memset(table_scales[0:96, :].bitcast(I32), 0)
-
-        moved = sb([P, PASSES, 2 * J], U8, "moved")
-        nc.vector.memset(moved[:].bitcast(I32), 0)
-        pages = [sb([P, T], F32, "page%d" % t) for t in range(2)]
-        nc.vector.memset(pages[0][:], 0.0)
-
+        nc.gpsimd.memset(table_scales[0:96, :].bitcast(I32), 0)
         wd_scales_raw = sb([P, 2 * N], U8, "wd_scales_raw")
         nc.gpsimd.memset(wd_scales_raw[:].bitcast(I32), 0)
-
-        def load_wd_scales(w):
+        for w, scales in enumerate((wd4_scales, wd8_scales)):
             for q in range(QUADS):
                 nc.gpsimd.dma_start(
                     wd_scales_raw[32 * q : 32 * q + 4, w * N : (w + 1) * N].bitcast(I32),
-                    (wd4_scales, wd8_scales)[w][0, 4 * q : 4 * q + 4, :].bitcast(I32),
+                    scales[0, 4 * q : 4 * q + 4, :].bitcast(I32),
                 )
 
-        vectors = sb([P, 16], F32, "vectors")
-        sm_sb = vectors[:, 0:PACK]
-        b_sb = vectors[:, 8 : 8 + PACK]
-        load_wd_scales(0)
-        nc.gpsimd.memset(pages[1][:], 0.0)
-        nc.gpsimd.dma_start(sm_sb, sm.rearrange("(p t) -> p t", t=PACK))
-        load_wd_scales(1)
-        nc.gpsimd.dma_start(b_sb, b.rearrange("(p t) -> p t", t=PACK))
+        moved = sb([P, 2, PASSES, J], U8, "moved")
+        nc.vector.memset(moved[:].rearrange("p h a n -> p (h a n)").bitcast(I32), 0)
+        pages = [sb([P, T], F32, "page0")]
+        nc.vector.memset(pages[0][:], 0.0)
 
         def late_page(tag):
             page = sb([P, T], F32, "page%d" % len(pages), tag=tag)
@@ -98,14 +87,28 @@ def tile_list_msg_tanh_res_biasP_kernel(
         load_raw(0, 0)
         nc.sync.dma_start(table[:], tab_words[0].rearrange("p t c -> p (t c)").bitcast(I32))
         load_raw(0, 1)
+        vectors = sb([P, 16], F32, "vectors")
+        sm_sb = vectors[:, 0:PACK]
+        b_sb = vectors[:, 8 : 8 + PACK]
+        nc.sync.dma_start(sm_sb, sm.rearrange("(p t) -> p t", t=PACK))
+        nc.sync.dma_start(b_sb, b.rearrange("(p t) -> p t", t=PACK))
 
-        picked_scales = sb([P, 2 * J], U8, "picked_scales")
-        for s in range(2):
-            nc.vector.tensor_copy(picked_scales[:, s * J : (s + 1) * J], table_scales[:].indirect(lists[s][:]))
-        for q in range(QUADS):
-            nc.sync.dma_start(
-                moved[32 * q : 32 * q + 4, :, :].bitcast(I32), picked_scales[96 + 8 * q : 104 + 8 * q, :].bitcast(I32)
-            )
+        picked_scales = [sb([P, 2 * HALF], U8, "picked_scales%d" % h) for h in range(2)]
+        for h in range(2):
+            cut = slice(h * HALF_COLS, (h + 1) * HALF_COLS)
+            for s in range(2):
+                nc.vector.tensor_copy(
+                    picked_scales[h][:, s * HALF : (s + 1) * HALF], table_scales[:].indirect(lists[s][:, cut])
+                )
+
+        def move_scales(h):
+            for q in range(QUADS):
+                nc.sync.dma_start(
+                    moved[32 * q : 32 * q + 4, h, :, :].bitcast(I32),
+                    picked_scales[h][96 + 8 * q : 104 + 8 * q, :].bitcast(I32),
+                )
+
+        move_scales(0)
         load_raw(1, 0, "table_scales")
 
         def look_up(h, s, tag=None):
@@ -131,7 +134,7 @@ def tile_list_msg_tanh_res_biasP_kernel(
             for u in range(W_SPLIT):
                 dst = grouped[:, :, u * m_cols : (u + 1) * m_cols, :].rearrange("p t m j -> p m j t")
                 src = raw[a, s][:, :, u * cols : (u + 1) * cols].rearrange("p j (m t) -> p m j t", t=PACK)
-                if (a, s) == w_order[-1] and u == W_SPLIT - 1:
+                if (a, s) == w_order[-1]:
                     nc.vector.tensor_copy(dst, src)
                 else:
                     nc.scalar.activation(dst, src, ACT.Copy)
@@ -143,12 +146,13 @@ def tile_list_msg_tanh_res_biasP_kernel(
 
         quantise_weight(0, 0)
         load_raw(1, 1, "raw00")
+        move_scales(1)
         picked0 = [look_up(0, s) for s in range(2)]
         parted0 = [part(0, s, picked0[s]) for s in range(2)]
         for a, s in w_order[1:]:
             quantise_weight(a, s)
 
-        wd_raw = sb([P, N + N // 2], I32, "wd_raw", tag="picked00")
+        wd_raw = sb([P, N + N // 2], I32, "wd_raw", tag="grouped00")
         wd8_raw = wd_raw[:, 0:N]
         wd4_raw = wd_raw[:, N : N + N // 2]
         nc.sync.dma_start(wd4_raw, wd4_words[0].bitcast(I32))
@@ -158,13 +162,13 @@ def tile_list_msg_tanh_res_biasP_kernel(
 
         def first_pass(out, h, lo, width, t, a, s, parted, start, stop):
             wc = slice(t * P, (t + 1) * P)
-            at = s * J + h * HALF + lo
+            at = s * HALF + lo
             nc.tensor.matmul_mx(
                 out,
                 lhsT=w_codes[a, s][:, wc].bitcast(FP8X4),
                 lhsT_scale=w_scales[a, s][:, wc],
                 rhs=parted[s][:, a, 2 * lo : 2 * (lo + width)].bitcast(FP4X4),
-                rhs_scale=moved[:, a, at : at + width],
+                rhs_scale=moved[:, h, a, at : at + width],
                 start=start,
                 stop=stop,
             )
@@ -173,7 +177,7 @@ def tile_list_msg_tanh_res_biasP_kernel(
             codes = sb([P, width], U32, "h_codes" + name)
             scales = sb([P, width], U8, "h_scales" + name)
             nc.vector.quantize_mx(codes[:].bitcast(FP8X4), scales[:], woven[:].rearrange("p n t -> p (n t)"))
-            return codes, scales
+            return codes[:], scales[:]
 
         def weave_views(woven, hidden):
             return (
@@ -190,8 +194,31 @@ def tile_list_msg_tanh_res_biasP_kernel(
                         (a, s) == w_order[0] and t == 0, (a, s) == w_order[-1] and t == PACK - 1,
                     )
 
-        picked10 = look_up(1, 0, "grouped01")
-        parted1 = [part(1, 0, picked10)]
+        parted1 = [part(1, s, look_up(1, s, ("grouped01", "grouped11")[s])) for s in range(2)]
+
+        h_codes = sb([P, HALF], U32, "h_codes0")
+        h_scales = sb([P, HALF], U8, "h_scales0")
+
+        def squash(e):
+            th = sb([P, P, PACK], F32, "th%d" % e)
+            nc.scalar.activation(th[:], accs0[e][:].rearrange("p (t n) -> p n t", t=PACK), ACT.Tanh)
+            return th
+
+        def smooth(u):
+            woven = sb([P, QUARTER, PACK], BF16, "woven%d" % u)
+            for e in range(2):
+                nc.vector.tensor_tensor(
+                    woven[:, e * P : (e + 1) * P, :],
+                    squash(2 * u + e)[:],
+                    sm_sb.unsqueeze(1).to_broadcast([P, P, PACK]),
+                    MULT,
+                )
+            cut = slice(u * QUARTER, (u + 1) * QUARTER)
+            nc.vector.quantize_mx(
+                h_codes[:, cut].bitcast(FP8X4), h_scales[:, cut], woven[:].rearrange("p n t -> p (n t)")
+            )
+
+        smooth(0)
 
         wd4 = sb([P, PACK, 2 * P], U8, "wd4")
         wd8 = sb([P, PACK, P], I32, "wd8")
@@ -206,28 +233,15 @@ def tile_list_msg_tanh_res_biasP_kernel(
             wd_scales_raw[:].rearrange("p (w m t) -> p w m t", w=2, t=PACK),
         )
 
-        woven_a = sb([P, QUARTER, PACK], BF16, "woven_a")
-        for e in range(2):
-            th = sb([P, P, PACK], F32, "th_a%d" % e)
-            nc.scalar.activation(th[:], accs0[e][:].rearrange("p (t n) -> p n t", t=PACK), ACT.Tanh)
-            nc.vector.tensor_tensor(
-                woven_a[:, e * P : (e + 1) * P, :], th[:], sm_sb.unsqueeze(1).to_broadcast([P, P, PACK]), MULT
-            )
-        h_a = quantise_hidden("a", woven_a, QUARTER)
-
-        th_b = sb([P, 2, PACK, P], F32, "th_b")
-        for e in range(2):
-            nc.scalar.activation(th_b[:, e, :, :].rearrange("p t n -> p (t n)"), accs0[2 + e][:], ACT.Tanh)
-
-        parted1.append(part(1, 1, look_up(1, 1, "woven_a")))
-        late_page("woven_a")
+        smooth(1)
+        late_page("woven1")
 
         def second_layer(name, hidden_mx, width, t):
             codes, scales = hidden_mx
             acc = bank(PACK + t, "y%s%d" % (name, t))
             nc.tensor.matmul_mx(
                 acc[:, 0:width], lhsT=wd8[:, t, :].bitcast(FP8X4), lhsT_scale=wd_scales[:, 1, t, :],
-                rhs=codes[:].bitcast(FP8X4), rhs_scale=scales[:], start=True, stop=False,
+                rhs=codes.bitcast(FP8X4), rhs_scale=scales, start=True, stop=False,
             )
             step = HALF if width == HALF else P
             for lo in range(0, width, step):
@@ -248,25 +262,14 @@ def tile_list_msg_tanh_res_biasP_kernel(
                 MULT,
             )
 
-        ys_a = [second_layer("a", h_a, QUARTER, t) for t in range(PACK)]
-        put("a", 0, QUARTER, 0, ys_a[0])
-        late_page("messagea0")
+        for u in range(2):
+            cut = slice(u * QUARTER, (u + 1) * QUARTER)
+            name = "q%d" % u
+            put(name, cut.start, QUARTER, 0, second_layer(name, (h_codes[:, cut], h_scales[:, cut]), QUARTER, 0))
+            late_page("message%s0" % name)
+        ys_a = {t: second_layer("a", (h_codes[:], h_scales[:]), HALF, t) for t in range(1, PACK)}
         for t in range(1, PACK - 1):
-            put("a", 0, QUARTER, t, ys_a[t])
-
-        hidden_b = sb([P, PACK, QUARTER], BF16, "hidden_b")
-        for t in range(PACK):
-            nc.scalar.activation(
-                hidden_b[:, t, :].rearrange("p (e n) -> p e n", e=2), th_b[:, :, t, :], ACT.Copy,
-                scale=sm_sb[:, t : t + 1],
-            )
-        woven_b = sb([P, QUARTER, PACK], BF16, "woven_b", tag="h_codesa")
-        nc.scalar.copy(*weave_views(woven_b, hidden_b))
-        h_b = quantise_hidden("b", woven_b, QUARTER)
-        put("a", 0, QUARTER, PACK - 1, ys_a[PACK - 1], tag="hidden_b")
-        ys_b = [second_layer("b", h_b, QUARTER, t) for t in range(PACK)]
-        for t in range(PACK - 1):
-            put("b", QUARTER, QUARTER, t, ys_b[t])
+            put("a", 0, HALF, t, ys_a[t])
 
         hidden_c = sb([P, PACK, HALF], BF16, "hidden_c")
         for t in range(PACK):
@@ -279,44 +282,52 @@ def tile_list_msg_tanh_res_biasP_kernel(
         woven_c = sb([P, HALF, PACK], BF16, "woven_c")
         nc.scalar.copy(*weave_views(woven_c, hidden_c))
         h_c = quantise_hidden("c", woven_c, HALF)
-        put("b", QUARTER, QUARTER, PACK - 1, ys_b[PACK - 1], tag="hidden_c")
+        put("a", 0, HALF, PACK - 1, ys_a[PACK - 1], tag="hidden_c")
 
         out_rows = out_0.rearrange("(p t) c -> t p c", t=PACK)
-        pairs = [sb([P, 2, OUT_CHUNK, 2], BF16, "pairs%d" % c) for c in range(OUT_CHUNKS)]
+        starts = [sum(OUT_WIDTHS[:c]) for c in range(len(OUT_WIDTHS))]
+        pairs = [sb([P, 2, width, 2], BF16, "pairs%d" % c) for c, width in enumerate(OUT_WIDTHS)]
         ys_c = [second_layer("c", h_c, HALF, t) for t in range(PACK)]
         for t in range(PACK):
             put("c", HALF, HALF, t, ys_c[t])
         out_words = out_1[0].rearrange("p t c -> p (t c)").bitcast(I32)
-        out_scales = sb([P, 2 * OUT_CHUNK], U8, "out_scales")
-        out_codes = [sb([P, 2 * OUT_CHUNK], U32, "out_codes%d" % g) for g in range(OUT_CHUNKS // 2)]
+        out_scales = sb([P, OUT_GROUP], U8, "out_scales")
+        out_codes = [sb([P, OUT_GROUP], U32, "out_codes%d" % g) for g in range(T // OUT_GROUP)]
         for t in range(PACK):
             nc.sync.dma_start(out_rows[t], pages[t][:])
-            for c in range(OUT_CHUNKS):
-                nc.scalar.activation(
-                    pairs[c][:, t // 2, :, t % 2], pages[t][:, c * OUT_CHUNK : (c + 1) * OUT_CHUNK], ACT.Copy
-                )
-        for c in range(OUT_CHUNKS):
-            g, e = divmod(c, 2)
-            woven_out = sb([P, OUT_CHUNK, PACK], BF16, "woven_out%d" % c)
-            word = U32 if c >= OUT_CHUNKS - SCALAR_WEAVES else I32
+            for c, width in enumerate(OUT_WIDTHS):
+                nc.scalar.activation(pairs[c][:, t // 2, :, t % 2], pages[t][:, starts[c] : starts[c] + width], ACT.Copy)
+
+        def weave_out(c):
+            on_scalar = c >= len(OUT_WIDTHS) - SCALAR_WEAVES
+            woven_out = sb([P, OUT_WIDTHS[c], PACK], BF16, "woven_out%d" % c)
+            word = U32 if on_scalar else I32
             dst = woven_out[:].rearrange("p n t -> p (n t)").bitcast(word).rearrange("p (n u) -> p n u", u=2)
             src = pairs[c][:].rearrange("p u n e -> p u (n e)").bitcast(word).rearrange("p u n -> p n u")
-            if c >= OUT_CHUNKS - SCALAR_WEAVES:
+            if on_scalar:
                 nc.scalar.copy(dst, src)
             else:
                 nc.vector.tensor_copy(dst, src)
-            cut = slice(e * OUT_CHUNK, (e + 1) * OUT_CHUNK)
+            return woven_out
+
+        def quantise_out(c, woven_out):
+            g, lo = divmod(starts[c], OUT_GROUP)
+            cut = slice(lo, lo + OUT_WIDTHS[c])
             nc.vector.quantize_mx(
                 out_codes[g][:, cut].bitcast(FP8X4),
                 out_scales[4 * g : P, cut],
                 woven_out[:].rearrange("p n t -> p (n t)"),
             )
-            if e == 1:
-                nc.sync.dma_start(
-                    out_words[:, g * 2 * OUT_CHUNK : (g + 1) * 2 * OUT_CHUNK], out_codes[g][:].bitcast(I32)
-                )
+            if cut.stop == OUT_GROUP:
+                nc.sync.dma_start(out_words[:, g * OUT_GROUP : (g + 1) * OUT_GROUP], out_codes[g][:].bitcast(I32))
+
+        woven_outs = [weave_out(0)]
+        for c in range(len(OUT_WIDTHS)):
+            if c + 1 < len(OUT_WIDTHS):
+                woven_outs.append(weave_out(c + 1))
+            quantise_out(c, woven_outs[c])
         for q in range(QUADS):
             (nc.sync, nc.scalar)[q % 2].dma_start(
-                out_2[0, 4 * q : 4 * q + 4, :].bitcast(I32).rearrange("r (g n) -> g r n", g=OUT_CHUNKS // 2),
+                out_2[0, 4 * q : 4 * q + 4, :].bitcast(I32).rearrange("r (g n) -> g r n", g=T // OUT_GROUP),
                 out_scales[32 * q : 32 * q + 16, :].bitcast(I32),
             )

@@ -21,13 +21,14 @@ PACK = 4
 K_PASS = P * PACK
 PASSES = K // K_PASS
 QUADS = 4
+LAST_QUAD = P - 32
+LIST_ROWS = 16
 HALF = J // 2
-HALF_COLS = HALF // 16
+QUARTER = HALF // 2
 W_SPLIT = 2
 OUT_GROUP = 512
-OUT_WIDTHS = (256, 256, 512, 512, 256, 256)
+OUT_WIDTHS = (128, 128, 256, 512, 512, 256, 256)
 SCALAR_WEAVES = 2
-QUARTER = HALF // 2
 
 
 def tile_list_msg_tanh_res_biasP_kernel(
@@ -45,18 +46,22 @@ def tile_list_msg_tanh_res_biasP_kernel(
         def bank(i, name):
             return psum.tile([P, HALF], F32, name=name, tag="bank%d" % i)
 
-        src_list = keep.tile([P, J // 16], U16, name="src_list")
-        dst_list = keep.tile([P, J // 16], U16, name="dst_list")
+        src_list = keep.tile([P, J // LIST_ROWS], U16, name="src_list")
+        dst_list = keep.tile([P, J // LIST_ROWS], U16, name="dst_list")
         lists = (src_list, dst_list)
         table = sb([P, T], I32, "table")
         table_scales = sb([P, T], U8, "table_scales")
 
+        def entries(s, lo, width):
+            return lists[s][:, lo // LIST_ROWS : (lo + width) // LIST_ROWS]
+
+        nc.sync.dma_start(
+            table_scales[LAST_QUAD:P, :].bitcast(I32), tab_scales.bitcast(I32).rearrange("a r n -> r a n")
+        )
         nc.sync.dma_start(src_list[:], offs)
         nc.sync.dma_start(dst_list[:], offs2)
-        nc.sync.dma_start(
-            table_scales[96:P, :].bitcast(I32), tab_scales.bitcast(I32).rearrange("a r n -> r a n")
-        )
-        nc.gpsimd.memset(table_scales[0:96, :].bitcast(I32), 0)
+        nc.gpsimd.memset(table_scales[0:LAST_QUAD, :].bitcast(I32), 0)
+
         wd_scales_raw = sb([P, 2 * N], U8, "wd_scales_raw")
         nc.gpsimd.memset(wd_scales_raw[:].bitcast(I32), 0)
         for w, scales in enumerate((wd4_scales, wd8_scales)):
@@ -66,8 +71,9 @@ def tile_list_msg_tanh_res_biasP_kernel(
                     scales[0, 4 * q : 4 * q + 4, :].bitcast(I32),
                 )
 
-        moved = sb([P, 2, PASSES, J], U8, "moved")
-        nc.vector.memset(moved[:].rearrange("p h a n -> p (h a n)").bitcast(I32), 0)
+        edge_scales = sb([P, 2, PASSES, J], U8, "edge_scales")
+        nc.vector.memset(edge_scales[:].rearrange("p h a n -> p (h a n)").bitcast(I32), 0)
+
         pages = [sb([P, T], F32, "page0")]
         nc.vector.memset(pages[0][:], 0.0)
 
@@ -87,38 +93,42 @@ def tile_list_msg_tanh_res_biasP_kernel(
         load_raw(0, 0)
         nc.sync.dma_start(table[:], tab_words[0].rearrange("p t c -> p (t c)").bitcast(I32))
         load_raw(0, 1)
+
         vectors = sb([P, 16], F32, "vectors")
         sm_sb = vectors[:, 0:PACK]
         b_sb = vectors[:, 8 : 8 + PACK]
-        nc.sync.dma_start(sm_sb, sm.rearrange("(p t) -> p t", t=PACK))
-        nc.sync.dma_start(b_sb, b.rearrange("(p t) -> p t", t=PACK))
+        nc.scalar.dma_start(sm_sb, sm.rearrange("(p t) -> p t", t=PACK))
+        nc.scalar.dma_start(b_sb, b.rearrange("(p t) -> p t", t=PACK))
+
+        sm_rows = sb([P, P, PACK], F32, "sm_rows")
+        nc.scalar.activation(sm_rows[:], sm_sb.unsqueeze(1).to_broadcast([P, P, PACK]), ACT.Copy)
 
         picked_scales = [sb([P, 2 * HALF], U8, "picked_scales%d" % h) for h in range(2)]
         for h in range(2):
-            cut = slice(h * HALF_COLS, (h + 1) * HALF_COLS)
             for s in range(2):
                 nc.vector.tensor_copy(
-                    picked_scales[h][:, s * HALF : (s + 1) * HALF], table_scales[:].indirect(lists[s][:, cut])
+                    picked_scales[h][:, s * HALF : (s + 1) * HALF],
+                    table_scales[:].indirect(entries(s, h * HALF, HALF)),
                 )
 
         def move_scales(h):
             for q in range(QUADS):
+                first = LAST_QUAD + 8 * q
                 nc.sync.dma_start(
-                    moved[32 * q : 32 * q + 4, h, :, :].bitcast(I32),
-                    picked_scales[h][96 + 8 * q : 104 + 8 * q, :].bitcast(I32),
+                    edge_scales[32 * q : 32 * q + 4, h, :, :].bitcast(I32),
+                    picked_scales[h][first : first + 8, :].bitcast(I32),
                 )
 
         move_scales(0)
         load_raw(1, 0, "table_scales")
 
         def look_up(h, s, tag=None):
-            cut = slice(h * HALF_COLS, (h + 1) * HALF_COLS)
             picked = sb([P, HALF], U32, "picked%d%d" % (h, s), tag=tag)
-            nc.vector.tensor_copy(picked[:], table[:].bitcast(U32).indirect(lists[s][:, cut]))
+            nc.vector.tensor_copy(picked[:], table[:].bitcast(U32).indirect(entries(s, h * HALF, HALF)))
             return picked
 
-        def part(h, s, picked, tag=None):
-            parted = sb([P, PASSES, 2 * HALF], U8, "parted%d%d" % (h, s), tag=tag)
+        def part(h, s, picked):
+            parted = sb([P, PASSES, 2 * HALF], U8, "parted%d%d" % (h, s))
             nc.vector.tensor_copy(
                 parted[:].bitcast(U16), picked[:].bitcast(U16).rearrange("p (n d) -> p d n", d=PASSES)
             )
@@ -127,14 +137,14 @@ def tile_list_msg_tanh_res_biasP_kernel(
         w_codes = {}
         w_scales = {}
         m_cols = P // W_SPLIT
-        cols = R // W_SPLIT
+        r_cols = R // W_SPLIT
 
         def quantise_weight(a, s):
             grouped = sb([P, PACK, P, PACK], BF16, "grouped%d%d" % (a, s))
             for u in range(W_SPLIT):
                 dst = grouped[:, :, u * m_cols : (u + 1) * m_cols, :].rearrange("p t m j -> p m j t")
-                src = raw[a, s][:, :, u * cols : (u + 1) * cols].rearrange("p j (m t) -> p m j t", t=PACK)
-                if (a, s) == w_order[-1]:
+                src = raw[a, s][:, :, u * r_cols : (u + 1) * r_cols].rearrange("p j (m t) -> p m j t", t=PACK)
+                if (a, s) == w_order[-1] and u == W_SPLIT - 1:
                     nc.vector.tensor_copy(dst, src)
                 else:
                     nc.scalar.activation(dst, src, ACT.Copy)
@@ -161,83 +171,60 @@ def tile_list_msg_tanh_res_biasP_kernel(
         nc.sync.dma_start(wgo_sb[:], wgo)
 
         def first_pass(out, h, lo, width, t, a, s, parted, start, stop):
-            wc = slice(t * P, (t + 1) * P)
+            w_cols = slice(t * P, (t + 1) * P)
             at = s * HALF + lo
             nc.tensor.matmul_mx(
                 out,
-                lhsT=w_codes[a, s][:, wc].bitcast(FP8X4),
-                lhsT_scale=w_scales[a, s][:, wc],
+                lhsT=w_codes[a, s][:, w_cols].bitcast(FP8X4),
+                lhsT_scale=w_scales[a, s][:, w_cols],
                 rhs=parted[s][:, a, 2 * lo : 2 * (lo + width)].bitcast(FP4X4),
-                rhs_scale=moved[:, h, a, at : at + width],
+                rhs_scale=edge_scales[:, h, a, at : at + width],
                 start=start,
                 stop=stop,
             )
 
-        def quantise_hidden(name, woven, width):
-            codes = sb([P, width], U32, "h_codes" + name)
-            scales = sb([P, width], U8, "h_scales" + name)
-            nc.vector.quantize_mx(codes[:].bitcast(FP8X4), scales[:], woven[:].rearrange("p n t -> p (n t)"))
-            return codes[:], scales[:]
-
-        def weave_views(woven, hidden):
-            return (
-                woven[:].rearrange("p (c i) t -> p c t i", i=4),
-                hidden[:].rearrange("p t (c i) -> p c t i", i=4),
-            )
-
-        accs0 = [bank(e, "a0%d" % e) for e in range(HALF // P)]
+        sums0 = [bank(e, "sums0%d" % e) for e in range(HALF // P)]
         for a, s in w_order:
             for e in range(HALF // P):
                 for t in range(PACK):
                     first_pass(
-                        accs0[e][:, t * P : (t + 1) * P], 0, e * P, P, t, a, s, parted0,
+                        sums0[e][:, t * P : (t + 1) * P], 0, e * P, P, t, a, s, parted0,
                         (a, s) == w_order[0] and t == 0, (a, s) == w_order[-1] and t == PACK - 1,
                     )
 
         parted1 = [part(1, s, look_up(1, s, ("grouped01", "grouped11")[s])) for s in range(2)]
 
-        h_codes = sb([P, HALF], U32, "h_codes0")
-        h_scales = sb([P, HALF], U8, "h_scales0")
+        h0_codes = sb([P, HALF], U32, "h0_codes")
+        h0_scales = sb([P, HALF], U8, "h0_scales")
 
         def squash(e):
-            th = sb([P, P, PACK], F32, "th%d" % e)
-            nc.scalar.activation(th[:], accs0[e][:].rearrange("p (t n) -> p n t", t=PACK), ACT.Tanh)
+            th = sb([P, P, PACK], F32, "th0%d" % e)
+            nc.scalar.activation(th[:], sums0[e][:].rearrange("p (t n) -> p n t", t=PACK), ACT.Tanh)
             return th
 
-        def smooth(u):
-            woven = sb([P, QUARTER, PACK], BF16, "woven%d" % u)
-            for e in range(2):
-                nc.vector.tensor_tensor(
-                    woven[:, e * P : (e + 1) * P, :],
-                    squash(2 * u + e)[:],
-                    sm_sb.unsqueeze(1).to_broadcast([P, P, PACK]),
-                    MULT,
-                )
+        def hidden_quarter(u):
+            woven = sb([P, QUARTER, PACK], BF16, "woven0%d" % u)
+            for e in range(QUARTER // P):
+                th = squash(u * (QUARTER // P) + e)
+                nc.vector.tensor_tensor(woven[:, e * P : (e + 1) * P, :], th[:], sm_rows[:], MULT)
             cut = slice(u * QUARTER, (u + 1) * QUARTER)
             nc.vector.quantize_mx(
-                h_codes[:, cut].bitcast(FP8X4), h_scales[:, cut], woven[:].rearrange("p n t -> p (n t)")
+                h0_codes[:, cut].bitcast(FP8X4), h0_scales[:, cut], woven[:].rearrange("p n t -> p (n t)")
             )
 
-        smooth(0)
+        hidden_quarter(0)
 
         wd4 = sb([P, PACK, 2 * P], U8, "wd4")
         wd8 = sb([P, PACK, P], I32, "wd8")
         wd_scales = sb([P, 2, PACK, P], U8, "wd_scales", tag="grouped10")
-        nc.vector.tensor_copy(
-            wd4[:].bitcast(U16).rearrange("p t m -> p m t"),
-            wd4_raw.bitcast(U16).rearrange("p (m t) -> p m t", t=PACK),
-        )
-        nc.vector.tensor_copy(wd8[:].rearrange("p t m -> p m t"), wd8_raw.rearrange("p (m t) -> p m t", t=PACK))
-        nc.vector.tensor_copy(
-            wd_scales[:].rearrange("p w t m -> p w m t"),
-            wd_scales_raw[:].rearrange("p (w m t) -> p w m t", w=2, t=PACK),
-        )
+        nc.vector.tensor_copy(wd4[:].bitcast(U16), wd4_raw.bitcast(U16).rearrange("p (m t) -> p t m", t=PACK))
+        nc.vector.tensor_copy(wd8[:], wd8_raw.rearrange("p (m t) -> p t m", t=PACK))
+        nc.vector.tensor_copy(wd_scales[:], wd_scales_raw[:].rearrange("p (w m t) -> p w t m", w=2, t=PACK))
 
-        smooth(1)
-        late_page("woven1")
+        hidden_quarter(1)
+        late_page("woven01")
 
-        def second_layer(name, hidden_mx, width, t):
-            codes, scales = hidden_mx
+        def second_layer(name, codes, scales, width, t):
             acc = bank(PACK + t, "y%s%d" % (name, t))
             nc.tensor.matmul_mx(
                 acc[:, 0:width], lhsT=wd8[:, t, :].bitcast(FP8X4), lhsT_scale=wd_scales[:, 1, t, :],
@@ -256,40 +243,43 @@ def tile_list_msg_tanh_res_biasP_kernel(
             message = sb([P, width], F32, "message%s%d" % (name, t), tag=tag)
             nc.scalar.activation(message[:], acc[:, 0:width], ACT.Identity, bias=b_sb[:, t : t + 1])
             nc.vector.tensor_tensor(
-                pages[t][:].indirect(dst_list[:, lo // 16 : (lo + width) // 16]),
-                message[:],
-                wgo_sb[:, lo : lo + width],
-                MULT,
+                pages[t][:].indirect(entries(1, lo, width)), message[:], wgo_sb[:, lo : lo + width], MULT
             )
 
         for u in range(2):
             cut = slice(u * QUARTER, (u + 1) * QUARTER)
-            name = "q%d" % u
-            put(name, cut.start, QUARTER, 0, second_layer(name, (h_codes[:, cut], h_scales[:, cut]), QUARTER, 0))
+            name = "quarter%d" % u
+            put(name, cut.start, QUARTER, 0, second_layer(name, h0_codes[:, cut], h0_scales[:, cut], QUARTER, 0))
             late_page("message%s0" % name)
-        ys_a = {t: second_layer("a", (h_codes[:], h_scales[:]), HALF, t) for t in range(1, PACK)}
+        ys0 = {t: second_layer("half0", h0_codes[:], h0_scales[:], HALF, t) for t in range(1, PACK)}
         for t in range(1, PACK - 1):
-            put("a", 0, HALF, t, ys_a[t])
+            put("half0", 0, HALF, t, ys0[t])
 
-        hidden_c = sb([P, PACK, HALF], BF16, "hidden_c")
+        hidden1 = sb([P, PACK, HALF], BF16, "hidden1")
         for t in range(PACK):
-            acc = bank(t, "a1%d" % t)
+            acc = bank(t, "sums1%d" % t)
             for a, s in w_order:
                 first_pass(acc[:], 1, 0, HALF, t, a, s, parted1, (a, s) == w_order[0], (a, s) == w_order[-1])
-            th = sb([P, HALF], F32, "th_c%d" % t, tag="th_c%d" % (t % 2))
+            th = sb([P, HALF], F32, "th1%d" % t, tag="th1%d" % (t % 2))
             nc.scalar.activation(th[:], acc[:], ACT.Tanh)
-            nc.scalar.activation(hidden_c[:, t, :], th[:], ACT.Copy, scale=sm_sb[:, t : t + 1])
-        woven_c = sb([P, HALF, PACK], BF16, "woven_c")
-        nc.scalar.copy(*weave_views(woven_c, hidden_c))
-        h_c = quantise_hidden("c", woven_c, HALF)
-        put("a", 0, HALF, PACK - 1, ys_a[PACK - 1], tag="hidden_c")
+            nc.scalar.activation(hidden1[:, t, :], th[:], ACT.Copy, scale=sm_sb[:, t : t + 1])
+        woven1 = sb([P, HALF, PACK], BF16, "woven1")
+        nc.scalar.copy(
+            woven1[:].rearrange("p (c i) t -> p c t i", i=4), hidden1[:].rearrange("p t (c i) -> p c t i", i=4)
+        )
+        h1_codes = sb([P, HALF], U32, "h1_codes")
+        h1_scales = sb([P, HALF], U8, "h1_scales")
+        nc.vector.quantize_mx(h1_codes[:].bitcast(FP8X4), h1_scales[:], woven1[:].rearrange("p n t -> p (n t)"))
+
+        put("half0", 0, HALF, PACK - 1, ys0[PACK - 1], tag="hidden1")
 
         out_rows = out_0.rearrange("(p t) c -> t p c", t=PACK)
         starts = [sum(OUT_WIDTHS[:c]) for c in range(len(OUT_WIDTHS))]
         pairs = [sb([P, 2, width, 2], BF16, "pairs%d" % c) for c, width in enumerate(OUT_WIDTHS)]
-        ys_c = [second_layer("c", h_c, HALF, t) for t in range(PACK)]
+        ys1 = [second_layer("half1", h1_codes[:], h1_scales[:], HALF, t) for t in range(PACK)]
         for t in range(PACK):
-            put("c", HALF, HALF, t, ys_c[t])
+            put("half1", HALF, HALF, t, ys1[t])
+
         out_words = out_1[0].rearrange("p t c -> p (t c)").bitcast(I32)
         out_scales = sb([P, OUT_GROUP], U8, "out_scales")
         out_codes = [sb([P, OUT_GROUP], U32, "out_codes%d" % g) for g in range(T // OUT_GROUP)]
@@ -300,25 +290,25 @@ def tile_list_msg_tanh_res_biasP_kernel(
 
         def weave_out(c):
             on_scalar = c >= len(OUT_WIDTHS) - SCALAR_WEAVES
-            woven_out = sb([P, OUT_WIDTHS[c], PACK], BF16, "woven_out%d" % c)
+            woven = sb([P, OUT_WIDTHS[c], PACK], BF16, "woven_out%d" % c)
             word = U32 if on_scalar else I32
-            dst = woven_out[:].rearrange("p n t -> p (n t)").bitcast(word).rearrange("p (n u) -> p n u", u=2)
+            dst = woven[:].rearrange("p n t -> p (n t)").bitcast(word).rearrange("p (n u) -> p n u", u=2)
             src = pairs[c][:].rearrange("p u n e -> p u (n e)").bitcast(word).rearrange("p u n -> p n u")
             if on_scalar:
                 nc.scalar.copy(dst, src)
             else:
                 nc.vector.tensor_copy(dst, src)
-            return woven_out
+            return woven
 
-        def quantise_out(c, woven_out):
+        def quantise_out(c, woven):
             g, lo = divmod(starts[c], OUT_GROUP)
             cut = slice(lo, lo + OUT_WIDTHS[c])
             nc.vector.quantize_mx(
-                out_codes[g][:, cut].bitcast(FP8X4),
-                out_scales[4 * g : P, cut],
-                woven_out[:].rearrange("p n t -> p (n t)"),
+                out_codes[g][:, cut].bitcast(FP8X4), out_scales[4 * g : P, cut], woven[:].rearrange("p n t -> p (n t)")
             )
-            if cut.stop == OUT_GROUP:
+            if g == T // OUT_GROUP - 1:
+                nc.sync.dma_start(out_words[:, starts[c] : starts[c] + OUT_WIDTHS[c]], out_codes[g][:, cut].bitcast(I32))
+            elif cut.stop == OUT_GROUP:
                 nc.sync.dma_start(out_words[:, g * OUT_GROUP : (g + 1) * OUT_GROUP], out_codes[g][:].bitcast(I32))
 
         woven_outs = [weave_out(0)]

@@ -60,20 +60,24 @@ def tile_list_msg_tanh_res_biasP_kernel(
         )
         nc.sync.dma_start(src_list[:], offs)
         nc.sync.dma_start(dst_list[:], offs2)
-        nc.gpsimd.memset(table_scales[0:LAST_QUAD, :].bitcast(I32), 0)
+        nc.sync.dma_start(table[:], tab_words[0].rearrange("p t c -> p (t c)").bitcast(I32))
+        w_order = [(a, s) for a in range(PASSES) for s in range(2)]
+        raw = {}
+        for a, s in w_order:
+            rows = (ws, wt)[s][a * K_PASS : (a + 1) * K_PASS, :].rearrange("(p j) r -> p j r", j=PACK)
+            raw[a, s] = sb([P, PACK, R], F32, "raw%d%d" % (a, s))
+            nc.sync.dma_start(raw[a, s][:], rows)
 
-        wd_scales_raw = sb([P, 2 * N], U8, "wd_scales_raw")
-        nc.gpsimd.memset(wd_scales_raw[:].bitcast(I32), 0)
-        for w, scales in enumerate((wd4_scales, wd8_scales)):
-            for q in range(QUADS):
-                nc.gpsimd.dma_start(
-                    wd_scales_raw[32 * q : 32 * q + 4, w * N : (w + 1) * N].bitcast(I32),
-                    scales[0, 4 * q : 4 * q + 4, :].bitcast(I32),
-                )
+        sm_raw = sb([P, PACK], F32, "sm_raw")
+        b_sb = sb([P, PACK], F32, "b_sb")
+        nc.scalar.dma_start(sm_raw[:], sm.rearrange("(p t) -> p t", t=PACK))
+        nc.scalar.dma_start(b_sb[:], b.rearrange("(p t) -> p t", t=PACK))
 
+        wd_scales_raw = sb([P, N], U8, "wd_scales_raw")
+        nc.vector.memset(wd_scales_raw[:].bitcast(I32), 0)
+        nc.vector.memset(table_scales[0:LAST_QUAD, :].bitcast(I32), 0)
         edge_scales = sb([P, 2, PASSES, J], U8, "edge_scales")
         nc.vector.memset(edge_scales[:].rearrange("p h a n -> p (h a n)").bitcast(I32), 0)
-
         pages = [sb([P, T], F32, "page0")]
         nc.vector.memset(pages[0][:], 0.0)
 
@@ -82,26 +86,18 @@ def tile_list_msg_tanh_res_biasP_kernel(
             nc.gpsimd.memset(page[:], 0.0)
             pages.append(page)
 
-        w_order = [(a, s) for a in range(PASSES) for s in range(2)]
-        raw = {}
-
-        def load_raw(a, s, tag=None):
-            rows = (ws, wt)[s][a * K_PASS : (a + 1) * K_PASS, :].rearrange("(p j) r -> p j r", j=PACK)
-            raw[a, s] = sb([P, PACK, R], F32, "raw%d%d" % (a, s), tag=tag)
-            nc.sync.dma_start(raw[a, s][:], rows)
-
-        load_raw(0, 0)
-        nc.sync.dma_start(table[:], tab_words[0].rearrange("p t c -> p (t c)").bitcast(I32))
-        load_raw(0, 1)
-
-        vectors = sb([P, 16], F32, "vectors")
-        sm_sb = vectors[:, 0:PACK]
-        b_sb = vectors[:, 8 : 8 + PACK]
-        nc.scalar.dma_start(sm_sb, sm.rearrange("(p t) -> p t", t=PACK))
-        nc.scalar.dma_start(b_sb, b.rearrange("(p t) -> p t", t=PACK))
+        def load_wd_scales(w):
+            for q in range(QUADS):
+                first = 32 * q + 4 * w
+                nc.gpsimd.dma_start(
+                    wd_scales_raw[first : first + 4, :].bitcast(I32),
+                    (wd4_scales, wd8_scales)[w][0, 4 * q : 4 * q + 4, :].bitcast(I32),
+                )
 
         sm_rows = sb([P, P, PACK], F32, "sm_rows")
-        nc.scalar.activation(sm_rows[:], sm_sb.unsqueeze(1).to_broadcast([P, P, PACK]), ACT.Copy)
+        nc.scalar.activation(sm_rows[:], sm_raw[:].unsqueeze(1).to_broadcast([P, P, PACK]), ACT.Copy)
+        late_page("sm_raw")
+        load_wd_scales(0)
 
         picked_scales = [sb([P, 2 * HALF], U8, "picked_scales%d" % h) for h in range(2)]
         for h in range(2):
@@ -110,25 +106,22 @@ def tile_list_msg_tanh_res_biasP_kernel(
                     picked_scales[h][:, s * HALF : (s + 1) * HALF],
                     table_scales[:].indirect(entries(s, h * HALF, HALF)),
                 )
-
-        def move_scales(h):
             for q in range(QUADS):
                 first = LAST_QUAD + 8 * q
-                nc.sync.dma_start(
+                (nc.scalar, nc.sync)[h].dma_start(
                     edge_scales[32 * q : 32 * q + 4, h, :, :].bitcast(I32),
                     picked_scales[h][first : first + 8, :].bitcast(I32),
                 )
-
-        move_scales(0)
-        load_raw(1, 0, "table_scales")
+        late_page("table_scales")
+        load_wd_scales(1)
 
         def look_up(h, s, tag=None):
             picked = sb([P, HALF], U32, "picked%d%d" % (h, s), tag=tag)
             nc.vector.tensor_copy(picked[:], table[:].bitcast(U32).indirect(entries(s, h * HALF, HALF)))
             return picked
 
-        def part(h, s, picked):
-            parted = sb([P, PASSES, 2 * HALF], U8, "parted%d%d" % (h, s))
+        def part(h, s, picked, tag=None):
+            parted = sb([P, PASSES, 2 * HALF], U8, "parted%d%d" % (h, s), tag=tag)
             nc.vector.tensor_copy(
                 parted[:].bitcast(U16), picked[:].bitcast(U16).rearrange("p (n d) -> p d n", d=PASSES)
             )
@@ -154,20 +147,20 @@ def tile_list_msg_tanh_res_biasP_kernel(
                 w_codes[a, s][:].bitcast(FP8X4), w_scales[a, s][:], grouped[:].rearrange("p t m j -> p (t m j)")
             )
 
-        quantise_weight(0, 0)
-        load_raw(1, 1, "raw00")
-        move_scales(1)
         picked0 = [look_up(0, s) for s in range(2)]
         parted0 = [part(0, s, picked0[s]) for s in range(2)]
-        for a, s in w_order[1:]:
+        picked1 = []
+        for i, (a, s) in enumerate(w_order):
             quantise_weight(a, s)
+            if i < 2:
+                picked1.append(look_up(1, i, "grouped%d%d" % (a, s)))
 
-        wd_raw = sb([P, N + N // 2], I32, "wd_raw", tag="grouped00")
+        wd_raw = sb([P, N + N // 2], I32, "wd_raw", tag="picked_scales0")
         wd8_raw = wd_raw[:, 0:N]
         wd4_raw = wd_raw[:, N : N + N // 2]
+        wgo_sb = sb([P, J], F32, "wgo_sb", tag="picked_scales1")
         nc.sync.dma_start(wd4_raw, wd4_words[0].bitcast(I32))
         nc.sync.dma_start(wd8_raw, wd8_words[0].rearrange("p n c -> p (n c)").bitcast(I32))
-        wgo_sb = sb([P, J], F32, "wgo_sb", tag="raw01")
         nc.sync.dma_start(wgo_sb[:], wgo)
 
         def first_pass(out, h, lo, width, t, a, s, parted, start, stop):
@@ -192,50 +185,48 @@ def tile_list_msg_tanh_res_biasP_kernel(
                         (a, s) == w_order[0] and t == 0, (a, s) == w_order[-1] and t == PACK - 1,
                     )
 
-        parted1 = [part(1, s, look_up(1, s, ("grouped01", "grouped11")[s])) for s in range(2)]
+        parted1 = [part(1, 0, picked1[0], "grouped11")]
 
-        h0_codes = sb([P, HALF], U32, "h0_codes")
-        h0_scales = sb([P, HALF], U8, "h0_scales")
+        wd4 = sb([P, PACK, 2 * P], U8, "wd4", tag="raw11")
+        wd8 = sb([P, PACK, P], I32, "wd8", tag="raw10")
+        wd_scales = sb([P, PACK, P], U8, "wd_scales", tag="grouped10")
+        nc.vector.tensor_copy(wd4[:].bitcast(U16), wd4_raw.bitcast(U16).rearrange("p (m t) -> p t m", t=PACK))
+        nc.vector.tensor_copy(wd8[:].rearrange("p t m -> p m t"), wd8_raw.rearrange("p (m t) -> p m t", t=PACK))
+        nc.vector.tensor_copy(wd_scales[:], wd_scales_raw[:].rearrange("p (m t) -> p t m", t=PACK))
 
-        def squash(e):
-            th = sb([P, P, PACK], F32, "th0%d" % e)
-            nc.scalar.activation(th[:], sums0[e][:].rearrange("p (t n) -> p n t", t=PACK), ACT.Tanh)
-            return th
+        h_codes = [sb([P, HALF], U32, "h_codes%d" % h) for h in range(2)]
+        h_scales = [sb([P, HALF], U8, "h_scales%d" % h) for h in range(2)]
 
-        def hidden_quarter(u):
-            woven = sb([P, QUARTER, PACK], BF16, "woven0%d" % u)
-            for e in range(QUARTER // P):
-                th = squash(u * (QUARTER // P) + e)
-                nc.vector.tensor_tensor(woven[:, e * P : (e + 1) * P, :], th[:], sm_rows[:], MULT)
+        def quantise_hidden(c, woven):
+            h, u = divmod(c, 2)
             cut = slice(u * QUARTER, (u + 1) * QUARTER)
             nc.vector.quantize_mx(
-                h0_codes[:, cut].bitcast(FP8X4), h0_scales[:, cut], woven[:].rearrange("p n t -> p (n t)")
+                h_codes[h][:, cut].bitcast(FP8X4), h_scales[h][:, cut], woven[:].rearrange("p n t -> p (n t)")
             )
 
-        hidden_quarter(0)
+        woven0 = sb([P, QUARTER, PACK], BF16, "woven0")
+        for e in range(QUARTER // P):
+            th = sb([P, P, PACK], F32, "th0%d" % e)
+            nc.scalar.activation(th[:], sums0[e][:].rearrange("p (t n) -> p n t", t=PACK), ACT.Tanh)
+            nc.vector.tensor_tensor(woven0[:, e * P : (e + 1) * P, :], th[:], sm_rows[:], MULT)
+        quantise_hidden(0, woven0)
+        parted1.append(part(1, 1, picked1[1], "woven0"))
+        late_page("grouped01")
 
-        wd4 = sb([P, PACK, 2 * P], U8, "wd4")
-        wd8 = sb([P, PACK, P], I32, "wd8")
-        wd_scales = sb([P, 2, PACK, P], U8, "wd_scales", tag="grouped10")
-        nc.vector.tensor_copy(wd4[:].bitcast(U16), wd4_raw.bitcast(U16).rearrange("p (m t) -> p t m", t=PACK))
-        nc.vector.tensor_copy(wd8[:], wd8_raw.rearrange("p (m t) -> p t m", t=PACK))
-        nc.vector.tensor_copy(wd_scales[:], wd_scales_raw[:].rearrange("p (w m t) -> p w t m", w=2, t=PACK))
-
-        hidden_quarter(1)
-        late_page("woven01")
-
-        def second_layer(name, codes, scales, width, t):
-            acc = bank(PACK + t, "y%s%d" % (name, t))
+        def second_layer(name, i, h, lo, width, t):
+            acc = bank(i, "y%s%d" % (name, t))
+            codes = h_codes[h][:, lo : lo + width]
+            scales = h_scales[h][:, lo : lo + width]
             nc.tensor.matmul_mx(
-                acc[:, 0:width], lhsT=wd8[:, t, :].bitcast(FP8X4), lhsT_scale=wd_scales[:, 1, t, :],
+                acc[:, 0:width], lhsT=wd8[:, t, :].bitcast(FP8X4), lhsT_scale=wd_scales[4:P, t, :],
                 rhs=codes.bitcast(FP8X4), rhs_scale=scales, start=True, stop=False,
             )
             step = HALF if width == HALF else P
-            for lo in range(0, width, step):
+            for at in range(0, width, step):
                 nc.tensor.matmul_mx(
-                    acc[:, lo : lo + step], lhsT=wd4[:, t, :].bitcast(FP4X4), lhsT_scale=wd_scales[:, 0, t, :],
-                    rhs=codes[:, lo : lo + step].bitcast(FP8X4), rhs_scale=scales[:, lo : lo + step],
-                    start=False, stop=lo + step == width,
+                    acc[:, at : at + step], lhsT=wd4[:, t, :].bitcast(FP4X4), lhsT_scale=wd_scales[:, t, :],
+                    rhs=codes[:, at : at + step].bitcast(FP8X4), rhs_scale=scales[:, at : at + step],
+                    start=False, stop=at + step == width,
                 )
             return acc
 
@@ -246,39 +237,65 @@ def tile_list_msg_tanh_res_biasP_kernel(
                 pages[t][:].indirect(entries(1, lo, width)), message[:], wgo_sb[:, lo : lo + width], MULT
             )
 
-        for u in range(2):
-            cut = slice(u * QUARTER, (u + 1) * QUARTER)
-            name = "quarter%d" % u
-            put(name, cut.start, QUARTER, 0, second_layer(name, h0_codes[:, cut], h0_scales[:, cut], QUARTER, 0))
-            late_page("message%s0" % name)
-        ys0 = {t: second_layer("half0", h0_codes[:], h0_scales[:], HALF, t) for t in range(1, PACK)}
-        for t in range(1, PACK - 1):
-            put("half0", 0, HALF, t, ys0[t])
+        def scale(hidden, t, th):
+            nc.scalar.activation(hidden[:, t, :], th, ACT.Copy, scale=sm_rows[:, 0, t : t + 1])
 
-        hidden1 = sb([P, PACK, HALF], BF16, "hidden1")
-        for t in range(PACK):
-            acc = bank(t, "sums1%d" % t)
-            for a, s in w_order:
-                first_pass(acc[:], 1, 0, HALF, t, a, s, parted1, (a, s) == w_order[0], (a, s) == w_order[-1])
-            th = sb([P, HALF], F32, "th1%d" % t, tag="th1%d" % (t % 2))
+        def weave_hidden(c, hidden):
+            woven = sb([P, QUARTER, PACK], BF16, "woven%d" % c)
+            nc.scalar.copy(
+                woven[:].rearrange("p (c i) t -> p c t i", i=4), hidden[:].rearrange("p t (c i) -> p c t i", i=4)
+            )
+            quantise_hidden(c, woven)
+
+        hidden = {c: sb([P, PACK, QUARTER], BF16, "hidden%d" % c) for c in (1, 2, 3)}
+
+        th1 = sb([P, PACK, QUARTER], F32, "th1")
+        for e in range(QUARTER // P):
+            nc.scalar.activation(
+                th1[:, :, e * P : (e + 1) * P], sums0[2 + e][:].rearrange("p (t n) -> p t n", t=PACK), ACT.Tanh
+            )
+        ys = [second_layer("q0", t, 0, 0, QUARTER, t) for t in range(PACK)]
+        for t in range(2):
+            scale(hidden[1], t, th1[:, t, :])
+        for t in range(2):
+            put("q0", 0, QUARTER, t, ys[t])
+        for t in range(2, PACK):
+            scale(hidden[1], t, th1[:, t, :])
+        weave_hidden(1, hidden[1])
+        put("q0", 0, QUARTER, 2, ys[2], tag="hidden1")
+        put("q0", 0, QUARTER, 3, ys[3])
+
+        def first_layer_late(t):
+            acc = bank(PACK + t, "sums1%d" % t)
+            order = w_order[::-1]
+            for a, s in order:
+                first_pass(acc[:], 1, 0, HALF, t, a, s, parted1, (a, s) == order[0], (a, s) == order[-1])
+            th = sb([P, HALF], F32, "th2%d" % t, tag="th2%d" % (t % 2))
             nc.scalar.activation(th[:], acc[:], ACT.Tanh)
-            nc.scalar.activation(hidden1[:, t, :], th[:], ACT.Copy, scale=sm_sb[:, t : t + 1])
-        woven1 = sb([P, HALF, PACK], BF16, "woven1")
-        nc.scalar.copy(
-            woven1[:].rearrange("p (c i) t -> p c t i", i=4), hidden1[:].rearrange("p t (c i) -> p c t i", i=4)
-        )
-        h1_codes = sb([P, HALF], U32, "h1_codes")
-        h1_scales = sb([P, HALF], U8, "h1_scales")
-        nc.vector.quantize_mx(h1_codes[:].bitcast(FP8X4), h1_scales[:], woven1[:].rearrange("p n t -> p (n t)"))
+            for u in range(2):
+                scale(hidden[2 + u], t, th[:, u * QUARTER : (u + 1) * QUARTER])
 
-        put("half0", 0, HALF, PACK - 1, ys0[PACK - 1], tag="hidden1")
+        for t in range(2):
+            first_layer_late(t)
+        ys = [second_layer("q1", t, 0, QUARTER, QUARTER, t) for t in range(PACK)]
+        for t in range(2):
+            put("q1", QUARTER, QUARTER, t, ys[t])
+        first_layer_late(2)
+        put("q1", QUARTER, QUARTER, 2, ys[2])
+        first_layer_late(3)
+        weave_hidden(2, hidden[2])
+        put("q1", QUARTER, QUARTER, 3, ys[3], tag="hidden2")
+        weave_hidden(3, hidden[3])
+
+        for u in range(2):
+            name = "q%d" % (2 + u)
+            put(name, HALF + u * QUARTER, QUARTER, 0, second_layer(name, PACK * u, 1, u * QUARTER, QUARTER, 0))
+        for t in range(1, PACK):
+            put("half1", HALF, HALF, t, second_layer("half1", t, 1, 0, HALF, t))
 
         out_rows = out_0.rearrange("(p t) c -> t p c", t=PACK)
         starts = [sum(OUT_WIDTHS[:c]) for c in range(len(OUT_WIDTHS))]
         pairs = [sb([P, 2, width, 2], BF16, "pairs%d" % c) for c, width in enumerate(OUT_WIDTHS)]
-        ys1 = [second_layer("half1", h1_codes[:], h1_scales[:], HALF, t) for t in range(PACK)]
-        for t in range(PACK):
-            put("half1", HALF, HALF, t, ys1[t])
 
         out_words = out_1[0].rearrange("p t c -> p (t c)").bitcast(I32)
         out_scales = sb([P, OUT_GROUP], U8, "out_scales")

@@ -78,8 +78,9 @@ def tile_list_msg_tanh_res_biasP_kernel(
         nc.vector.memset(table_scales[0:LAST_QUAD, :].bitcast(I32), 0)
         edge_scales = sb([P, 2, PASSES, J], U8, "edge_scales")
         nc.vector.memset(edge_scales[:].rearrange("p h a n -> p (h a n)").bitcast(I32), 0)
-        pages = [sb([P, T], F32, "page0")]
-        nc.vector.memset(pages[0][:], 0.0)
+        pages = [sb([P, T], F32, "page%d" % t) for t in range(2)]
+        for page in pages:
+            nc.vector.memset(page[:], 0.0)
 
         def late_page(tag):
             page = sb([P, T], F32, "page%d" % len(pages), tag=tag)
@@ -96,24 +97,22 @@ def tile_list_msg_tanh_res_biasP_kernel(
 
         sm_rows = sb([P, P, PACK], F32, "sm_rows")
         nc.scalar.activation(sm_rows[:], sm_raw[:].unsqueeze(1).to_broadcast([P, P, PACK]), ACT.Copy)
-        late_page("sm_raw")
-        load_wd_scales(0)
+        for w in range(2):
+            load_wd_scales(w)
 
-        picked_scales = [sb([P, 2 * HALF], U8, "picked_scales%d" % h) for h in range(2)]
-        for h in range(2):
+        def look_up_scales(h, tag=None):
+            picked = sb([P, 2 * HALF], U8, "picked_scales%d" % h, tag=tag)
             for s in range(2):
                 nc.vector.tensor_copy(
-                    picked_scales[h][:, s * HALF : (s + 1) * HALF],
-                    table_scales[:].indirect(entries(s, h * HALF, HALF)),
+                    picked[:, s * HALF : (s + 1) * HALF], table_scales[:].indirect(entries(s, h * HALF, HALF))
                 )
             for q in range(QUADS):
                 first = LAST_QUAD + 8 * q
                 (nc.scalar, nc.sync)[h].dma_start(
-                    edge_scales[32 * q : 32 * q + 4, h, :, :].bitcast(I32),
-                    picked_scales[h][first : first + 8, :].bitcast(I32),
+                    edge_scales[32 * q : 32 * q + 4, h, :, :].bitcast(I32), picked[first : first + 8, :].bitcast(I32)
                 )
-        late_page("table_scales")
-        load_wd_scales(1)
+
+        look_up_scales(0)
 
         def look_up(h, s, tag=None):
             picked = sb([P, HALF], U32, "picked%d%d" % (h, s), tag=tag)
@@ -149,19 +148,19 @@ def tile_list_msg_tanh_res_biasP_kernel(
 
         picked0 = [look_up(0, s) for s in range(2)]
         parted0 = [part(0, s, picked0[s]) for s in range(2)]
+        wd_raw = sb([P, N + N // 2], I32, "wd_raw", tag="picked00")
+        wd8_raw = wd_raw[:, 0:N]
+        wd4_raw = wd_raw[:, N : N + N // 2]
+        nc.sync.dma_start(wd4_raw, wd4_words[0].bitcast(I32))
+        nc.sync.dma_start(wd8_raw, wd8_words[0].rearrange("p n c -> p (n c)").bitcast(I32))
+        look_up_scales(1, "picked01")
+        wgo_sb = sb([P, J], F32, "wgo_sb", tag="picked_scales0")
+        nc.sync.dma_start(wgo_sb[:], wgo)
         picked1 = []
         for i, (a, s) in enumerate(w_order):
             quantise_weight(a, s)
             if i < 2:
                 picked1.append(look_up(1, i, "grouped%d%d" % (a, s)))
-
-        wd_raw = sb([P, N + N // 2], I32, "wd_raw", tag="picked_scales0")
-        wd8_raw = wd_raw[:, 0:N]
-        wd4_raw = wd_raw[:, N : N + N // 2]
-        wgo_sb = sb([P, J], F32, "wgo_sb", tag="picked_scales1")
-        nc.sync.dma_start(wd4_raw, wd4_words[0].bitcast(I32))
-        nc.sync.dma_start(wd8_raw, wd8_words[0].rearrange("p n c -> p (n c)").bitcast(I32))
-        nc.sync.dma_start(wgo_sb[:], wgo)
 
         def first_pass(out, h, lo, width, t, a, s, parted, start, stop):
             w_cols = slice(t * P, (t + 1) * P)
@@ -259,6 +258,7 @@ def tile_list_msg_tanh_res_biasP_kernel(
             scale(hidden[1], t, th1[:, t, :])
         for t in range(2):
             put("q0", 0, QUARTER, t, ys[t])
+        late_page("messageq00")
         for t in range(2, PACK):
             scale(hidden[1], t, th1[:, t, :])
         weave_hidden(1, hidden[1])

@@ -55,7 +55,7 @@ def tile_list_msg_tanh_res_biasP_kernel(
         def entries(s, lo, width):
             return lists[s][:, lo // LIST_ROWS : (lo + width) // LIST_ROWS]
 
-        nc.sync.dma_start(
+        nc.scalar.dma_start(
             table_scales[LAST_QUAD:P, :].bitcast(I32), tab_scales.bitcast(I32).rearrange("a r n -> r a n")
         )
         nc.sync.dma_start(src_list[:], offs)
@@ -78,9 +78,8 @@ def tile_list_msg_tanh_res_biasP_kernel(
         nc.vector.memset(table_scales[0:LAST_QUAD, :].bitcast(I32), 0)
         edge_scales = sb([P, 2, PASSES, J], U8, "edge_scales")
         nc.vector.memset(edge_scales[:].rearrange("p h a n -> p (h a n)").bitcast(I32), 0)
-        pages = [sb([P, T], F32, "page%d" % t) for t in range(2)]
-        for page in pages:
-            nc.vector.memset(page[:], 0.0)
+        pages = [sb([P, T], F32, "page0")]
+        nc.vector.memset(pages[0][:], 0.0)
 
         def late_page(tag):
             page = sb([P, T], F32, "page%d" % len(pages), tag=tag)
@@ -185,6 +184,7 @@ def tile_list_msg_tanh_res_biasP_kernel(
                     )
 
         parted1 = [part(1, 0, picked1[0], "grouped11")]
+        parted1.append(part(1, 1, picked1[1], "grouped00"))
 
         wd4 = sb([P, PACK, 2 * P], U8, "wd4", tag="raw11")
         wd8 = sb([P, PACK, P], I32, "wd8", tag="raw10")
@@ -196,21 +196,26 @@ def tile_list_msg_tanh_res_biasP_kernel(
         h_codes = [sb([P, HALF], U32, "h_codes%d" % h) for h in range(2)]
         h_scales = [sb([P, HALF], U8, "h_scales%d" % h) for h in range(2)]
 
-        def quantise_hidden(c, woven):
-            h, u = divmod(c, 2)
-            cut = slice(u * QUARTER, (u + 1) * QUARTER)
+        def quantise_hidden(h, lo, woven):
+            cut = slice(lo, lo + woven.shape[1])
             nc.vector.quantize_mx(
                 h_codes[h][:, cut].bitcast(FP8X4), h_scales[h][:, cut], woven[:].rearrange("p n t -> p (n t)")
             )
 
-        woven0 = sb([P, QUARTER, PACK], BF16, "woven0")
-        for e in range(QUARTER // P):
+        woven0 = [sb([P, QUARTER, PACK], BF16, "woven0%d" % u) for u in range(2)]
+
+        def squash(e):
             th = sb([P, P, PACK], F32, "th0%d" % e)
             nc.scalar.activation(th[:], sums0[e][:].rearrange("p (t n) -> p n t", t=PACK), ACT.Tanh)
-            nc.vector.tensor_tensor(woven0[:, e * P : (e + 1) * P, :], th[:], sm_rows[:], MULT)
-        quantise_hidden(0, woven0)
-        parted1.append(part(1, 1, picked1[1], "woven0"))
-        late_page("grouped01")
+            u, at = divmod(e * P, QUARTER)
+            nc.vector.tensor_tensor(woven0[u][:, at : at + P, :], th[:], sm_rows[:], MULT)
+
+        for e in range(3):
+            squash(e)
+        quantise_hidden(0, 0, woven0[0])
+        squash(3)
+        quantise_hidden(0, QUARTER, woven0[1])
+        late_page("woven01")
 
         def second_layer(name, i, h, lo, width, t):
             acc = bank(i, "y%s%d" % (name, t))
@@ -236,62 +241,33 @@ def tile_list_msg_tanh_res_biasP_kernel(
                 pages[t][:].indirect(entries(1, lo, width)), message[:], wgo_sb[:, lo : lo + width], MULT
             )
 
-        def scale(hidden, t, th):
-            nc.scalar.activation(hidden[:, t, :], th, ACT.Copy, scale=sm_rows[:, 0, t : t + 1])
+        for u in range(2):
+            name = "quarter%d" % u
+            put(name, u * QUARTER, QUARTER, 0, second_layer(name, 0, 0, u * QUARTER, QUARTER, 0))
+            late_page("message%s0" % name)
+        ys0 = {t: second_layer("half0", t, 0, 0, HALF, t) for t in range(1, PACK)}
+        for t in range(1, PACK - 1):
+            put("half0", 0, HALF, t, ys0[t])
 
-        def weave_hidden(c, hidden):
-            woven = sb([P, QUARTER, PACK], BF16, "woven%d" % c)
-            nc.scalar.copy(
-                woven[:].rearrange("p (c i) t -> p c t i", i=4), hidden[:].rearrange("p t (c i) -> p c t i", i=4)
-            )
-            quantise_hidden(c, woven)
-
-        hidden = {c: sb([P, PACK, QUARTER], BF16, "hidden%d" % c) for c in (1, 2, 3)}
-
-        th1 = sb([P, PACK, QUARTER], F32, "th1")
-        for e in range(QUARTER // P):
-            nc.scalar.activation(
-                th1[:, :, e * P : (e + 1) * P], sums0[2 + e][:].rearrange("p (t n) -> p t n", t=PACK), ACT.Tanh
-            )
-        ys = [second_layer("q0", t, 0, 0, QUARTER, t) for t in range(PACK)]
-        for t in range(2):
-            scale(hidden[1], t, th1[:, t, :])
-        for t in range(2):
-            put("q0", 0, QUARTER, t, ys[t])
-        late_page("messageq00")
-        for t in range(2, PACK):
-            scale(hidden[1], t, th1[:, t, :])
-        weave_hidden(1, hidden[1])
-        put("q0", 0, QUARTER, 2, ys[2], tag="hidden1")
-        put("q0", 0, QUARTER, 3, ys[3])
-
-        def first_layer_late(t):
+        hidden1 = sb([P, PACK, HALF], BF16, "hidden1")
+        order = w_order[::-1]
+        for t in range(PACK):
             acc = bank(PACK + t, "sums1%d" % t)
-            order = w_order[::-1]
             for a, s in order:
                 first_pass(acc[:], 1, 0, HALF, t, a, s, parted1, (a, s) == order[0], (a, s) == order[-1])
-            th = sb([P, HALF], F32, "th2%d" % t, tag="th2%d" % (t % 2))
+            th = sb([P, HALF], F32, "th1%d" % t, tag="th1%d" % (t % 2))
             nc.scalar.activation(th[:], acc[:], ACT.Tanh)
-            for u in range(2):
-                scale(hidden[2 + u], t, th[:, u * QUARTER : (u + 1) * QUARTER])
+            nc.scalar.activation(hidden1[:, t, :], th[:], ACT.Copy, scale=sm_rows[:, 0, t : t + 1])
+        woven1 = sb([P, HALF, PACK], BF16, "woven1")
+        nc.scalar.copy(
+            woven1[:].rearrange("p (c i) t -> p c t i", i=4), hidden1[:].rearrange("p t (c i) -> p c t i", i=4)
+        )
+        quantise_hidden(1, 0, woven1)
 
-        for t in range(2):
-            first_layer_late(t)
-        ys = [second_layer("q1", t, 0, QUARTER, QUARTER, t) for t in range(PACK)]
-        for t in range(2):
-            put("q1", QUARTER, QUARTER, t, ys[t])
-        first_layer_late(2)
-        put("q1", QUARTER, QUARTER, 2, ys[2])
-        first_layer_late(3)
-        weave_hidden(2, hidden[2])
-        put("q1", QUARTER, QUARTER, 3, ys[3], tag="hidden2")
-        weave_hidden(3, hidden[3])
-
-        for u in range(2):
-            name = "q%d" % (2 + u)
-            put(name, HALF + u * QUARTER, QUARTER, 0, second_layer(name, PACK * u, 1, u * QUARTER, QUARTER, 0))
-        for t in range(1, PACK):
-            put("half1", HALF, HALF, t, second_layer("half1", t, 1, 0, HALF, t))
+        put("half0", 0, HALF, PACK - 1, ys0[PACK - 1], tag="hidden1")
+        ys1 = [second_layer("half1", PACK + t, 1, 0, HALF, t) for t in range(PACK)]
+        for t in range(PACK):
+            put("half1", HALF, HALF, t, ys1[t])
 
         out_rows = out_0.rearrange("(p t) c -> t p c", t=PACK)
         starts = [sum(OUT_WIDTHS[:c]) for c in range(len(OUT_WIDTHS))]

@@ -60,13 +60,14 @@ def tile_list_msg_tanh_res_biasP_kernel(
         )
         nc.sync.dma_start(src_list[:], offs)
         nc.sync.dma_start(dst_list[:], offs2)
-        nc.sync.dma_start(table[:], tab_words[0].rearrange("p t c -> p (t c)").bitcast(I32))
         w_order = [(a, s) for a in range(PASSES) for s in range(2)]
         raw = {}
         for a, s in w_order:
             rows = (ws, wt)[s][a * K_PASS : (a + 1) * K_PASS, :].rearrange("(p j) r -> p j r", j=PACK)
             raw[a, s] = sb([P, PACK, R], F32, "raw%d%d" % (a, s))
             nc.sync.dma_start(raw[a, s][:], rows)
+            if (a, s) == w_order[0]:
+                nc.sync.dma_start(table[:], tab_words[0].rearrange("p t c -> p (t c)").bitcast(I32))
 
         sm_raw = sb([P, PACK], F32, "sm_raw")
         b_sb = sb([P, PACK], F32, "b_sb")
@@ -99,19 +100,31 @@ def tile_list_msg_tanh_res_biasP_kernel(
         for w in range(2):
             load_wd_scales(w)
 
-        def look_up_scales(h, tag=None):
-            picked = sb([P, 2 * HALF], U8, "picked_scales%d" % h, tag=tag)
+        picked_scales = [sb([P, 2 * HALF], U8, "picked_scales%d" % h) for h in range(2)]
+        for h in range(2):
             for s in range(2):
                 nc.vector.tensor_copy(
-                    picked[:, s * HALF : (s + 1) * HALF], table_scales[:].indirect(entries(s, h * HALF, HALF))
+                    picked_scales[h][:, s * HALF : (s + 1) * HALF],
+                    table_scales[:].indirect(entries(s, h * HALF, HALF)),
                 )
+
+        def move_scales(h):
+            picked = picked_scales[h]
             for q in range(QUADS):
                 first = LAST_QUAD + 8 * q
                 (nc.scalar, nc.sync)[h].dma_start(
                     edge_scales[32 * q : 32 * q + 4, h, :, :].bitcast(I32), picked[first : first + 8, :].bitcast(I32)
                 )
 
-        look_up_scales(0)
+        move_scales(0)
+        wd_raw = sb([P, N + N // 2], I32, "wd_raw", tag="table_scales")
+        wd8_raw = wd_raw[:, 0:N]
+        wd4_raw = wd_raw[:, N : N + N // 2]
+        nc.sync.dma_start(wd4_raw, wd4_words[0].bitcast(I32))
+        nc.sync.dma_start(wd8_raw, wd8_words[0].rearrange("p n c -> p (n c)").bitcast(I32))
+        move_scales(1)
+        wgo_sb = sb([P, J], F32, "wgo_sb", tag="picked_scales0")
+        nc.sync.dma_start(wgo_sb[:], wgo)
 
         def look_up(h, s, tag=None):
             picked = sb([P, HALF], U32, "picked%d%d" % (h, s), tag=tag)
@@ -147,14 +160,6 @@ def tile_list_msg_tanh_res_biasP_kernel(
 
         picked0 = [look_up(0, s) for s in range(2)]
         parted0 = [part(0, s, picked0[s]) for s in range(2)]
-        wd_raw = sb([P, N + N // 2], I32, "wd_raw", tag="picked00")
-        wd8_raw = wd_raw[:, 0:N]
-        wd4_raw = wd_raw[:, N : N + N // 2]
-        nc.sync.dma_start(wd4_raw, wd4_words[0].bitcast(I32))
-        nc.sync.dma_start(wd8_raw, wd8_words[0].rearrange("p n c -> p (n c)").bitcast(I32))
-        look_up_scales(1, "picked01")
-        wgo_sb = sb([P, J], F32, "wgo_sb", tag="picked_scales0")
-        nc.sync.dma_start(wgo_sb[:], wgo)
         picked1 = []
         for i, (a, s) in enumerate(w_order):
             quantise_weight(a, s)
@@ -186,12 +191,27 @@ def tile_list_msg_tanh_res_biasP_kernel(
         parted1 = [part(1, 0, picked1[0], "grouped11")]
         parted1.append(part(1, 1, picked1[1], "grouped00"))
 
-        wd4 = sb([P, PACK, 2 * P], U8, "wd4", tag="raw11")
-        wd8 = sb([P, PACK, P], I32, "wd8", tag="raw10")
-        wd_scales = sb([P, PACK, P], U8, "wd_scales", tag="grouped10")
-        nc.vector.tensor_copy(wd4[:].bitcast(U16), wd4_raw.bitcast(U16).rearrange("p (m t) -> p t m", t=PACK))
-        nc.vector.tensor_copy(wd8[:].rearrange("p t m -> p m t"), wd8_raw.rearrange("p (m t) -> p m t", t=PACK))
-        nc.vector.tensor_copy(wd_scales[:], wd_scales_raw[:].rearrange("p (m t) -> p t m", t=PACK))
+        wd4 = {}
+        wd8 = {}
+        wd_scales = {}
+
+        def deal(ts, tags):
+            count = ts.stop - ts.start
+            words4 = sb([P, count, 2 * P], U8, "wd4_%d" % ts.start, tag=tags[0])
+            words8 = sb([P, count, P], I32, "wd8_%d" % ts.start, tag=tags[1])
+            scales = sb([P, count, P], U8, "wd_scales_%d" % ts.start, tag=tags[2])
+            for dealt, arrived in (
+                (words4[:].bitcast(U16), wd4_raw.bitcast(U16)), (words8[:], wd8_raw), (scales[:], wd_scales_raw[:])
+            ):
+                nc.vector.tensor_copy(
+                    dealt.rearrange("p t m -> p m t"), arrived.rearrange("p (m t) -> p m t", t=PACK)[:, :, ts]
+                )
+            for t in range(ts.start, ts.stop):
+                wd4[t] = words4[:, t - ts.start, :]
+                wd8[t] = words8[:, t - ts.start, :]
+                wd_scales[t] = scales[:, t - ts.start, :]
+
+        deal(slice(0, 1), ("raw11", "raw10", "grouped10"))
 
         h_codes = [sb([P, HALF], U32, "h_codes%d" % h) for h in range(2)]
         h_scales = [sb([P, HALF], U8, "h_scales%d" % h) for h in range(2)]
@@ -214,6 +234,7 @@ def tile_list_msg_tanh_res_biasP_kernel(
             squash(e)
         quantise_hidden(0, 0, woven0[0])
         squash(3)
+        deal(slice(1, PACK), ("th01", "th02", "th03"))
         quantise_hidden(0, QUARTER, woven0[1])
         late_page("woven01")
 
@@ -222,13 +243,13 @@ def tile_list_msg_tanh_res_biasP_kernel(
             codes = h_codes[h][:, lo : lo + width]
             scales = h_scales[h][:, lo : lo + width]
             nc.tensor.matmul_mx(
-                acc[:, 0:width], lhsT=wd8[:, t, :].bitcast(FP8X4), lhsT_scale=wd_scales[4:P, t, :],
+                acc[:, 0:width], lhsT=wd8[t].bitcast(FP8X4), lhsT_scale=wd_scales[t][4:P, :],
                 rhs=codes.bitcast(FP8X4), rhs_scale=scales, start=True, stop=False,
             )
             step = HALF if width == HALF else P
             for at in range(0, width, step):
                 nc.tensor.matmul_mx(
-                    acc[:, at : at + step], lhsT=wd4[:, t, :].bitcast(FP4X4), lhsT_scale=wd_scales[:, t, :],
+                    acc[:, at : at + step], lhsT=wd4[t].bitcast(FP4X4), lhsT_scale=wd_scales[t],
                     rhs=codes[:, at : at + step].bitcast(FP8X4), rhs_scale=scales[:, at : at + step],
                     start=False, stop=at + step == width,
                 )
@@ -271,22 +292,23 @@ def tile_list_msg_tanh_res_biasP_kernel(
 
         out_rows = out_0.rearrange("(p t) c -> t p c", t=PACK)
         starts = [sum(OUT_WIDTHS[:c]) for c in range(len(OUT_WIDTHS))]
-        pairs = [sb([P, 2, width, 2], BF16, "pairs%d" % c) for c, width in enumerate(OUT_WIDTHS)]
+        pairs = sb([P, 2, T, 2], BF16, "pairs", tag="b_sb")
 
         out_words = out_1[0].rearrange("p t c -> p (t c)").bitcast(I32)
         out_scales = sb([P, OUT_GROUP], U8, "out_scales")
         out_codes = [sb([P, OUT_GROUP], U32, "out_codes%d" % g) for g in range(T // OUT_GROUP)]
         for t in range(PACK):
             nc.sync.dma_start(out_rows[t], pages[t][:])
-            for c, width in enumerate(OUT_WIDTHS):
-                nc.scalar.activation(pairs[c][:, t // 2, :, t % 2], pages[t][:, starts[c] : starts[c] + width], ACT.Copy)
+            for lo, width in zip(starts, OUT_WIDTHS) if t == PACK - 1 else ((0, T),):
+                nc.scalar.activation(pairs[:, t // 2, lo : lo + width, t % 2], pages[t][:, lo : lo + width], ACT.Copy)
 
         def weave_out(c):
             on_scalar = c >= len(OUT_WIDTHS) - SCALAR_WEAVES
             woven = sb([P, OUT_WIDTHS[c], PACK], BF16, "woven_out%d" % c)
             word = U32 if on_scalar else I32
             dst = woven[:].rearrange("p n t -> p (n t)").bitcast(word).rearrange("p (n u) -> p n u", u=2)
-            src = pairs[c][:].rearrange("p u n e -> p u (n e)").bitcast(word).rearrange("p u n -> p n u")
+            src = pairs[:, :, starts[c] : starts[c] + OUT_WIDTHS[c], :].rearrange("p u n e -> p u (n e)")
+            src = src.bitcast(word).rearrange("p u n -> p n u")
             if on_scalar:
                 nc.scalar.copy(dst, src)
             else:

@@ -27,7 +27,7 @@ HALF = J // 2
 QUARTER = HALF // 2
 W_SPLIT = 2
 OUT_GROUP = 512
-OUT_WIDTHS = (128, 128, 256, 512, 512, 256, 256)
+OUT_WIDTHS = (128, 128, 256, 256, 256, 256, 256, 128, 256, 128)
 SCALAR_WEAVES = 2
 
 
@@ -295,7 +295,7 @@ def tile_list_msg_tanh_res_biasP_kernel(
         pairs = sb([P, 2, T, 2], BF16, "pairs", tag="b_sb")
 
         out_words = out_1[0].rearrange("p t c -> p (t c)").bitcast(I32)
-        out_scales = sb([P, OUT_GROUP], U8, "out_scales")
+        out_scales = sb([P, 2, OUT_GROUP], U8, "out_scales")
         out_codes = [sb([P, OUT_GROUP], U32, "out_codes%d" % g) for g in range(T // OUT_GROUP)]
         for t in range(PACK):
             nc.sync.dma_start(out_rows[t], pages[t][:])
@@ -319,12 +319,14 @@ def tile_list_msg_tanh_res_biasP_kernel(
             g, lo = divmod(starts[c], OUT_GROUP)
             cut = slice(lo, lo + OUT_WIDTHS[c])
             nc.vector.quantize_mx(
-                out_codes[g][:, cut].bitcast(FP8X4), out_scales[4 * g : P, cut], woven[:].rearrange("p n t -> p (n t)")
+                out_codes[g][:, cut].bitcast(FP8X4), out_scales[4 * (g // 2) : P, g % 2, cut], woven[:].rearrange("p n t -> p (n t)")
             )
-            if g == T // OUT_GROUP - 1:
-                nc.sync.dma_start(out_words[:, starts[c] : starts[c] + OUT_WIDTHS[c]], out_codes[g][:, cut].bitcast(I32))
-            elif cut.stop == OUT_GROUP:
-                nc.sync.dma_start(out_words[:, g * OUT_GROUP : (g + 1) * OUT_GROUP], out_codes[g][:].bitcast(I32))
+            if c == len(OUT_WIDTHS) - 1 or c == len(OUT_WIDTHS) - 2 or cut.stop == OUT_GROUP:
+                first = lo if c == len(OUT_WIDTHS) - 1 else 0
+                nc.sync.dma_start(
+                    out_words[:, g * OUT_GROUP + first : g * OUT_GROUP + cut.stop],
+                    out_codes[g][:, first : cut.stop].bitcast(I32),
+                )
 
         woven_outs = [weave_out(0)]
         for c in range(len(OUT_WIDTHS)):
@@ -333,6 +335,6 @@ def tile_list_msg_tanh_res_biasP_kernel(
             quantise_out(c, woven_outs[c])
         for q in range(QUADS):
             (nc.sync, nc.scalar)[q % 2].dma_start(
-                out_2[0, 4 * q : 4 * q + 4, :].bitcast(I32).rearrange("r (g n) -> g r n", g=T // OUT_GROUP),
-                out_scales[32 * q : 32 * q + 16, :].bitcast(I32),
+                out_2[0, 4 * q : 4 * q + 4, :].bitcast(I32).rearrange("r (g n) -> g r n", g=2),
+                out_scales[32 * q : 32 * q + 8, :, :].rearrange("p d n -> p (d n)").bitcast(I32),
             )

@@ -164,7 +164,7 @@ def tile_list_msg_tanh_res_biasP_kernel(
         for i, (a, s) in enumerate(w_order):
             quantise_weight(a, s)
             if i < 2:
-                picked1.append(look_up(1, i, "grouped%d%d" % (a, s)))
+                picked1.append(look_up(1, i, "raw%d%d" % (a, s)))
 
         def first_pass(out, h, lo, width, t, a, s, parted, start, stop):
             w_cols = slice(t * P, (t + 1) * P)
@@ -188,8 +188,7 @@ def tile_list_msg_tanh_res_biasP_kernel(
                         (a, s) == w_order[0] and t == 0, (a, s) == w_order[-1] and t == PACK - 1,
                     )
 
-        parted1 = [part(1, 0, picked1[0], "grouped11")]
-        parted1.append(part(1, 1, picked1[1], "grouped00"))
+        parted1 = [part(1, s, picked1[s], ("raw10", "raw11")[s]) for s in range(2)]
 
         wd4 = {}
         wd8 = {}
@@ -211,7 +210,7 @@ def tile_list_msg_tanh_res_biasP_kernel(
                 wd8[t] = words8[:, t - ts.start, :]
                 wd_scales[t] = scales[:, t - ts.start, :]
 
-        deal(slice(0, 1), ("raw11", "raw10", "grouped10"))
+        deal(slice(0, 1), ("grouped00", "grouped01", "grouped10"))
 
         h_codes = [sb([P, HALF], U32, "h_codes%d" % h) for h in range(2)]
         h_scales = [sb([P, HALF], U8, "h_scales%d" % h) for h in range(2)]

@@ -25,7 +25,7 @@ LAST_QUAD = P - 32
 LIST_ROWS = 16
 HALF = J // 2
 QUARTER = HALF // 2
-W_SPLIT = 2
+SCALAR_LAST = 48
 OUT_GROUP = 512
 OUT_WIDTHS = (128, 128, 256, 256, 256, 256, 256, 128, 256, 128)
 SCALAR_WEAVES = 2
@@ -140,23 +140,30 @@ def tile_list_msg_tanh_res_biasP_kernel(
 
         w_codes = {}
         w_scales = {}
-        m_cols = P // W_SPLIT
-        r_cols = R // W_SPLIT
 
         def quantise_weight(a, s):
             grouped = sb([P, PACK, P, PACK], BF16, "grouped%d%d" % (a, s))
-            for u in range(W_SPLIT):
-                dst = grouped[:, :, u * m_cols : (u + 1) * m_cols, :].rearrange("p t m j -> p m j t")
-                src = raw[a, s][:, :, u * r_cols : (u + 1) * r_cols].rearrange("p j (m t) -> p m j t", t=PACK)
-                if (a, s) == w_order[-1] and u == W_SPLIT - 1:
-                    nc.vector.tensor_copy(dst, src)
-                else:
-                    nc.scalar.activation(dst, src, ACT.Copy)
+            last = (a, s) == w_order[-1]
+
+            def round_columns(copy, lo, hi):
+                copy(
+                    grouped[:, :, lo:hi, :].rearrange("p t m j -> p m j t"),
+                    raw[a, s][:, :, lo * PACK : hi * PACK].rearrange("p j (m t) -> p m j t", t=PACK),
+                )
+
+            round_columns(lambda dst, src: nc.scalar.activation(dst, src, ACT.Copy), 0, SCALAR_LAST if last else P)
+            if last:
+                round_columns(nc.vector.tensor_copy, SCALAR_LAST, P)
             w_codes[a, s] = sb([P, R], U32, "w_codes%d%d" % (a, s))
             w_scales[a, s] = sb([P, R], U8, "w_scales%d%d" % (a, s))
-            nc.vector.quantize_mx(
-                w_codes[a, s][:].bitcast(FP8X4), w_scales[a, s][:], grouped[:].rearrange("p t m j -> p (t m j)")
-            )
+            step = PACK // 2 if last else PACK
+            for t in range(0, PACK, step):
+                cut = slice(t * P, (t + step) * P)
+                nc.vector.quantize_mx(
+                    w_codes[a, s][:, cut].bitcast(FP8X4),
+                    w_scales[a, s][:, cut],
+                    grouped[:, t : t + step, :, :].rearrange("p t m j -> p (t m j)"),
+                )
 
         picked0 = [look_up(0, s) for s in range(2)]
         parted0 = [part(0, s, picked0[s]) for s in range(2)]
@@ -190,27 +197,21 @@ def tile_list_msg_tanh_res_biasP_kernel(
 
         parted1 = [part(1, s, picked1[s], ("raw10", "raw11")[s]) for s in range(2)]
 
-        wd4 = {}
+        wd4 = sb([P, PACK, 2 * P], U8, "wd4", tag="grouped00")
+        wd_scales = sb([P, PACK, P], U8, "wd_scales", tag="grouped01")
+        nc.vector.tensor_copy(wd4[:].bitcast(U16), wd4_raw.bitcast(U16).rearrange("p (m t) -> p t m", t=PACK))
+        nc.vector.tensor_copy(wd_scales[:], wd_scales_raw[:].rearrange("p (m t) -> p t m", t=PACK))
         wd8 = {}
-        wd_scales = {}
 
-        def deal(ts, tags):
-            count = ts.stop - ts.start
-            words4 = sb([P, count, 2 * P], U8, "wd4_%d" % ts.start, tag=tags[0])
-            words8 = sb([P, count, P], I32, "wd8_%d" % ts.start, tag=tags[1])
-            scales = sb([P, count, P], U8, "wd_scales_%d" % ts.start, tag=tags[2])
-            for dealt, arrived in (
-                (words4[:].bitcast(U16), wd4_raw.bitcast(U16)), (words8[:], wd8_raw), (scales[:], wd_scales_raw[:])
-            ):
-                nc.vector.tensor_copy(
-                    dealt.rearrange("p t m -> p m t"), arrived.rearrange("p (m t) -> p m t", t=PACK)[:, :, ts]
-                )
+        def deal_wd8(ts, tag):
+            words = sb([P, ts.stop - ts.start, P], I32, "wd8_%d" % ts.start, tag=tag)
+            nc.vector.tensor_copy(
+                words[:].rearrange("p t m -> p m t"), wd8_raw.rearrange("p (m t) -> p m t", t=PACK)[:, :, ts]
+            )
             for t in range(ts.start, ts.stop):
-                wd4[t] = words4[:, t - ts.start, :]
-                wd8[t] = words8[:, t - ts.start, :]
-                wd_scales[t] = scales[:, t - ts.start, :]
+                wd8[t] = words[:, t - ts.start, :]
 
-        deal(slice(0, 1), ("grouped00", "grouped01", "grouped10"))
+        deal_wd8(slice(0, 1), "grouped10")
 
         h_codes = [sb([P, HALF], U32, "h_codes%d" % h) for h in range(2)]
         h_scales = [sb([P, HALF], U8, "h_scales%d" % h) for h in range(2)]
@@ -233,7 +234,7 @@ def tile_list_msg_tanh_res_biasP_kernel(
             squash(e)
         quantise_hidden(0, 0, woven0[0])
         squash(3)
-        deal(slice(1, PACK), ("th01", "th02", "th03"))
+        deal_wd8(slice(1, PACK), "th02")
         quantise_hidden(0, QUARTER, woven0[1])
         late_page("woven01")
 
@@ -242,13 +243,13 @@ def tile_list_msg_tanh_res_biasP_kernel(
             codes = h_codes[h][:, lo : lo + width]
             scales = h_scales[h][:, lo : lo + width]
             nc.tensor.matmul_mx(
-                acc[:, 0:width], lhsT=wd8[t].bitcast(FP8X4), lhsT_scale=wd_scales[t][4:P, :],
+                acc[:, 0:width], lhsT=wd8[t].bitcast(FP8X4), lhsT_scale=wd_scales[4:P, t, :],
                 rhs=codes.bitcast(FP8X4), rhs_scale=scales, start=True, stop=False,
             )
             step = HALF if width == HALF else P
             for at in range(0, width, step):
                 nc.tensor.matmul_mx(
-                    acc[:, at : at + step], lhsT=wd4[t].bitcast(FP4X4), lhsT_scale=wd_scales[t],
+                    acc[:, at : at + step], lhsT=wd4[:, t, :].bitcast(FP4X4), lhsT_scale=wd_scales[:, t, :],
                     rhs=codes[:, at : at + step].bitcast(FP8X4), rhs_scale=scales[:, at : at + step],
                     start=False, stop=at + step == width,
                 )
@@ -294,7 +295,7 @@ def tile_list_msg_tanh_res_biasP_kernel(
         pairs = sb([P, 2, T, 2], BF16, "pairs", tag="b_sb")
 
         out_words = out_1[0].rearrange("p t c -> p (t c)").bitcast(I32)
-        out_scales = sb([P, 2, OUT_GROUP], U8, "out_scales")
+        out_scales = sb([P, OUT_GROUP], U8, "out_scales")
         out_codes = [sb([P, OUT_GROUP], U32, "out_codes%d" % g) for g in range(T // OUT_GROUP)]
         for t in range(PACK):
             nc.sync.dma_start(out_rows[t], pages[t][:])
@@ -318,7 +319,7 @@ def tile_list_msg_tanh_res_biasP_kernel(
             g, lo = divmod(starts[c], OUT_GROUP)
             cut = slice(lo, lo + OUT_WIDTHS[c])
             nc.vector.quantize_mx(
-                out_codes[g][:, cut].bitcast(FP8X4), out_scales[4 * (g // 2) : P, g % 2, cut], woven[:].rearrange("p n t -> p (n t)")
+                out_codes[g][:, cut].bitcast(FP8X4), out_scales[4 * g : P, cut], woven[:].rearrange("p n t -> p (n t)")
             )
             if c == len(OUT_WIDTHS) - 1 or c == len(OUT_WIDTHS) - 2 or cut.stop == OUT_GROUP:
                 first = lo if c == len(OUT_WIDTHS) - 1 else 0
@@ -334,6 +335,6 @@ def tile_list_msg_tanh_res_biasP_kernel(
             quantise_out(c, woven_outs[c])
         for q in range(QUADS):
             (nc.sync, nc.scalar)[q % 2].dma_start(
-                out_2[0, 4 * q : 4 * q + 4, :].bitcast(I32).rearrange("r (g n) -> g r n", g=2),
-                out_scales[32 * q : 32 * q + 8, :, :].rearrange("p d n -> p (d n)").bitcast(I32),
+                out_2[0, 4 * q : 4 * q + 4, :].bitcast(I32).rearrange("r (g n) -> g r n", g=T // OUT_GROUP),
+                out_scales[32 * q : 32 * q + 16, :].bitcast(I32),
             )

@@ -25,10 +25,11 @@ LAST_QUAD = P - 32
 LIST_ROWS = 16
 HALF = J // 2
 QUARTER = HALF // 2
-SCALAR_LAST = 48
+SCALAR_LAST = 64
 OUT_GROUP = 512
-OUT_WIDTHS = (128, 128, 256, 256, 256, 256, 256, 128, 256, 128)
-SCALAR_WEAVES = 2
+OUT_WIDTHS = (256, 256, 256, 256, 256, 256, 256, 128, 128)
+VECTOR_ROUNDS = 2
+SCALAR_WEAVES = 3
 
 
 def tile_list_msg_tanh_res_biasP_kernel(
@@ -187,13 +188,16 @@ def tile_list_msg_tanh_res_biasP_kernel(
             )
 
         sums0 = [bank(e, "sums0%d" % e) for e in range(HALF // P)]
-        for a, s in w_order:
-            for e in range(HALF // P):
-                for t in range(PACK):
-                    first_pass(
-                        sums0[e][:, t * P : (t + 1) * P], 0, e * P, P, t, a, s, parted0,
-                        (a, s) == w_order[0] and t == 0, (a, s) == w_order[-1] and t == PACK - 1,
-                    )
+        swapped = w_order[:2] + w_order[:1:-1]
+        for banks, steps in (((0, 1, 2, 3), (0, 1)), ((0, 1), (2, 3)), ((2, 3), (2, 3))):
+            for i in steps:
+                for e in banks:
+                    a, s = (w_order if e < 2 else swapped)[i]
+                    for t in range(PACK):
+                        first_pass(
+                            sums0[e][:, t * P : (t + 1) * P], 0, e * P, P, t, a, s, parted0,
+                            i == 0 and t == 0, i == len(w_order) - 1 and t == PACK - 1,
+                        )
 
         parted1 = [part(1, s, picked1[s], ("raw10", "raw11")[s]) for s in range(2)]
 
@@ -295,12 +299,23 @@ def tile_list_msg_tanh_res_biasP_kernel(
         pairs = sb([P, 2, T, 2], BF16, "pairs", tag="b_sb")
 
         out_words = out_1[0].rearrange("p t c -> p (t c)").bitcast(I32)
-        out_scales = sb([P, OUT_GROUP], U8, "out_scales")
+        out_scales = sb([P, 2, OUT_GROUP], U8, "out_scales")
         out_codes = [sb([P, OUT_GROUP], U32, "out_codes%d" % g) for g in range(T // OUT_GROUP)]
+        own = starts[VECTOR_ROUNDS]
         for t in range(PACK):
             nc.sync.dma_start(out_rows[t], pages[t][:])
-            for lo, width in zip(starts, OUT_WIDTHS) if t == PACK - 1 else ((0, T),):
-                nc.scalar.activation(pairs[:, t // 2, lo : lo + width, t % 2], pages[t][:, lo : lo + width], ACT.Copy)
+            if t == PACK - 1:
+                steps = list(zip(starts, OUT_WIDTHS))
+            elif t == PACK - 2:
+                steps = [(0, own), (own, T - own)]
+            else:
+                steps = [(0, T)]
+            for lo, width in steps:
+                rounded = pairs[:, t // 2, lo : lo + width, t % 2]
+                if t >= PACK - 2 and lo < own:
+                    nc.vector.tensor_copy(rounded, pages[t][:, lo : lo + width])
+                else:
+                    nc.scalar.activation(rounded, pages[t][:, lo : lo + width], ACT.Copy)
 
         def weave_out(c):
             on_scalar = c >= len(OUT_WIDTHS) - SCALAR_WEAVES
@@ -319,7 +334,7 @@ def tile_list_msg_tanh_res_biasP_kernel(
             g, lo = divmod(starts[c], OUT_GROUP)
             cut = slice(lo, lo + OUT_WIDTHS[c])
             nc.vector.quantize_mx(
-                out_codes[g][:, cut].bitcast(FP8X4), out_scales[4 * g : P, cut], woven[:].rearrange("p n t -> p (n t)")
+                out_codes[g][:, cut].bitcast(FP8X4), out_scales[4 * (g // 2) : P, g % 2, cut], woven[:].rearrange("p n t -> p (n t)")
             )
             if c == len(OUT_WIDTHS) - 1 or c == len(OUT_WIDTHS) - 2 or cut.stop == OUT_GROUP:
                 first = lo if c == len(OUT_WIDTHS) - 1 else 0
@@ -335,6 +350,6 @@ def tile_list_msg_tanh_res_biasP_kernel(
             quantise_out(c, woven_outs[c])
         for q in range(QUADS):
             (nc.sync, nc.scalar)[q % 2].dma_start(
-                out_2[0, 4 * q : 4 * q + 4, :].bitcast(I32).rearrange("r (g n) -> g r n", g=T // OUT_GROUP),
-                out_scales[32 * q : 32 * q + 16, :].bitcast(I32),
+                out_2[0, 4 * q : 4 * q + 4, :].bitcast(I32).rearrange("r (g n) -> g r n", g=2),
+                out_scales[32 * q : 32 * q + 8, :, :].rearrange("p d n -> p (d n)").bitcast(I32),
             )

@@ -15,6 +15,7 @@ FP8X4 = mybir.dt.float8_e4m3fn_x4
 FP4X4 = mybir.dt.float4_e2m1fn_x4
 ACT = mybir.ActivationFunctionType
 MULT = mybir.AluOpType.mult
+ADD = mybir.AluOpType.add
 
 P = 128
 PACK = 4
@@ -25,7 +26,7 @@ LAST_QUAD = P - 32
 LIST_ROWS = 16
 HALF = J // 2
 QUARTER = HALF // 2
-SCALAR_LAST = 64
+SCALAR_COLS = 88
 OUT_GROUP = 512
 OUT_WIDTHS = (256, 256, 256, 256, 256, 256, 256, 128, 128)
 VECTOR_ROUNDS = 2
@@ -75,13 +76,12 @@ def tile_list_msg_tanh_res_biasP_kernel(
         nc.scalar.dma_start(sm_raw[:], sm.rearrange("(p t) -> p t", t=PACK))
         nc.scalar.dma_start(b_sb[:], b.rearrange("(p t) -> p t", t=PACK))
 
-        wd_scales_raw = sb([P, N], U8, "wd_scales_raw")
-        nc.vector.memset(wd_scales_raw[:].bitcast(I32), 0)
         nc.vector.memset(table_scales[0:LAST_QUAD, :].bitcast(I32), 0)
         edge_scales = sb([P, 2, PASSES, J], U8, "edge_scales")
         nc.vector.memset(edge_scales[:].rearrange("p h a n -> p (h a n)").bitcast(I32), 0)
-        pages = [sb([P, T], F32, "page0")]
-        nc.vector.memset(pages[0][:], 0.0)
+        wd_scales_raw = sb([P, N], U8, "wd_scales_raw")
+        nc.vector.memset(wd_scales_raw[:].bitcast(I32), 0)
+        pages = []
 
         def late_page(tag):
             page = sb([P, T], F32, "page%d" % len(pages), tag=tag)
@@ -98,6 +98,7 @@ def tile_list_msg_tanh_res_biasP_kernel(
 
         sm_rows = sb([P, P, PACK], F32, "sm_rows")
         nc.scalar.activation(sm_rows[:], sm_raw[:].unsqueeze(1).to_broadcast([P, P, PACK]), ACT.Copy)
+        late_page("sm_raw")
         for w in range(2):
             load_wd_scales(w)
 
@@ -132,32 +133,35 @@ def tile_list_msg_tanh_res_biasP_kernel(
             nc.vector.tensor_copy(picked[:], table[:].bitcast(U32).indirect(entries(s, h * HALF, HALF)))
             return picked
 
-        def part(h, s, picked, tag=None):
-            parted = sb([P, PASSES, 2 * HALF], U8, "parted%d%d" % (h, s), tag=tag)
-            nc.vector.tensor_copy(
-                parted[:].bitcast(U16), picked[:].bitcast(U16).rearrange("p (n d) -> p d n", d=PASSES)
-            )
+        def part(h, picked, tag):
+            parted = sb([P, 2, PASSES, 2 * HALF], U8, "parted%d" % h, tag=tag)
+            for s in range(2):
+                nc.vector.tensor_copy(
+                    parted[:, s, :, :].bitcast(U16), picked[s][:].bitcast(U16).rearrange("p (n d) -> p d n", d=PASSES)
+                )
             return parted
 
         w_codes = {}
         w_scales = {}
 
-        def quantise_weight(a, s):
-            grouped = sb([P, PACK, P, PACK], BF16, "grouped%d%d" % (a, s))
-            last = (a, s) == w_order[-1]
-
-            def round_columns(copy, lo, hi):
-                copy(
-                    grouped[:, :, lo:hi, :].rearrange("p t m j -> p m j t"),
-                    raw[a, s][:, :, lo * PACK : hi * PACK].rearrange("p j (m t) -> p m j t", t=PACK),
+        def quantise_weight(i, tag=None):
+            a, s = w_order[i]
+            grouped = sb([P, PACK, P, PACK], BF16, "grouped%d" % i, tag=tag)
+            split = P if i < 2 else SCALAR_COLS
+            nc.scalar.activation(
+                grouped[:, :, 0:split, :].rearrange("p t m j -> p m j t"),
+                raw[a, s][:, :, 0 : split * PACK].rearrange("p j (m t) -> p m j t", t=PACK),
+                ACT.Copy,
+            )
+            if split < P:
+                nc.gpsimd.tensor_scalar(
+                    grouped[:, :, split:P, :],
+                    raw[a, s][:, :, split * PACK : R].rearrange("p j (m t) -> p t m j", t=PACK),
+                    1.0, 0.0, MULT, ADD,
                 )
-
-            round_columns(lambda dst, src: nc.scalar.activation(dst, src, ACT.Copy), 0, SCALAR_LAST if last else P)
-            if last:
-                round_columns(nc.vector.tensor_copy, SCALAR_LAST, P)
             w_codes[a, s] = sb([P, R], U32, "w_codes%d%d" % (a, s))
             w_scales[a, s] = sb([P, R], U8, "w_scales%d%d" % (a, s))
-            step = PACK // 2 if last else PACK
+            step = PACK // 2 if i == 3 else PACK
             for t in range(0, PACK, step):
                 cut = slice(t * P, (t + step) * P)
                 nc.vector.quantize_mx(
@@ -167,12 +171,24 @@ def tile_list_msg_tanh_res_biasP_kernel(
                 )
 
         picked0 = [look_up(0, s) for s in range(2)]
-        parted0 = [part(0, s, picked0[s]) for s in range(2)]
-        picked1 = []
-        for i, (a, s) in enumerate(w_order):
-            quantise_weight(a, s)
-            if i < 2:
-                picked1.append(look_up(1, i, "raw%d%d" % (a, s)))
+        quantise_weight(0)
+        parted0 = part(0, picked0, "raw00")
+        picked1 = [look_up(1, 0, "picked00")]
+        quantise_weight(1)
+        picked1.append(look_up(1, 1, "raw01"))
+        quantise_weight(2, "picked01")
+        wd_scales = {}
+
+        def deal_wd_scales(first, tag):
+            dealt = sb([P, 2, P], U8, "wd_scales%d" % first, tag=tag)
+            nc.vector.tensor_copy(
+                dealt[:], wd_scales_raw[:].rearrange("p (m t) -> p t m", t=PACK)[:, first : first + 2, :]
+            )
+            for t in range(2):
+                wd_scales[first + t] = dealt[:, t, :]
+
+        deal_wd_scales(0, "picked01")
+        quantise_weight(3, "grouped1")
 
         def first_pass(out, h, lo, width, t, a, s, parted, start, stop):
             w_cols = slice(t * P, (t + 1) * P)
@@ -181,7 +197,7 @@ def tile_list_msg_tanh_res_biasP_kernel(
                 out,
                 lhsT=w_codes[a, s][:, w_cols].bitcast(FP8X4),
                 lhsT_scale=w_scales[a, s][:, w_cols],
-                rhs=parted[s][:, a, 2 * lo : 2 * (lo + width)].bitcast(FP4X4),
+                rhs=parted[:, s, a, 2 * lo : 2 * (lo + width)].bitcast(FP4X4),
                 rhs_scale=edge_scales[:, h, a, at : at + width],
                 start=start,
                 stop=stop,
@@ -199,23 +215,21 @@ def tile_list_msg_tanh_res_biasP_kernel(
                             i == 0 and t == 0, i == len(w_order) - 1 and t == PACK - 1,
                         )
 
-        parted1 = [part(1, s, picked1[s], ("raw10", "raw11")[s]) for s in range(2)]
+        parted1 = part(1, picked1, "raw11")
 
-        wd4 = sb([P, PACK, 2 * P], U8, "wd4", tag="grouped00")
-        wd_scales = sb([P, PACK, P], U8, "wd_scales", tag="grouped01")
-        nc.vector.tensor_copy(wd4[:].bitcast(U16), wd4_raw.bitcast(U16).rearrange("p (m t) -> p t m", t=PACK))
-        nc.vector.tensor_copy(wd_scales[:], wd_scales_raw[:].rearrange("p (m t) -> p t m", t=PACK))
-        wd8 = {}
+        wd8 = sb([P, PACK, P], U32, "wd8")
+        nc.scalar.copy(
+            wd8[:].rearrange("p t m -> p m t"), wd8_raw.bitcast(U32).rearrange("p (m t) -> p m t", t=PACK)
+        )
+        wd4 = {}
 
-        def deal_wd8(ts, tag):
-            words = sb([P, ts.stop - ts.start, P], I32, "wd8_%d" % ts.start, tag=tag)
-            nc.vector.tensor_copy(
-                words[:].rearrange("p t m -> p m t"), wd8_raw.rearrange("p (m t) -> p m t", t=PACK)[:, :, ts]
-            )
+        def deal_wd4(ts, tag=None):
+            words = sb([P, ts.stop - ts.start, 2 * P], U8, "wd4_%d" % ts.start, tag=tag)
+            nc.scalar.copy(words[:].bitcast(U16), wd4_raw.bitcast(U16).rearrange("p (m t) -> p t m", t=PACK)[:, ts, :])
             for t in range(ts.start, ts.stop):
-                wd8[t] = words[:, t - ts.start, :]
+                wd4[t] = words[:, t - ts.start, :]
 
-        deal_wd8(slice(0, 1), "grouped10")
+        deal_wd4(slice(0, 1))
 
         h_codes = [sb([P, HALF], U32, "h_codes%d" % h) for h in range(2)]
         h_scales = [sb([P, HALF], U8, "h_scales%d" % h) for h in range(2)]
@@ -238,7 +252,8 @@ def tile_list_msg_tanh_res_biasP_kernel(
             squash(e)
         quantise_hidden(0, 0, woven0[0])
         squash(3)
-        deal_wd8(slice(1, PACK), "th02")
+        deal_wd4(slice(1, PACK), "woven00")
+        deal_wd_scales(2, "th02")
         quantise_hidden(0, QUARTER, woven0[1])
         late_page("woven01")
 
@@ -247,13 +262,13 @@ def tile_list_msg_tanh_res_biasP_kernel(
             codes = h_codes[h][:, lo : lo + width]
             scales = h_scales[h][:, lo : lo + width]
             nc.tensor.matmul_mx(
-                acc[:, 0:width], lhsT=wd8[t].bitcast(FP8X4), lhsT_scale=wd_scales[4:P, t, :],
+                acc[:, 0:width], lhsT=wd8[:, t, :].bitcast(FP8X4), lhsT_scale=wd_scales[t][4:P, :],
                 rhs=codes.bitcast(FP8X4), rhs_scale=scales, start=True, stop=False,
             )
             step = HALF if width == HALF else P
             for at in range(0, width, step):
                 nc.tensor.matmul_mx(
-                    acc[:, at : at + step], lhsT=wd4[:, t, :].bitcast(FP4X4), lhsT_scale=wd_scales[:, t, :],
+                    acc[:, at : at + step], lhsT=wd4[t].bitcast(FP4X4), lhsT_scale=wd_scales[t],
                     rhs=codes[:, at : at + step].bitcast(FP8X4), rhs_scale=scales[:, at : at + step],
                     start=False, stop=at + step == width,
                 )

@@ -15,7 +15,6 @@ FP8X4 = mybir.dt.float8_e4m3fn_x4
 FP4X4 = mybir.dt.float4_e2m1fn_x4
 ACT = mybir.ActivationFunctionType
 MULT = mybir.AluOpType.mult
-ADD = mybir.AluOpType.add
 
 P = 128
 PACK = 4
@@ -26,7 +25,7 @@ LAST_QUAD = P - 32
 LIST_ROWS = 16
 HALF = J // 2
 QUARTER = HALF // 2
-SCALAR_COLS = 88
+SCALAR_LAST = 64
 OUT_GROUP = 512
 OUT_WIDTHS = (256, 256, 256, 256, 256, 256, 256, 128, 128)
 VECTOR_ROUNDS = 2
@@ -147,17 +146,16 @@ def tile_list_msg_tanh_res_biasP_kernel(
         def quantise_weight(i, tag=None):
             a, s = w_order[i]
             grouped = sb([P, PACK, P, PACK], BF16, "grouped%d" % i, tag=tag)
-            split = P if i < 2 else SCALAR_COLS
+            split = P if i < 3 else SCALAR_LAST
             nc.scalar.activation(
                 grouped[:, :, 0:split, :].rearrange("p t m j -> p m j t"),
                 raw[a, s][:, :, 0 : split * PACK].rearrange("p j (m t) -> p m j t", t=PACK),
                 ACT.Copy,
             )
             if split < P:
-                nc.gpsimd.tensor_scalar(
-                    grouped[:, :, split:P, :],
-                    raw[a, s][:, :, split * PACK : R].rearrange("p j (m t) -> p t m j", t=PACK),
-                    1.0, 0.0, MULT, ADD,
+                nc.vector.tensor_copy(
+                    grouped[:, :, split:P, :].rearrange("p t m j -> p m j t"),
+                    raw[a, s][:, :, split * PACK : R].rearrange("p j (m t) -> p m j t", t=PACK),
                 )
             w_codes[a, s] = sb([P, R], U32, "w_codes%d%d" % (a, s))
             w_scales[a, s] = sb([P, R], U8, "w_scales%d%d" % (a, s))
@@ -176,7 +174,7 @@ def tile_list_msg_tanh_res_biasP_kernel(
         picked1 = [look_up(1, 0, "picked00")]
         quantise_weight(1)
         picked1.append(look_up(1, 1, "raw01"))
-        quantise_weight(2, "picked01")
+        quantise_weight(2)
         wd_scales = {}
 
         def deal_wd_scales(first, tag):
@@ -187,8 +185,8 @@ def tile_list_msg_tanh_res_biasP_kernel(
             for t in range(2):
                 wd_scales[first + t] = dealt[:, t, :]
 
-        deal_wd_scales(0, "picked01")
-        quantise_weight(3, "grouped1")
+        deal_wd_scales(0, "grouped2")
+        quantise_weight(3)
 
         def first_pass(out, h, lo, width, t, a, s, parted, start, stop):
             w_cols = slice(t * P, (t + 1) * P)

@@ -75,12 +75,13 @@ def tile_list_msg_tanh_res_biasP_kernel(
         nc.scalar.dma_start(sm_raw[:], sm.rearrange("(p t) -> p t", t=PACK))
         nc.scalar.dma_start(b_sb[:], b.rearrange("(p t) -> p t", t=PACK))
 
+        wd_scales_raw = sb([P, N], U8, "wd_scales_raw")
+        nc.vector.memset(wd_scales_raw[:].bitcast(I32), 0)
         nc.vector.memset(table_scales[0:LAST_QUAD, :].bitcast(I32), 0)
         edge_scales = sb([P, 2, PASSES, J], U8, "edge_scales")
         nc.vector.memset(edge_scales[:].rearrange("p h a n -> p (h a n)").bitcast(I32), 0)
-        wd_scales_raw = sb([P, N], U8, "wd_scales_raw")
-        nc.vector.memset(wd_scales_raw[:].bitcast(I32), 0)
-        pages = []
+        pages = [sb([P, T], F32, "page0")]
+        nc.vector.memset(pages[0][:], 0.0)
 
         def late_page(tag):
             page = sb([P, T], F32, "page%d" % len(pages), tag=tag)
@@ -97,7 +98,6 @@ def tile_list_msg_tanh_res_biasP_kernel(
 
         sm_rows = sb([P, P, PACK], F32, "sm_rows")
         nc.scalar.activation(sm_rows[:], sm_raw[:].unsqueeze(1).to_broadcast([P, P, PACK]), ACT.Copy)
-        late_page("sm_raw")
         for w in range(2):
             load_wd_scales(w)
 
@@ -185,7 +185,6 @@ def tile_list_msg_tanh_res_biasP_kernel(
             for t in range(2):
                 wd_scales[first + t] = dealt[:, t, :]
 
-        deal_wd_scales(0, "grouped2")
         quantise_weight(3)
 
         def first_pass(out, h, lo, width, t, a, s, parted, start, stop):
@@ -214,6 +213,8 @@ def tile_list_msg_tanh_res_biasP_kernel(
                         )
 
         parted1 = part(1, picked1, "raw11")
+
+        deal_wd_scales(0, "grouped3")
 
         wd8 = sb([P, PACK, P], U32, "wd8")
         nc.scalar.copy(

@@ -25,7 +25,7 @@ LAST_QUAD = P - 32
 LIST_ROWS = 16
 HALF = J // 2
 QUARTER = HALF // 2
-SCALAR_LAST = 64
+SCALAR_LAST = 96
 OUT_GROUP = 512
 OUT_WIDTHS = (256, 256, 256, 256, 256, 256, 256, 128, 128)
 VECTOR_ROUNDS = 2
@@ -56,7 +56,7 @@ def tile_list_msg_tanh_res_biasP_kernel(
         def entries(s, lo, width):
             return lists[s][:, lo // LIST_ROWS : (lo + width) // LIST_ROWS]
 
-        nc.scalar.dma_start(
+        nc.sync.dma_start(
             table_scales[LAST_QUAD:P, :].bitcast(I32), tab_scales.bitcast(I32).rearrange("a r n -> r a n")
         )
         nc.sync.dma_start(src_list[:], offs)

@@ -15,6 +15,7 @@ FP8X4 = mybir.dt.float8_e4m3fn_x4
 FP4X4 = mybir.dt.float4_e2m1fn_x4
 ACT = mybir.ActivationFunctionType
 MULT = mybir.AluOpType.mult
+ADD = mybir.AluOpType.add
 
 P = 128
 PACK = 4
@@ -25,7 +26,7 @@ LAST_QUAD = P - 32
 LIST_ROWS = 16
 HALF = J // 2
 QUARTER = HALF // 2
-SCALAR_LAST = 96
+SCALAR_LAST = 72
 OUT_GROUP = 512
 OUT_WIDTHS = (256, 256, 256, 256, 256, 256, 256, 128, 128)
 VECTOR_ROUNDS = 2
@@ -153,9 +154,10 @@ def tile_list_msg_tanh_res_biasP_kernel(
                 ACT.Copy,
             )
             if split < P:
-                nc.vector.tensor_copy(
+                nc.gpsimd.tensor_scalar(
                     grouped[:, :, split:P, :].rearrange("p t m j -> p m j t"),
                     raw[a, s][:, :, split * PACK : R].rearrange("p j (m t) -> p m j t", t=PACK),
+                    1.0, 0.0, MULT, ADD,
                 )
             w_codes[a, s] = sb([P, R], U32, "w_codes%d%d" % (a, s))
             w_scales[a, s] = sb([P, R], U8, "w_scales%d%d" % (a, s))

@@ -30,7 +30,7 @@ SCALAR_LAST = 72
 OUT_GROUP = 512
 OUT_WIDTHS = (256, 256, 256, 256, 256, 256, 256, 128, 128)
 VECTOR_ROUNDS = 2
-SCALAR_WEAVES = 3
+SCALAR_WEAVES = 4
 
 
 def tile_list_msg_tanh_res_biasP_kernel(
@@ -41,9 +41,13 @@ def tile_list_msg_tanh_res_biasP_kernel(
     with ExitStack() as ctx:
         keep = ctx.enter_context(tc.tile_pool(name="keep", bufs=1))
         psum = ctx.enter_context(tc.psum_pool(name="psum", bufs=1))
+        shared = ctx.enter_context(tc.tile_pool(name="shared", bufs=1))
 
         def sb(shape, dtype, name, tag=None):
             return keep.tile(shape, dtype, name=name, tag=tag or name, align_bytes=64)
+
+        def placed(shape, dtype, name, offset):
+            return shared.tile(shape, dtype, name=name, offset=offset, align_bytes=64)
 
         def bank(i, name):
             return psum.tile([P, HALF], F32, name=name, tag="bank%d" % i)
@@ -52,7 +56,7 @@ def tile_list_msg_tanh_res_biasP_kernel(
         dst_list = keep.tile([P, J // LIST_ROWS], U16, name="dst_list")
         lists = (src_list, dst_list)
         table = sb([P, T], I32, "table")
-        table_scales = sb([P, T], U8, "table_scales")
+        table_scales = placed([P, T], U8, "table_scales", 4 * T - T // 2)
 
         def entries(s, lo, width):
             return lists[s][:, lo // LIST_ROWS : (lo + width) // LIST_ROWS]
@@ -61,7 +65,6 @@ def tile_list_msg_tanh_res_biasP_kernel(
             table_scales[LAST_QUAD:P, :].bitcast(I32), tab_scales.bitcast(I32).rearrange("a r n -> r a n")
         )
         nc.sync.dma_start(src_list[:], offs)
-        nc.sync.dma_start(dst_list[:], offs2)
         w_order = [(a, s) for a in range(PASSES) for s in range(2)]
         raw = {}
         for a, s in w_order:
@@ -69,6 +72,7 @@ def tile_list_msg_tanh_res_biasP_kernel(
             raw[a, s] = sb([P, PACK, R], F32, "raw%d%d" % (a, s))
             nc.sync.dma_start(raw[a, s][:], rows)
             if (a, s) == w_order[0]:
+                nc.sync.dma_start(dst_list[:], offs2)
                 nc.sync.dma_start(table[:], tab_words[0].rearrange("p t c -> p (t c)").bitcast(I32))
 
         sm_raw = sb([P, PACK], F32, "sm_raw")
@@ -79,13 +83,14 @@ def tile_list_msg_tanh_res_biasP_kernel(
         wd_scales_raw = sb([P, N], U8, "wd_scales_raw")
         nc.vector.memset(wd_scales_raw[:].bitcast(I32), 0)
         nc.vector.memset(table_scales[0:LAST_QUAD, :].bitcast(I32), 0)
-        edge_scales = sb([P, 2, PASSES, J], U8, "edge_scales")
-        nc.vector.memset(edge_scales[:].rearrange("p h a n -> p (h a n)").bitcast(I32), 0)
+        edge_scales = [sb([P, PASSES, J], U8, "edge_scales0")]
+        nc.vector.memset(edge_scales[0][:].rearrange("p a n -> p (a n)").bitcast(I32), 0)
         pages = [sb([P, T], F32, "page0")]
         nc.vector.memset(pages[0][:], 0.0)
 
         def late_page(tag):
-            page = sb([P, T], F32, "page%d" % len(pages), tag=tag)
+            name = "page%d" % len(pages)
+            page = sb([P, T], F32, name, tag=tag) if tag else placed([P, T], F32, name, 0)
             nc.gpsimd.memset(page[:], 0.0)
             pages.append(page)
 
@@ -103,8 +108,8 @@ def tile_list_msg_tanh_res_biasP_kernel(
             load_wd_scales(w)
 
         picked_scales = [sb([P, 2 * HALF], U8, "picked_scales%d" % h) for h in range(2)]
-        for h in range(2):
-            for s in range(2):
+        for s in range(2):
+            for h in range(2):
                 nc.vector.tensor_copy(
                     picked_scales[h][:, s * HALF : (s + 1) * HALF],
                     table_scales[:].indirect(entries(s, h * HALF, HALF)),
@@ -115,18 +120,16 @@ def tile_list_msg_tanh_res_biasP_kernel(
             for q in range(QUADS):
                 first = LAST_QUAD + 8 * q
                 (nc.scalar, nc.sync)[h].dma_start(
-                    edge_scales[32 * q : 32 * q + 4, h, :, :].bitcast(I32), picked[first : first + 8, :].bitcast(I32)
+                    edge_scales[h][32 * q : 32 * q + 4, :, :].bitcast(I32), picked[first : first + 8, :].bitcast(I32)
                 )
 
         move_scales(0)
-        wd_raw = sb([P, N + N // 2], I32, "wd_raw", tag="table_scales")
+        late_page(None)
+        wd_raw = placed([P, N + N // 2], I32, "wd_raw", 4 * T)
         wd8_raw = wd_raw[:, 0:N]
         wd4_raw = wd_raw[:, N : N + N // 2]
         nc.sync.dma_start(wd4_raw, wd4_words[0].bitcast(I32))
         nc.sync.dma_start(wd8_raw, wd8_words[0].rearrange("p n c -> p (n c)").bitcast(I32))
-        move_scales(1)
-        wgo_sb = sb([P, J], F32, "wgo_sb", tag="picked_scales0")
-        nc.sync.dma_start(wgo_sb[:], wgo)
 
         def look_up(h, s, tag=None):
             picked = sb([P, HALF], U32, "picked%d%d" % (h, s), tag=tag)
@@ -173,6 +176,11 @@ def tile_list_msg_tanh_res_biasP_kernel(
         picked0 = [look_up(0, s) for s in range(2)]
         quantise_weight(0)
         parted0 = part(0, picked0, "raw00")
+        edge_scales.append(sb([P, PASSES, J], U8, "edge_scales1", tag="picked01"))
+        nc.gpsimd.memset(edge_scales[1][:].rearrange("p a n -> p (a n)").bitcast(I32), 0)
+        move_scales(1)
+        wgo_sb = sb([P, J], F32, "wgo_sb", tag="picked_scales0")
+        nc.sync.dma_start(wgo_sb[:], wgo)
         picked1 = [look_up(1, 0, "picked00")]
         quantise_weight(1)
         picked1.append(look_up(1, 1, "raw01"))
@@ -197,7 +205,7 @@ def tile_list_msg_tanh_res_biasP_kernel(
                 lhsT=w_codes[a, s][:, w_cols].bitcast(FP8X4),
                 lhsT_scale=w_scales[a, s][:, w_cols],
                 rhs=parted[:, s, a, 2 * lo : 2 * (lo + width)].bitcast(FP4X4),
-                rhs_scale=edge_scales[:, h, a, at : at + width],
+                rhs_scale=edge_scales[h][:, a, at : at + width],
                 start=start,
                 stop=stop,
             )
@@ -230,7 +238,7 @@ def tile_list_msg_tanh_res_biasP_kernel(
             for t in range(ts.start, ts.stop):
                 wd4[t] = words[:, t - ts.start, :]
 
-        deal_wd4(slice(0, 1))
+        deal_wd4(slice(0, 2))
 
         h_codes = [sb([P, HALF], U32, "h_codes%d" % h) for h in range(2)]
         h_scales = [sb([P, HALF], U8, "h_scales%d" % h) for h in range(2)]
@@ -253,7 +261,7 @@ def tile_list_msg_tanh_res_biasP_kernel(
             squash(e)
         quantise_hidden(0, 0, woven0[0])
         squash(3)
-        deal_wd4(slice(1, PACK), "woven00")
+        deal_wd4(slice(2, PACK), "woven00")
         deal_wd_scales(2, "th02")
         quantise_hidden(0, QUARTER, woven0[1])
         late_page("woven01")
@@ -266,7 +274,7 @@ def tile_list_msg_tanh_res_biasP_kernel(
                 acc[:, 0:width], lhsT=wd8[:, t, :].bitcast(FP8X4), lhsT_scale=wd_scales[t][4:P, :],
                 rhs=codes.bitcast(FP8X4), rhs_scale=scales, start=True, stop=False,
             )
-            step = HALF if width == HALF else P
+            step = width
             for at in range(0, width, step):
                 nc.tensor.matmul_mx(
                     acc[:, at : at + step], lhsT=wd4[t].bitcast(FP4X4), lhsT_scale=wd_scales[t],
@@ -283,12 +291,12 @@ def tile_list_msg_tanh_res_biasP_kernel(
             )
 
         for u in range(2):
-            name = "quarter%d" % u
-            put(name, u * QUARTER, QUARTER, 0, second_layer(name, 0, 0, u * QUARTER, QUARTER, 0))
-            late_page("message%s0" % name)
-        ys0 = {t: second_layer("half0", t, 0, 0, HALF, t) for t in range(1, PACK)}
-        for t in range(1, PACK - 1):
-            put("half0", 0, HALF, t, ys0[t])
+            for t in range(2):
+                name = "quarter%d" % u
+                put(name, u * QUARTER, QUARTER, t, second_layer(name, t, 0, u * QUARTER, QUARTER, t))
+        late_page("messagequarter01")
+        ys0 = {t: second_layer("half0", t, 0, 0, HALF, t) for t in range(2, PACK)}
+        put("half0", 0, HALF, 2, ys0[2])
 
         hidden1 = sb([P, PACK, HALF], BF16, "hidden1")
         order = w_order[::-1]
@@ -311,24 +319,24 @@ def tile_list_msg_tanh_res_biasP_kernel(
             put("half1", HALF, HALF, t, ys1[t])
 
         out_rows = out_0.rearrange("(p t) c -> t p c", t=PACK)
-        starts = [sum(OUT_WIDTHS[:c]) for c in range(len(OUT_WIDTHS))]
+        starts = [(OUT_GROUP + sum(OUT_WIDTHS[:c])) % T for c in range(len(OUT_WIDTHS))]
         pairs = sb([P, 2, T, 2], BF16, "pairs", tag="b_sb")
 
         out_words = out_1[0].rearrange("p t c -> p (t c)").bitcast(I32)
-        out_scales = sb([P, 2, OUT_GROUP], U8, "out_scales")
+        out_scales = sb([P, OUT_GROUP], U8, "out_scales")
         out_codes = [sb([P, OUT_GROUP], U32, "out_codes%d" % g) for g in range(T // OUT_GROUP)]
-        own = starts[VECTOR_ROUNDS]
+        own = range(starts[0], starts[VECTOR_ROUNDS])
         for t in range(PACK):
             nc.sync.dma_start(out_rows[t], pages[t][:])
             if t == PACK - 1:
                 steps = list(zip(starts, OUT_WIDTHS))
             elif t == PACK - 2:
-                steps = [(0, own), (own, T - own)]
+                steps = [(own.start, len(own)), (own.stop, T - own.stop), (0, own.start)]
             else:
                 steps = [(0, T)]
             for lo, width in steps:
                 rounded = pairs[:, t // 2, lo : lo + width, t % 2]
-                if t >= PACK - 2 and lo < own:
+                if t >= PACK - 2 and lo in own:
                     nc.vector.tensor_copy(rounded, pages[t][:, lo : lo + width])
                 else:
                     nc.scalar.activation(rounded, pages[t][:, lo : lo + width], ACT.Copy)
@@ -350,7 +358,7 @@ def tile_list_msg_tanh_res_biasP_kernel(
             g, lo = divmod(starts[c], OUT_GROUP)
             cut = slice(lo, lo + OUT_WIDTHS[c])
             nc.vector.quantize_mx(
-                out_codes[g][:, cut].bitcast(FP8X4), out_scales[4 * (g // 2) : P, g % 2, cut], woven[:].rearrange("p n t -> p (n t)")
+                out_codes[g][:, cut].bitcast(FP8X4), out_scales[4 * g : P, cut], woven[:].rearrange("p n t -> p (n t)")
             )
             if c == len(OUT_WIDTHS) - 1 or c == len(OUT_WIDTHS) - 2 or cut.stop == OUT_GROUP:
                 first = lo if c == len(OUT_WIDTHS) - 1 else 0
@@ -366,6 +374,6 @@ def tile_list_msg_tanh_res_biasP_kernel(
             quantise_out(c, woven_outs[c])
         for q in range(QUADS):
             (nc.sync, nc.scalar)[q % 2].dma_start(
-                out_2[0, 4 * q : 4 * q + 4, :].bitcast(I32).rearrange("r (g n) -> g r n", g=2),
-                out_scales[32 * q : 32 * q + 8, :, :].rearrange("p d n -> p (d n)").bitcast(I32),
+                out_2[0, 4 * q : 4 * q + 4, :].bitcast(I32).rearrange("r (g n) -> g r n", g=4),
+                out_scales[32 * q : 32 * q + 16, :].bitcast(I32),
             )

@@ -27,6 +27,7 @@ LIST_ROWS = 16
 HALF = J // 2
 QUARTER = HALF // 2
 SCALAR_LAST = 72
+SCALAR_THIRD = 104
 OUT_GROUP = 512
 OUT_WIDTHS = (256, 256, 256, 256, 256, 256, 256, 128, 128)
 VECTOR_ROUNDS = 2
@@ -150,7 +151,7 @@ def tile_list_msg_tanh_res_biasP_kernel(
         def quantise_weight(i, tag=None):
             a, s = w_order[i]
             grouped = sb([P, PACK, P, PACK], BF16, "grouped%d" % i, tag=tag)
-            split = P if i < 3 else SCALAR_LAST
+            split = (P, P, SCALAR_THIRD, SCALAR_LAST)[i]
             nc.scalar.activation(
                 grouped[:, :, 0:split, :].rearrange("p t m j -> p m j t"),
                 raw[a, s][:, :, 0 : split * PACK].rearrange("p j (m t) -> p m j t", t=PACK),

from contextlib import ExitStack

import concourse.mybir as mybir

K, R, N, T, J = 1024, 512, 512, 2048, 1024
FLOPS = 2 * J * (2 * K * R + 2 * R * N)

F32 = mybir.dt.float32
BF16 = mybir.dt.bfloat16
I32 = mybir.dt.int32
U32 = mybir.dt.uint32
U16 = mybir.dt.uint16
U8 = mybir.dt.uint8
FP8X4 = mybir.dt.float8_e4m3fn_x4
FP4X4 = mybir.dt.float4_e2m1fn_x4
ACT = mybir.ActivationFunctionType
MULT = mybir.AluOpType.mult
ADD = mybir.AluOpType.add

P = 128
PACK = 4
K_PASS = P * PACK
PASSES = K // K_PASS
QUADS = 4
LAST_QUAD = P - 32
LIST_ROWS = 16
HALF = J // 2
QUARTER = HALF // 2
SCALAR_LAST = 72
SCALAR_THIRD = 104
OUT_GROUP = 512
OUT_WIDTHS = (256, 256, 256, 256, 256, 256, 256, 128, 128)
VECTOR_ROUNDS = 2
SCALAR_WEAVES = 4


def tile_list_msg_tanh_res_biasP_kernel(
    tc, tab_words, tab_scales, ws, wt, sm, wd4_words, wd4_scales, wd8_words, wd8_scales, b, wgo, offs, offs2,
    out_0, out_1, out_2,
):
    nc = tc.nc
    with ExitStack() as ctx:
        keep = ctx.enter_context(tc.tile_pool(name="keep", bufs=1))
        psum = ctx.enter_context(tc.psum_pool(name="psum", bufs=1))
        shared = ctx.enter_context(tc.tile_pool(name="shared", bufs=1))

        def sb(shape, dtype, name, tag=None):
            return keep.tile(shape, dtype, name=name, tag=tag or name, align_bytes=64)

        def placed(shape, dtype, name, offset):
            return shared.tile(shape, dtype, name=name, offset=offset, align_bytes=64)

        def bank(i, name):
            return psum.tile([P, HALF], F32, name=name, tag="bank%d" % i)

        src_list = keep.tile([P, J // LIST_ROWS], U16, name="src_list")
        dst_list = keep.tile([P, J // LIST_ROWS], U16, name="dst_list")
        lists = (src_list, dst_list)
        table = sb([P, T], I32, "table")
        table_scales = placed([P, T], U8, "table_scales", 4 * T - T // 2)

        def entries(s, lo, width):
            return lists[s][:, lo // LIST_ROWS : (lo + width) // LIST_ROWS]

        nc.sync.dma_start(
            table_scales[LAST_QUAD:P, :].bitcast(I32), tab_scales.bitcast(I32).rearrange("a r n -> r a n")
        )
        nc.sync.dma_start(src_list[:], offs)
        w_order = [(a, s) for a in range(PASSES) for s in range(2)]
        raw = {}
        for a, s in w_order:
            rows = (ws, wt)[s][a * K_PASS : (a + 1) * K_PASS, :].rearrange("(p j) r -> p j r", j=PACK)
            raw[a, s] = sb([P, PACK, R], F32, "raw%d%d" % (a, s))
            nc.sync.dma_start(raw[a, s][:], rows)
            if (a, s) == w_order[0]:
                nc.sync.dma_start(dst_list[:], offs2)
                nc.sync.dma_start(table[:], tab_words[0].rearrange("p t c -> p (t c)").bitcast(I32))

        sm_raw = sb([P, PACK], F32, "sm_raw")
        b_sb = sb([P, PACK], F32, "b_sb")
        nc.scalar.dma_start(sm_raw[:], sm.rearrange("(p t) -> p t", t=PACK))
        nc.scalar.dma_start(b_sb[:], b.rearrange("(p t) -> p t", t=PACK))

        wd_scales_raw = sb([P, N], U8, "wd_scales_raw")
        nc.vector.memset(wd_scales_raw[:].bitcast(I32), 0)
        nc.vector.memset(table_scales[0:LAST_QUAD, :].bitcast(I32), 0)
        edge_scales = [sb([P, PASSES, J], U8, "edge_scales0")]
        nc.vector.memset(edge_scales[0][:].rearrange("p a n -> p (a n)").bitcast(I32), 0)
        pages = [sb([P, T], F32, "page0")]
        nc.vector.memset(pages[0][:], 0.0)

        def late_page(tag):
            name = "page%d" % len(pages)
            page = sb([P, T], F32, name, tag=tag) if tag else placed([P, T], F32, name, 0)
            nc.gpsimd.memset(page[:], 0.0)
            pages.append(page)

        def load_wd_scales(w):
            for q in range(QUADS):
                first = 32 * q + 4 * w
                nc.gpsimd.dma_start(
                    wd_scales_raw[first : first + 4, :].bitcast(I32),
                    (wd4_scales, wd8_scales)[w][0, 4 * q : 4 * q + 4, :].bitcast(I32),
                )

        sm_rows = sb([P, P, PACK], F32, "sm_rows")
        nc.scalar.activation(sm_rows[:], sm_raw[:].unsqueeze(1).to_broadcast([P, P, PACK]), ACT.Copy)
        for w in range(2):
            load_wd_scales(w)

        picked_scales = [sb([P, 2 * HALF], U8, "picked_scales%d" % h) for h in range(2)]
        for s in range(2):
            for h in range(2):
                nc.vector.tensor_copy(
                    picked_scales[h][:, s * HALF : (s + 1) * HALF],
                    table_scales[:].indirect(entries(s, h * HALF, HALF)),
                )

        def move_scales(h):
            picked = picked_scales[h]
            for q in range(QUADS):
                first = LAST_QUAD + 8 * q
                (nc.scalar, nc.sync)[h].dma_start(
                    edge_scales[h][32 * q : 32 * q + 4, :, :].bitcast(I32), picked[first : first + 8, :].bitcast(I32)
                )

        move_scales(0)
        late_page(None)
        wd_raw = placed([P, N + N // 2], I32, "wd_raw", 4 * T)
        wd8_raw = wd_raw[:, 0:N]
        wd4_raw = wd_raw[:, N : N + N // 2]
        nc.sync.dma_start(wd4_raw, wd4_words[0].bitcast(I32))
        nc.sync.dma_start(wd8_raw, wd8_words[0].rearrange("p n c -> p (n c)").bitcast(I32))

        def look_up(h, s, tag=None):
            picked = sb([P, HALF], U32, "picked%d%d" % (h, s), tag=tag)
            nc.vector.tensor_copy(picked[:], table[:].bitcast(U32).indirect(entries(s, h * HALF, HALF)))
            return picked

        def part(h, picked, tag):
            parted = sb([P, 2, PASSES, 2 * HALF], U8, "parted%d" % h, tag=tag)
            for s in range(2):
                nc.vector.tensor_copy(
                    parted[:, s, :, :].bitcast(U16), picked[s][:].bitcast(U16).rearrange("p (n d) -> p d n", d=PASSES)
                )
            return parted

        w_codes = {}
        w_scales = {}

        def quantise_weight(i, tag=None):
            a, s = w_order[i]
            grouped = sb([P, PACK, P, PACK], BF16, "grouped%d" % i, tag=tag)
            split = (P, P, SCALAR_THIRD, SCALAR_LAST)[i]
            nc.scalar.activation(
                grouped[:, :, 0:split, :].rearrange("p t m j -> p m j t"),
                raw[a, s][:, :, 0 : split * PACK].rearrange("p j (m t) -> p m j t", t=PACK),
                ACT.Copy,
            )
            if split < P:
                nc.gpsimd.tensor_scalar(
                    grouped[:, :, split:P, :].rearrange("p t m j -> p m j t"),
                    raw[a, s][:, :, split * PACK : R].rearrange("p j (m t) -> p m j t", t=PACK),
                    1.0, 0.0, MULT, ADD,
                )
            w_codes[a, s] = sb([P, R], U32, "w_codes%d%d" % (a, s))
            w_scales[a, s] = sb([P, R], U8, "w_scales%d%d" % (a, s))
            step = PACK // 2 if i == 3 else PACK
            for t in range(0, PACK, step):
                cut = slice(t * P, (t + step) * P)
                nc.vector.quantize_mx(
                    w_codes[a, s][:, cut].bitcast(FP8X4),
                    w_scales[a, s][:, cut],
                    grouped[:, t : t + step, :, :].rearrange("p t m j -> p (t m j)"),
                )

        picked0 = [look_up(0, s) for s in range(2)]
        quantise_weight(0)
        parted0 = part(0, picked0, "raw00")
        edge_scales.append(sb([P, PASSES, J], U8, "edge_scales1", tag="picked01"))
        nc.gpsimd.memset(edge_scales[1][:].rearrange("p a n -> p (a n)").bitcast(I32), 0)
        move_scales(1)
        wgo_sb = sb([P, J], F32, "wgo_sb", tag="picked_scales0")
        nc.sync.dma_start(wgo_sb[:], wgo)
        picked1 = [look_up(1, 0, "picked00")]
        quantise_weight(1)
        picked1.append(look_up(1, 1, "raw01"))
        quantise_weight(2)
        wd_scales = {}

        def deal_wd_scales(first, tag):
            dealt = sb([P, 2, P], U8, "wd_scales%d" % first, tag=tag)
            nc.vector.tensor_copy(
                dealt[:], wd_scales_raw[:].rearrange("p (m t) -> p t m", t=PACK)[:, first : first + 2, :]
            )
            for t in range(2):
                wd_scales[first + t] = dealt[:, t, :]

        quantise_weight(3)

        def first_pass(out, h, lo, width, t, a, s, parted, start, stop):
            w_cols = slice(t * P, (t + 1) * P)
            at = s * HALF + lo
            nc.tensor.matmul_mx(
                out,
                lhsT=w_codes[a, s][:, w_cols].bitcast(FP8X4),
                lhsT_scale=w_scales[a, s][:, w_cols],
                rhs=parted[:, s, a, 2 * lo : 2 * (lo + width)].bitcast(FP4X4),
                rhs_scale=edge_scales[h][:, a, at : at + width],
                start=start,
                stop=stop,
            )

        sums0 = [bank(e, "sums0%d" % e) for e in range(HALF // P)]
        swapped = w_order[:2] + w_order[:1:-1]
        for banks, steps in (((0, 1, 2, 3), (0, 1)), ((0, 1), (2, 3)), ((2, 3), (2, 3))):
            for i in steps:
                for e in banks:
                    a, s = (w_order if e < 2 else swapped)[i]
                    for t in range(PACK):
                        first_pass(
                            sums0[e][:, t * P : (t + 1) * P], 0, e * P, P, t, a, s, parted0,
                            i == 0 and t == 0, i == len(w_order) - 1 and t == PACK - 1,
                        )

        parted1 = part(1, picked1, "raw11")

        deal_wd_scales(0, "grouped3")

        wd8 = sb([P, PACK, P], U32, "wd8")
        nc.scalar.copy(
            wd8[:].rearrange("p t m -> p m t"), wd8_raw.bitcast(U32).rearrange("p (m t) -> p m t", t=PACK)
        )
        wd4 = {}

        def deal_wd4(ts, tag=None):
            words = sb([P, ts.stop - ts.start, 2 * P], U8, "wd4_%d" % ts.start, tag=tag)
            nc.scalar.copy(words[:].bitcast(U16), wd4_raw.bitcast(U16).rearrange("p (m t) -> p t m", t=PACK)[:, ts, :])
            for t in range(ts.start, ts.stop):
                wd4[t] = words[:, t - ts.start, :]

        deal_wd4(slice(0, 2))

        h_codes = [sb([P, HALF], U32, "h_codes%d" % h) for h in range(2)]
        h_scales = [sb([P, HALF], U8, "h_scales%d" % h) for h in range(2)]

        def quantise_hidden(h, lo, woven):
            cut = slice(lo, lo + woven.shape[1])
            nc.vector.quantize_mx(
                h_codes[h][:, cut].bitcast(FP8X4), h_scales[h][:, cut], woven[:].rearrange("p n t -> p (n t)")
            )

        woven0 = [sb([P, QUARTER, PACK], BF16, "woven0%d" % u) for u in range(2)]

        def squash(e):
            th = sb([P, P, PACK], F32, "th0%d" % e)
            nc.scalar.activation(th[:], sums0[e][:].rearrange("p (t n) -> p n t", t=PACK), ACT.Tanh)
            u, at = divmod(e * P, QUARTER)
            nc.vector.tensor_tensor(woven0[u][:, at : at + P, :], th[:], sm_rows[:], MULT)

        for e in range(3):
            squash(e)
        quantise_hidden(0, 0, woven0[0])
        squash(3)
        deal_wd4(slice(2, PACK), "woven00")
        deal_wd_scales(2, "th02")
        quantise_hidden(0, QUARTER, woven0[1])
        late_page("woven01")

        def second_layer(name, i, h, lo, width, t):
            acc = bank(i, "y%s%d" % (name, t))
            codes = h_codes[h][:, lo : lo + width]
            scales = h_scales[h][:, lo : lo + width]
            nc.tensor.matmul_mx(
                acc[:, 0:width], lhsT=wd8[:, t, :].bitcast(FP8X4), lhsT_scale=wd_scales[t][4:P, :],
                rhs=codes.bitcast(FP8X4), rhs_scale=scales, start=True, stop=False,
            )
            step = width
            for at in range(0, width, step):
                nc.tensor.matmul_mx(
                    acc[:, at : at + step], lhsT=wd4[t].bitcast(FP4X4), lhsT_scale=wd_scales[t],
                    rhs=codes[:, at : at + step].bitcast(FP8X4), rhs_scale=scales[:, at : at + step],
                    start=False, stop=at + step == width,
                )
            return acc

        def put(name, lo, width, t, acc, tag=None):
            message = sb([P, width], F32, "message%s%d" % (name, t), tag=tag)
            nc.scalar.activation(message[:], acc[:, 0:width], ACT.Identity, bias=b_sb[:, t : t + 1])
            nc.vector.tensor_tensor(
                pages[t][:].indirect(entries(1, lo, width)), message[:], wgo_sb[:, lo : lo + width], MULT
            )

        for u in range(2):
            for t in range(2):
                name = "quarter%d" % u
                put(name, u * QUARTER, QUARTER, t, second_layer(name, t, 0, u * QUARTER, QUARTER, t))
        late_page("messagequarter01")
        ys0 = {t: second_layer("half0", t, 0, 0, HALF, t) for t in range(2, PACK)}
        put("half0", 0, HALF, 2, ys0[2])

        hidden1 = sb([P, PACK, HALF], BF16, "hidden1")
        order = w_order[::-1]
        for t in range(PACK):
            acc = bank(PACK + t, "sums1%d" % t)
            for a, s in order:
                first_pass(acc[:], 1, 0, HALF, t, a, s, parted1, (a, s) == order[0], (a, s) == order[-1])
            th = sb([P, HALF], F32, "th1%d" % t, tag="th1%d" % (t % 2))
            nc.scalar.activation(th[:], acc[:], ACT.Tanh)
            nc.scalar.activation(hidden1[:, t, :], th[:], ACT.Copy, scale=sm_rows[:, 0, t : t + 1])
        woven1 = sb([P, HALF, PACK], BF16, "woven1")
        nc.scalar.copy(
            woven1[:].rearrange("p (c i) t -> p c t i", i=4), hidden1[:].rearrange("p t (c i) -> p c t i", i=4)
        )
        quantise_hidden(1, 0, woven1)

        put("half0", 0, HALF, PACK - 1, ys0[PACK - 1], tag="hidden1")
        ys1 = [second_layer("half1", PACK + t, 1, 0, HALF, t) for t in range(PACK)]
        for t in range(PACK):
            put("half1", HALF, HALF, t, ys1[t])

        out_rows = out_0.rearrange("(p t) c -> t p c", t=PACK)
        starts = [(OUT_GROUP + sum(OUT_WIDTHS[:c])) % T for c in range(len(OUT_WIDTHS))]
        pairs = sb([P, 2, T, 2], BF16, "pairs", tag="b_sb")

        out_words = out_1[0].rearrange("p t c -> p (t c)").bitcast(I32)
        out_scales = sb([P, OUT_GROUP], U8, "out_scales")
        out_codes = [sb([P, OUT_GROUP], U32, "out_codes%d" % g) for g in range(T // OUT_GROUP)]
        own = range(starts[0], starts[VECTOR_ROUNDS])
        for t in range(PACK):
            nc.sync.dma_start(out_rows[t], pages[t][:])
            if t == PACK - 1:
                steps = list(zip(starts, OUT_WIDTHS))
            elif t == PACK - 2:
                steps = [(own.start, len(own)), (own.stop, T - own.stop), (0, own.start)]
            else:
                steps = [(0, T)]
            for lo, width in steps:
                rounded = pairs[:, t // 2, lo : lo + width, t % 2]
                if t >= PACK - 2 and lo in own:
                    nc.vector.tensor_copy(rounded, pages[t][:, lo : lo + width])
                else:
                    nc.scalar.activation(rounded, pages[t][:, lo : lo + width], ACT.Copy)

        def weave_out(c):
            on_scalar = c >= len(OUT_WIDTHS) - SCALAR_WEAVES
            woven = sb([P, OUT_WIDTHS[c], PACK], BF16, "woven_out%d" % c)
            word = U32 if on_scalar else I32
            dst = woven[:].rearrange("p n t -> p (n t)").bitcast(word).rearrange("p (n u) -> p n u", u=2)
            src = pairs[:, :, starts[c] : starts[c] + OUT_WIDTHS[c], :].rearrange("p u n e -> p u (n e)")
            src = src.bitcast(word).rearrange("p u n -> p n u")
            if on_scalar:
                nc.scalar.copy(dst, src)
            else:
                nc.vector.tensor_copy(dst, src)
            return woven

        def quantise_out(c, woven):
            g, lo = divmod(starts[c], OUT_GROUP)
            cut = slice(lo, lo + OUT_WIDTHS[c])
            nc.vector.quantize_mx(
                out_codes[g][:, cut].bitcast(FP8X4), out_scales[4 * g : P, cut], woven[:].rearrange("p n t -> p (n t)")
            )
            if c == len(OUT_WIDTHS) - 1 or c == len(OUT_WIDTHS) - 2 or cut.stop == OUT_GROUP:
                first = lo if c == len(OUT_WIDTHS) - 1 else 0
                nc.sync.dma_start(
                    out_words[:, g * OUT_GROUP + first : g * OUT_GROUP + cut.stop],
                    out_codes[g][:, first : cut.stop].bitcast(I32),
                )

        woven_outs = [weave_out(0)]
        for c in range(len(OUT_WIDTHS)):
            if c + 1 < len(OUT_WIDTHS):
                woven_outs.append(weave_out(c + 1))
            quantise_out(c, woven_outs[c])
        for q in range(QUADS):
            (nc.sync, nc.scalar)[q % 2].dma_start(
                out_2[0, 4 * q : 4 * q + 4, :].bitcast(I32).rearrange("r (g n) -> g r n", g=4),
                out_scales[32 * q : 32 * q + 16, :].bitcast(I32),
            )
